import numpy as np
import ml_dtypes


def mxq(x, axis, fmt="e4m3"):
    dtype, down = {"e4m3": (ml_dtypes.float8_e4m3fn, 7), "e5m2": (ml_dtypes.float8_e5m2, 14)}[fmt]
    v = np.moveaxis(np.asarray(x, np.float32).astype(ml_dtypes.bfloat16).astype(np.float64), axis, -1)
    blocks = v.reshape(v.shape[:-1] + (-1, 32))
    amax = np.abs(blocks).max(-1, keepdims=True)
    byte = np.maximum(np.where(amax > 0, np.frexp(amax)[1] - 1 + 127, 0) - down, 1)
    scale = np.exp2(byte - 127.0)
    codes = (blocks / scale).astype(np.float32).astype(dtype).astype(np.float64)
    return np.moveaxis((codes * scale).reshape(v.shape), -1, axis)


WIDE = False


def mx_kscale(k):
    if not WIDE:
        return np.ones(k)
    levels = np.array([10, -10, 5, -5, 0])
    if k % 512:
        return np.exp2(np.random.permutation(np.resize(levels, k // 32))).repeat(32)
    a = np.empty((k // 512, 16))
    for p in range(k // 512):
        a[p, :8] = np.random.permutation(np.resize(levels, 8))
        for g in range(8):
            far = levels[np.abs(levels - a[p, g]) >= 10]
            a[p, g + 8] = far[np.random.randint(len(far))]
    return np.exp2(a.ravel()).repeat(32)


def f64(x):
    return np.asarray(x).astype(np.float64)


def striped(idx):
    return np.tile(idx.reshape(-1, 16).T, (8, 1)).astype(np.uint16)


def unstriped(offs):
    return offs[:16].T.reshape(-1).astype(np.int64)


E2M1 = np.array([0.0, 0.5, 1.0, 1.5, 2.0, 3.0, 4.0, 6.0, -0.0, -0.5, -1.0, -1.5, -2.0, -3.0, -4.0, -6.0])


def pack_weight(w, fmt):
    k, n = w.shape
    w = f64(np.asarray(w, np.float32).astype(ml_dtypes.bfloat16)).reshape(k // 32, 32, n)
    amax = np.abs(w).max(1)
    if fmt == "e4m3":
        byte = np.frexp(amax)[1] - 1 + 127 - 7
    else:
        mant, ex = np.frexp(amax / 6.0)
        byte = np.where(mant > 0.5, ex, ex - 1) + 127
    byte = np.clip(np.where(amax > 0, byte, 1), 1, 254)
    scaled = (w * np.exp2(127.0 - byte)[:, None, :]).reshape(k, n).astype(np.float32)
    by_word = np.ascontiguousarray(scaled.reshape(k // 512, 128, 4, n).transpose(0, 1, 3, 2))
    if fmt == "e4m3":
        words = by_word.astype(ml_dtypes.float8_e4m3fn).view(np.uint8)
    else:
        c = by_word.astype(ml_dtypes.float4_e2m1fn).view(np.uint8) & 0xF
        words = (c[..., 0::2] | (c[..., 1::2] << 4)).reshape(k // 512, 128, 2 * n)
    return np.ascontiguousarray(words), np.ascontiguousarray(byte.astype(np.uint8).reshape(k // 512, 16, n))


def unpack_weight(words, scales, fmt):
    g, _, n = scales.shape
    words = np.ascontiguousarray(words).reshape(g, 128, n, -1)
    if fmt == "e4m3":
        vals = words.view(ml_dtypes.float8_e4m3fn).astype(np.float64)
    else:
        nib = np.empty((g, 128, n, 4), np.uint8)
        nib[..., 0::2] = words & 0xF
        nib[..., 1::2] = words >> 4
        vals = E2M1[nib]
    vals = vals * np.repeat(np.exp2(scales.astype(np.float64) - 127.0), 8, axis=1)[..., None]
    return vals.transpose(0, 1, 3, 2).reshape(g * 512, n)


def gelu(v):
    return 0.5 * v * (1.0 + np.tanh(np.sqrt(2.0 / np.pi) * (v + 0.044715 * v**3)))


K, H, N, T, S, P = 512, 1024, 512, 4096, 1024, 512


def setup_inputs():
    n = np.random.standard_normal
    s = mx_kscale(K)[:, None]
    u = mx_kscale(H)[:, None]
    tab_words, tab_scales = pack_weight(n((K, T)) * s, "e4m3")
    w1_words, w1_scales = pack_weight(n((K, H)) / np.sqrt(K) / s, "e2m1")
    w3_words, w3_scales = pack_weight(n((K, H)) / np.sqrt(K) / s, "e4m3")
    w2 = (n((K, H)) / np.sqrt(K) / s * u.T).astype(np.float32)
    w4 = (n((H, N)) / np.sqrt(H) / u).astype(np.float32)
    return {
        "tab_words": tab_words, "tab_scales": tab_scales,
        "offs": striped(np.random.permutation(T)[:S]),
        "w1_words": w1_words, "w1_scales": w1_scales,
        "w2": w2,
        "w3_words": w3_words, "w3_scales": w3_scales,
        "pos1": striped(np.random.permutation(S)[:P]),
        "pos2": striped(np.random.permutation(S)[:P]),
        "pos3": striped(np.random.permutation(S)[:P]),
        "w4": w4,
    }


def reference(tab_words, tab_scales, offs, w1_words, w1_scales, w2, w3_words, w3_scales, pos1, pos2, pos3, w4):
    v = unpack_weight(tab_words, tab_scales, "e4m3")[:, unstriped(offs)]
    x1 = unpack_weight(w1_words, w1_scales, "e2m1").T @ v
    x2 = mxq(f64(w2), 0, "e4m3").T @ v
    x3 = unpack_weight(w3_words, w3_scales, "e4m3").T @ v
    lead = 1.0 / (1.0 + np.exp(-x1[:, unstriped(pos1)]))
    z = lead * x2[:, unstriped(pos2)] * x3[:, unstriped(pos3)]
    return mxq(f64(w4), 0, "e4m3").T @ mxq(z, 0, "e4m3")

@@ -1,0 +1,212 @@
+from contextlib import ExitStack
+
+import concourse.mybir as mybir
+
+K, H, N, T, S, M = 512, 1024, 512, 4096, 1024, 512
+FLOPS = 2 * (3 * K * H * S + H * N * M)
+
+F32 = mybir.dt.float32
+BF16 = mybir.dt.bfloat16
+I32 = mybir.dt.int32
+U32 = mybir.dt.uint32
+U16 = mybir.dt.uint16
+U8 = mybir.dt.uint8
+FP8X4 = mybir.dt.float8_e4m3fn_x4
+FP4X4 = mybir.dt.float4_e2m1fn_x4
+MULT = mybir.AluOpType.mult
+SIGMOID = mybir.ActivationFunctionType.Sigmoid
+
+P = 128
+PACK = 4
+PASS = P * PACK
+BANK = 512
+BANKS = 8
+PASSES = H // PASS
+SLICES = PASSES * PACK
+RUN = 8
+HALVES = 2
+HALF = M // HALVES
+X2_LAG = 1
+VECTOR_EVACS = ((3, 0, 0), (3, 0, 1), (2, 2, 1), (2, 4, 1), (2, 5, 1))
+
+
+def tile_list_breakaway_gap_scores_kernel(
+    tc, tab_words, tab_scales, offs, w1_words, w1_scales, w2, w3_words, w3_scales, pos1, pos2, pos3, w4, out
+):
+    nc = tc.nc
+    with ExitStack() as ctx:
+        keep = ctx.enter_context(tc.tile_pool(name="keep", bufs=1))
+        ring = ctx.enter_context(tc.tile_pool(name="ring", bufs=3))
+        psum = ctx.enter_context(tc.psum_pool(name="psum", bufs=1))
+
+        def kept(shape, dtype, name, tag=""):
+            return keep.tile(shape, dtype, name=name, tag=tag or name, align_bytes=64)
+
+        offs_sb = keep.tile([P, S // 16], U16, name="offs_sb")
+        pos1_sb = keep.tile([P, M // 16], U16, name="pos1_sb")
+        pos2_sb = keep.tile([P, M // 16], U16, name="pos2_sb")
+        pos3_sb = keep.tile([P, M // 16], U16, name="pos3_sb")
+        tab_w = kept([P, T], I32, "tab_w", "slot_c")
+        tab_s = kept([P, T], U8, "tab_s", "slot_b")
+        w1_raw = kept([P, 2 * H], U8, "w1_raw", "slot_a")
+        w1s_raw = kept([P, H], U8, "w1s_raw", "slot_e")
+
+        def load_scale_rows(queue, plane, scales):
+            for q in range(4):
+                queue.dma_start(plane[32 * q : 32 * q + 4, :].bitcast(I32), scales[0, 4 * q : 4 * q + 4, :].bitcast(I32))
+
+        nc.vector.memset(tab_s[:].bitcast(I32), 0)
+        nc.sync.dma_start(offs_sb[:], offs)
+        load_scale_rows(nc.sync, w1s_raw, w1_scales)
+        nc.sync.dma_start(w1_raw[:].bitcast(I32), w1_words[0].bitcast(I32))
+        nc.sync.dma_start(pos1_sb[:], pos1)
+        nc.sync.dma_start(tab_w[:], tab_words[0].rearrange("p t i -> p (t i)").bitcast(I32))
+        nc.sync.dma_start(pos3_sb[:], pos3)
+        nc.sync.dma_start(pos2_sb[:], pos2)
+        load_scale_rows(nc.scalar, tab_s, tab_scales)
+
+        warm = kept([P, 1], F32, "warm", "slot_d")
+        warm_out = keep.tile([P, 1], F32, name="warm_out")
+        nc.gpsimd.memset(warm[:], 0.0)
+        nc.scalar.activation(warm_out[:], warm[:], SIGMOID)
+
+        v_w = [kept([P, BANK], I32, f"v_w{h}") for h in range(S // BANK)]
+        v_s = [kept([P, BANK], U8, f"v_s{h}") for h in range(S // BANK)]
+        cols = BANK // 16
+
+        def reorder_into(done, raw):
+            src = raw.bitcast(I32).rearrange("p (b q t w) -> p b q t w", b=PASSES, q=16, t=PACK)
+            dst = done.bitcast(I32).rearrange("p (b t q w) -> p b q t w", b=PASSES, q=16, t=PACK)
+            nc.vector.tensor_copy(dst, src)
+
+        def reorder(name, raw, dtype, width):
+            done = kept([P, width], dtype, name)
+            reorder_into(done[:], raw)
+            return done
+
+        w1_w = reorder("w1_w", w1_raw[:], U8, 2 * H)
+        w1_s = kept([P, H], U8, "w1_s")
+        nc.gpsimd.memset(w1_s[:].bitcast(I32), 0)
+        for q in range(4):
+            reorder_into(w1_s[32 * q : 32 * q + 4, :], w1s_raw[32 * q : 32 * q + 4, :])
+        for h in range(S // BANK):
+            nc.vector.tensor_copy(v_s[h][:], tab_s[:].indirect(offs_sb[:, h * cols : (h + 1) * cols]))
+        w3s_raw = kept([P, H], U8, "w3s_raw", "slot_e")
+        nc.gpsimd.memset(w3s_raw[:].bitcast(I32), 0)
+        load_scale_rows(nc.scalar, w3s_raw, w3_scales)
+        w3_raw = kept([P, 4 * H], U8, "w3_raw", "slot_d")[:]
+        nc.sync.dma_start(w3_raw.bitcast(I32), w3_words[0].rearrange("p c i -> p (c i)").bitcast(I32))
+        w2_raw = [kept([P, PACK, PASS], F32, f"w2_raw{b}", ("slot_a", "slot_b")[b])[:] for b in range(PASSES)]
+        for b in range(PASSES):
+            nc.sync.dma_start(w2_raw[b], w2[:, b * PASS : (b + 1) * PASS].rearrange("(p j) c -> p j c", j=PACK))
+        for h in range(S // BANK):
+            nc.vector.tensor_copy(
+                v_w[h][:].bitcast(U32), tab_w[:].bitcast(U32).indirect(offs_sb[:, h * cols : (h + 1) * cols])
+            )
+        w3_w = reorder("w3_w", w3_raw, U8, 4 * H)
+        w3_s = reorder("w3_s", w3s_raw[:], U8, H)
+        w4_both = kept([P, PASSES, PACK, N], F32, "w4_raw", "slot_c")
+        w4_raw = [w4_both[:, b] for b in range(PASSES)]
+        for b in range(PASSES):
+            rows = w4[b * PASS : (b + 1) * PASS, :].rearrange("(q t i) n -> t q i n", t=PACK, i=RUN)
+            for t in range(PACK):
+                nc.sync.dma_start(w4_raw[b][:, t, :], rows[t])
+
+        def quantise(name, grouped):
+            width = grouped.shape[1]
+            words = kept([P, width], I32, name + "_w")
+            scales = kept([P, width], U8, name + "_s")
+            nc.vector.quantize_mx(words[:].bitcast(FP8X4), scales[:], grouped[:].rearrange("p c j -> p (c j)"))
+            return words, scales
+
+        def interleave(name, planes, copy=nc.vector.tensor_copy):
+            width = planes.shape[2]
+            grouped = kept([P, width, PACK], BF16, name)
+            copy(
+                grouped[:].rearrange("p (c i) j -> p c j i", i=4), planes.rearrange("p j (c i) -> p c j i", i=4)
+            )
+            return grouped
+
+        def quantise_w2(b):
+            grouped = kept([P, PASS, PACK], BF16, f"w2_g{b}")
+            src = w2_raw[b].rearrange("p j (q t h i) -> p t q h j i", q=16, t=PACK, h=2)
+            dst = grouped[:].rearrange("p (t q h i) j -> p t q h j i", q=16, t=PACK, h=2)
+            for t in range(PACK):
+                nc.vector.tensor_copy(dst[:, t], src[:, t])
+            return quantise(f"w2_q{b}", grouped)
+
+        used = []
+
+        def next_bank():
+            used.append(None)
+            i = len(used) - 1
+            return psum.tile([P, BANK], F32, name=f"acc{i}", tag=f"bank{i % BANKS}")
+
+        def project(role, s, lhs, lhs_scale):
+            x = ring.tile([P, S], F32, name=f"x1_{s}", tag="x1") if role == 1 else kept([P, S], F32, f"x{role}_{s}")
+            for h in range(S // BANK):
+                acc = next_bank()
+                nc.tensor.matmul_mx(acc[:], lhsT=lhs, lhsT_scale=lhs_scale, rhs=v_w[h][:].bitcast(FP8X4),
+                                    rhs_scale=v_s[h][:], start=True, stop=True)
+                if (role, s, h) in VECTOR_EVACS:
+                    nc.vector.tensor_copy(x[:, h * BANK : (h + 1) * BANK], acc[:])
+                else:
+                    nc.scalar.copy(x[:, h * BANK : (h + 1) * BANK], acc[:])
+            return x
+
+        z = [kept([P, PACK, M], F32, f"z{b}") for b in range(PASSES)]
+        w2_q, w4_q, z_q, gated = {}, {}, {}, {}
+        z_last = []
+
+        def lead_and_domestique(s):
+            c = slice(s * P, (s + 1) * P)
+            x1 = project(1, s, w1_w[:, 2 * s * P : 2 * (s + 1) * P].bitcast(FP4X4), w1_s[:, c])
+            x3 = project(3, s, w3_w[:, 4 * s * P : 4 * (s + 1) * P].bitcast(FP8X4), w3_s[:, c])
+            lead = ring.tile([P, M], F32, name=f"lead{s}", tag="lead")
+            nc.scalar.activation(lead[:], x1[:].indirect(pos1_sb[:]), SIGMOID)
+            both = ring.tile([P, M], F32, name=f"gated{s}", tag="gated", bufs=4)
+            nc.vector.tensor_tensor(both[:], x3[:].indirect(pos3_sb[:]), lead[:], MULT)
+            gated.setdefault(s, both)
+
+        def chaser(s):
+            b, t = divmod(s, PACK)
+            if t == 0:
+                w2_q.setdefault(b, quantise_w2(b))
+            c = slice(t * P, (t + 1) * P)
+            x2 = project(2, s, w2_q[b][0][:, c].bitcast(FP8X4), w2_q[b][1][:, c])
+            if s < SLICES - 1:
+                nc.vector.tensor_tensor(z[b][:, t, :], x2[:].indirect(pos2_sb[:]), gated[s][:], MULT)
+            else:
+                for h in range(HALVES):
+                    m = slice(h * HALF, (h + 1) * HALF)
+                    picks = pos2_sb[:, h * HALF // 16 : (h + 1) * HALF // 16]
+                    nc.vector.tensor_tensor(z[b][:, t, m], x2[:].indirect(picks), gated[s][:, m], MULT)
+                    z_last.append(quantise(f"z_last_q{h}", interleave(f"z_last_g{h}", z[b][:, :, m], (nc.scalar.copy, nc.vector.tensor_copy)[h])))
+            if t == 1:
+                w4_q.setdefault(b, quantise(f"w4_q{b}", interleave(f"w4_g{b}", w4_raw[b])))
+            if s == PACK - 1:
+                z_q.setdefault(b, quantise(f"z_q{b}", interleave(f"z_g{b}", z[b][:])))
+
+        for step in range(SLICES + X2_LAG):
+            if step < SLICES:
+                lead_and_domestique(step)
+            if step >= X2_LAG:
+                chaser(step - X2_LAG)
+
+        accs = [[next_bank() for j in range(N // P)] for h in range(HALVES)]
+        for b in range(PASSES):
+            for h in range(HALVES):
+                m = slice(h * HALF, (h + 1) * HALF)
+                words, scales = (z_q[0][0][:, m], z_q[0][1][:, m]) if b == 0 else (z_last[h][0][:], z_last[h][1][:])
+                for j in range(N // P):
+                    c = slice(j * P, (j + 1) * P)
+                    nc.tensor.matmul_mx(accs[h][j][:, 0:HALF], lhsT=w4_q[b][0][:, c].bitcast(FP8X4), lhsT_scale=w4_q[b][1][:, c],
+                                        rhs=words.bitcast(FP8X4), rhs_scale=scales, start=(b == 0), stop=(b == PASSES - 1))
+        out_rows = out.rearrange("(j p) m -> p j m", p=P)
+        for h in range(HALVES):
+            for pair in range(2):
+                res = kept([P, 2, HALF], F32, f"res{h}_{pair}")
+                copy = nc.vector.tensor_copy if (h, pair) == (1, 1) else nc.scalar.copy
+                for j in range(2):
+                    copy(res[:, j, :], accs[h][2 * pair + j][:, 0:HALF])
+                nc.sync.dma_start(out_rows[:, 2 * pair : 2 * pair + 2, h * HALF : (h + 1) * HALF], res[:])

@@ -19,15 +19,19 @@ SIGMOID = mybir.ActivationFunctionType.Sigmoid
 P = 128
 PACK = 4
 PASS = P * PACK
-BANK = 512
-BANKS = 8
+BLOCKS = PASS // 32
+RUN = 32 // PACK
 PASSES = H // PASS
 SLICES = PASSES * PACK
-RUN = 8
+BANK = 512
+BANKS = 8
+PARTS = S // BANK
+PER_COLUMN = 16
+LINE = 4
 HALVES = 2
 HALF = M // HALVES
-X2_LAG = 1
-VECTOR_EVACS = ((3, 0, 0), (3, 0, 1), (2, 2, 1), (2, 4, 1), (2, 5, 1))
+GPSIMD_CLEARS = T // 4
+VECTOR_EMPTIES = 3
 
 
 def tile_list_breakaway_gap_scores_kernel(
@@ -36,177 +40,179 @@ def tile_list_breakaway_gap_scores_kernel(
     nc = tc.nc
     with ExitStack() as ctx:
         keep = ctx.enter_context(tc.tile_pool(name="keep", bufs=1))
-        ring = ctx.enter_context(tc.tile_pool(name="ring", bufs=3))
+        ring = ctx.enter_context(tc.tile_pool(name="ring", bufs=4))
         psum = ctx.enter_context(tc.psum_pool(name="psum", bufs=1))
 
-        def kept(shape, dtype, name, tag=""):
-            return keep.tile(shape, dtype, name=name, tag=tag or name, align_bytes=64)
+        def kept(shape, dtype, name, after=""):
+            return keep.tile(shape, dtype, name=name, tag=after or name, align_bytes=64)
 
-        offs_sb = keep.tile([P, S // 16], U16, name="offs_sb")
-        pos1_sb = keep.tile([P, M // 16], U16, name="pos1_sb")
-        pos2_sb = keep.tile([P, M // 16], U16, name="pos2_sb")
-        pos3_sb = keep.tile([P, M // 16], U16, name="pos3_sb")
-        tab_w = kept([P, T], I32, "tab_w", "slot_c")
-        tab_s = kept([P, T], U8, "tab_s", "slot_b")
-        w1_raw = kept([P, 2 * H], U8, "w1_raw", "slot_a")
-        w1s_raw = kept([P, H], U8, "w1s_raw", "slot_e")
+        def load_scale_rows(plane, scales):
+            for quadrant in range(4):
+                rows = plane[32 * quadrant : 32 * quadrant + 4, :]
+                nc.sync.dma_start(rows.bitcast(I32), scales[0, 4 * quadrant : 4 * quadrant + 4, :].bitcast(I32))
 
-        def load_scale_rows(queue, plane, scales):
-            for q in range(4):
-                queue.dma_start(plane[32 * q : 32 * q + 4, :].bitcast(I32), scales[0, 4 * q : 4 * q + 4, :].bitcast(I32))
+        def load_w2(b, after):
+            raw = kept([P, PACK, PASS], F32, f"w2_raw{b}", after)
+            nc.sync.dma_start(raw[:], w2[:, b * PASS : (b + 1) * PASS].rearrange("(p j) c -> p j c", j=PACK))
+            return raw
 
-        nc.vector.memset(tab_s[:].bitcast(I32), 0)
-        nc.sync.dma_start(offs_sb[:], offs)
-        load_scale_rows(nc.sync, w1s_raw, w1_scales)
-        nc.sync.dma_start(w1_raw[:].bitcast(I32), w1_words[0].bitcast(I32))
-        nc.sync.dma_start(pos1_sb[:], pos1)
-        nc.sync.dma_start(tab_w[:], tab_words[0].rearrange("p t i -> p (t i)").bitcast(I32))
-        nc.sync.dma_start(pos3_sb[:], pos3)
-        nc.sync.dma_start(pos2_sb[:], pos2)
-        load_scale_rows(nc.scalar, tab_s, tab_scales)
-
-        warm = kept([P, 1], F32, "warm", "slot_d")
-        warm_out = keep.tile([P, 1], F32, name="warm_out")
-        nc.gpsimd.memset(warm[:], 0.0)
-        nc.scalar.activation(warm_out[:], warm[:], SIGMOID)
-
-        v_w = [kept([P, BANK], I32, f"v_w{h}") for h in range(S // BANK)]
-        v_s = [kept([P, BANK], U8, f"v_s{h}") for h in range(S // BANK)]
-        cols = BANK // 16
-
-        def reorder_into(done, raw):
-            src = raw.bitcast(I32).rearrange("p (b q t w) -> p b q t w", b=PASSES, q=16, t=PACK)
-            dst = done.bitcast(I32).rearrange("p (b t q w) -> p b q t w", b=PASSES, q=16, t=PACK)
-            nc.vector.tensor_copy(dst, src)
-
-        def reorder(name, raw, dtype, width):
-            done = kept([P, width], dtype, name)
-            reorder_into(done[:], raw)
-            return done
-
-        w1_w = reorder("w1_w", w1_raw[:], U8, 2 * H)
-        w1_s = kept([P, H], U8, "w1_s")
-        nc.gpsimd.memset(w1_s[:].bitcast(I32), 0)
-        for q in range(4):
-            reorder_into(w1_s[32 * q : 32 * q + 4, :], w1s_raw[32 * q : 32 * q + 4, :])
-        for h in range(S // BANK):
-            nc.vector.tensor_copy(v_s[h][:], tab_s[:].indirect(offs_sb[:, h * cols : (h + 1) * cols]))
-        w3s_raw = kept([P, H], U8, "w3s_raw", "slot_e")
-        nc.gpsimd.memset(w3s_raw[:].bitcast(I32), 0)
-        load_scale_rows(nc.scalar, w3s_raw, w3_scales)
-        w3_raw = kept([P, 4 * H], U8, "w3_raw", "slot_d")[:]
-        nc.sync.dma_start(w3_raw.bitcast(I32), w3_words[0].rearrange("p c i -> p (c i)").bitcast(I32))
-        w2_raw = [kept([P, PACK, PASS], F32, f"w2_raw{b}", ("slot_a", "slot_b")[b])[:] for b in range(PASSES)]
-        for b in range(PASSES):
-            nc.sync.dma_start(w2_raw[b], w2[:, b * PASS : (b + 1) * PASS].rearrange("(p j) c -> p j c", j=PACK))
-        for h in range(S // BANK):
-            nc.vector.tensor_copy(
-                v_w[h][:].bitcast(U32), tab_w[:].bitcast(U32).indirect(offs_sb[:, h * cols : (h + 1) * cols])
-            )
-        w3_w = reorder("w3_w", w3_raw, U8, 4 * H)
-        w3_s = reorder("w3_s", w3s_raw[:], U8, H)
-        w4_both = kept([P, PASSES, PACK, N], F32, "w4_raw", "slot_c")
-        w4_raw = [w4_both[:, b] for b in range(PASSES)]
-        for b in range(PASSES):
+        def load_w4(b, after):
+            raw = kept([P, PACK, N], F32, f"w4_raw{b}", after)
             rows = w4[b * PASS : (b + 1) * PASS, :].rearrange("(q t i) n -> t q i n", t=PACK, i=RUN)
             for t in range(PACK):
-                nc.sync.dma_start(w4_raw[b][:, t, :], rows[t])
+                nc.sync.dma_start(raw[:, t, :], rows[t])
+            return raw
 
-        def quantise(name, grouped):
-            width = grouped.shape[1]
-            words = kept([P, width], I32, name + "_w")
-            scales = kept([P, width], U8, name + "_s")
-            nc.vector.quantize_mx(words[:].bitcast(FP8X4), scales[:], grouped[:].rearrange("p c j -> p (c j)"))
-            return words, scales
+        def in_slice_order(name, raw):
+            ordered = kept(raw.shape, U8, name)
+            src = raw[:].bitcast(I32).rearrange("p (b q t w) -> p b q t w", b=PASSES, q=BLOCKS, t=PACK)
+            dst = ordered[:].bitcast(I32).rearrange("p (b t q w) -> p b q t w", b=PASSES, q=BLOCKS, t=PACK)
+            nc.vector.tensor_copy(dst, src)
+            return ordered
 
-        def interleave(name, planes, copy=nc.vector.tensor_copy):
-            width = planes.shape[2]
-            grouped = kept([P, width, PACK], BF16, name)
+        def interleave(name, planes, after="", copy=nc.vector.tensor_copy):
+            grouped = kept([P, planes.shape[2], PACK], BF16, name, after)
             copy(
-                grouped[:].rearrange("p (c i) j -> p c j i", i=4), planes.rearrange("p j (c i) -> p c j i", i=4)
+                grouped[:].rearrange("p (c i) j -> p c j i", i=LINE),
+                planes.rearrange("p j (c i) -> p c j i", i=LINE),
             )
             return grouped
 
-        def quantise_w2(b):
-            grouped = kept([P, PASS, PACK], BF16, f"w2_g{b}")
-            src = w2_raw[b].rearrange("p j (q t h i) -> p t q h j i", q=16, t=PACK, h=2)
-            dst = grouped[:].rearrange("p (t q h i) j -> p t q h j i", q=16, t=PACK, h=2)
+        def quantise(name, grouped):
+            words = kept([P, grouped.shape[1]], I32, name + "_words")
+            scales = kept([P, grouped.shape[1]], U8, name + "_scales")
+            nc.vector.quantize_mx(words[:].bitcast(FP8X4), scales[:], grouped[:].rearrange("p c j -> p (c j)"))
+            return words, scales
+
+        def quantise_w2(b, after):
+            grouped = kept([P, PASS, PACK], BF16, f"w2_grouped{b}", after)
+            src = w2_raw[b][:].rearrange("p j (q t u i) -> p t q u j i", q=BLOCKS, t=PACK, i=LINE)
+            dst = grouped[:].rearrange("p (t q u i) j -> p t q u j i", q=BLOCKS, t=PACK, i=LINE)
             for t in range(PACK):
                 nc.vector.tensor_copy(dst[:, t], src[:, t])
-            return quantise(f"w2_q{b}", grouped)
+            return quantise(f"w2_{b}", grouped)
 
-        used = []
+        taken = []
 
         def next_bank():
-            used.append(None)
-            i = len(used) - 1
-            return psum.tile([P, BANK], F32, name=f"acc{i}", tag=f"bank{i % BANKS}")
+            taken.append(psum.tile([P, BANK], F32, name=f"acc{len(taken)}", tag=f"bank{len(taken) % BANKS}"))
+            return taken[-1]
 
-        def project(role, s, lhs, lhs_scale):
-            x = ring.tile([P, S], F32, name=f"x1_{s}", tag="x1") if role == 1 else kept([P, S], F32, f"x{role}_{s}")
-            for h in range(S // BANK):
+        offs_sb = keep.tile([P, S // PER_COLUMN], U16, name="offs_sb")
+        pos1_sb = keep.tile([P, M // PER_COLUMN], U16, name="pos1_sb")
+        pos2_sb = keep.tile([P, M // PER_COLUMN], U16, name="pos2_sb")
+        pos3_sb = keep.tile([P, M // PER_COLUMN], U16, name="pos3_sb")
+        tab_s = kept([P, T], U8, "tab_s")
+        w1_raw = kept([P, 2 * H], U8, "w1_raw")
+        w1s_raw = kept([P, H], U8, "w1s_raw")
+        w3s_raw = kept([P, H], U8, "w3s_raw")
+        warm_bias = kept([P, 1], F32, "warm_bias")
+        warm_out = kept([P, 1], F32, "warm_out")
+        nc.gpsimd.memset(tab_s[:, 0:GPSIMD_CLEARS].bitcast(I32), 0)
+        nc.vector.memset(tab_s[:, GPSIMD_CLEARS:T].bitcast(I32), 0)
+        nc.gpsimd.memset(w1s_raw[:].bitcast(I32), 0)
+        nc.gpsimd.memset(w3s_raw[:].bitcast(I32), 0)
+        nc.gpsimd.memset(warm_bias[:], 0.0)
+
+        nc.scalar.activation(
+            warm_out[:], w1s_raw[:, 0:4].bitcast(F32), SIGMOID, bias=warm_bias[:], scale=w3s_raw[:, 0:4].bitcast(F32)
+        )
+        for picks_sb, picks in ((offs_sb, offs), (pos1_sb, pos1), (pos3_sb, pos3), (pos2_sb, pos2)):
+            nc.sync.dma_start(picks_sb[:], picks)
+        nc.sync.dma_start(w1_raw[:].bitcast(I32), w1_words[0].bitcast(I32))
+        load_scale_rows(tab_s, tab_scales)
+        tab_w = kept([P, T], I32, "tab_w", after="warm_out")
+        nc.sync.dma_start(tab_w[:], tab_words[0].rearrange("p t i -> p (t i)").bitcast(I32))
+        load_scale_rows(w1s_raw, w1_scales)
+        w3_raw = kept([P, PACK * H], U8, "w3_raw", after="warm_bias")
+        nc.sync.dma_start(w3_raw[:].bitcast(I32), w3_words[0].rearrange("p c i -> p (c i)").bitcast(I32))
+        load_scale_rows(w3s_raw, w3_scales)
+
+        part_offs = [offs_sb[:, h * BANK // PER_COLUMN : (h + 1) * BANK // PER_COLUMN] for h in range(PARTS)]
+        w1_w = in_slice_order("w1_w", w1_raw)
+        v_s = [kept([P, BANK], U8, f"v_s{h}") for h in range(PARTS)]
+        for h in range(PARTS):
+            nc.vector.tensor_copy(v_s[h][:], tab_s[:].indirect(part_offs[h]))
+        w2_raw = [load_w2(0, after="tab_s")]
+        w1_s = in_slice_order("w1_s", w1s_raw)
+        v_w = [kept([P, BANK], I32, "v_w0"), kept([P, BANK], I32, "v_w1", after="w1s_raw")]
+        for h in range(PARTS):
+            nc.vector.tensor_copy(v_w[h][:].bitcast(U32), tab_w[:].bitcast(U32).indirect(part_offs[h]))
+        w2_raw.append(load_w2(1, after="warm_out"))
+        w3_w = in_slice_order("w3_w", w3_raw)
+        w3_s = in_slice_order("w3_s", w3s_raw)
+        w4_raw = [load_w4(0, after="warm_bias")]
+
+        def project(x, s, lhs, lhs_scale, banks_on_vector=0):
+            for h in range(PARTS):
                 acc = next_bank()
-                nc.tensor.matmul_mx(acc[:], lhsT=lhs, lhsT_scale=lhs_scale, rhs=v_w[h][:].bitcast(FP8X4),
-                                    rhs_scale=v_s[h][:], start=True, stop=True)
-                if (role, s, h) in VECTOR_EVACS:
-                    nc.vector.tensor_copy(x[:, h * BANK : (h + 1) * BANK], acc[:])
-                else:
-                    nc.scalar.copy(x[:, h * BANK : (h + 1) * BANK], acc[:])
-            return x
+                nc.tensor.matmul_mx(
+                    acc[:], lhsT=lhs, lhsT_scale=lhs_scale, rhs=v_w[h][:].bitcast(FP8X4), rhs_scale=v_s[h][:],
+                    start=True, stop=True,
+                )
+                copy = nc.vector.tensor_copy if s * PARTS + h < banks_on_vector else nc.scalar.copy
+                copy(x[:, h * BANK : (h + 1) * BANK], acc[:])
 
         z = [kept([P, PACK, M], F32, f"z{b}") for b in range(PASSES)]
-        w2_q, w4_q, z_q, gated = {}, {}, {}, {}
-        z_last = []
+        gated, w2_q, w4_q, z_first, z_last = [], [], [], [], []
 
-        def lead_and_domestique(s):
-            c = slice(s * P, (s + 1) * P)
-            x1 = project(1, s, w1_w[:, 2 * s * P : 2 * (s + 1) * P].bitcast(FP4X4), w1_s[:, c])
-            x3 = project(3, s, w3_w[:, 4 * s * P : 4 * (s + 1) * P].bitcast(FP8X4), w3_s[:, c])
+        def gate(s):
+            cols = slice(s * P, (s + 1) * P)
+            x1 = ring.tile([P, S], F32, name=f"x1_{s}", tag="x1", bufs=3)
+            project(x1, s, w1_w[:, 2 * s * P : 2 * (s + 1) * P].bitcast(FP4X4), w1_s[:, cols])
             lead = ring.tile([P, M], F32, name=f"lead{s}", tag="lead")
             nc.scalar.activation(lead[:], x1[:].indirect(pos1_sb[:]), SIGMOID)
-            both = ring.tile([P, M], F32, name=f"gated{s}", tag="gated", bufs=4)
-            nc.vector.tensor_tensor(both[:], x3[:].indirect(pos3_sb[:]), lead[:], MULT)
-            gated.setdefault(s, both)
+            x3 = kept([P, S], F32, f"x3_{s}")
+            project(x3, s, w3_w[:, PACK * s * P : PACK * (s + 1) * P].bitcast(FP8X4), w3_s[:, cols], VECTOR_EMPTIES)
+            gated.append(ring.tile([P, M], F32, name=f"gated{s}", tag="gated"))
+            nc.vector.tensor_tensor(gated[s][:], x3[:].indirect(pos3_sb[:]), lead[:], MULT)
 
-        def chaser(s):
+        def chase(s):
             b, t = divmod(s, PACK)
             if t == 0:
-                w2_q.setdefault(b, quantise_w2(b))
-            c = slice(t * P, (t + 1) * P)
-            x2 = project(2, s, w2_q[b][0][:, c].bitcast(FP8X4), w2_q[b][1][:, c])
+                w2_q.append(quantise_w2(b, after="x2_0" if b else ""))
+            if s == 0:
+                w4_raw.append(load_w4(1, after="tab_s"))
+            cols = slice(t * P, (t + 1) * P)
+            x2 = kept([P, S], F32, f"x2_{s}")
+            project(x2, s, w2_q[b][0][:, cols].bitcast(FP8X4), w2_q[b][1][:, cols])
             if s < SLICES - 1:
                 nc.vector.tensor_tensor(z[b][:, t, :], x2[:].indirect(pos2_sb[:]), gated[s][:], MULT)
             else:
-                for h in range(HALVES):
-                    m = slice(h * HALF, (h + 1) * HALF)
-                    picks = pos2_sb[:, h * HALF // 16 : (h + 1) * HALF // 16]
+                for half, copy in enumerate((nc.scalar.copy, nc.vector.tensor_copy)):
+                    m = slice(half * HALF, (half + 1) * HALF)
+                    picks = pos2_sb[:, half * HALF // PER_COLUMN : (half + 1) * HALF // PER_COLUMN]
                     nc.vector.tensor_tensor(z[b][:, t, m], x2[:].indirect(picks), gated[s][:, m], MULT)
-                    z_last.append(quantise(f"z_last_q{h}", interleave(f"z_last_g{h}", z[b][:, :, m], (nc.scalar.copy, nc.vector.tensor_copy)[h])))
-            if t == 1:
-                w4_q.setdefault(b, quantise(f"w4_q{b}", interleave(f"w4_g{b}", w4_raw[b])))
+                    grouped = interleave(f"z_last_grouped{half}", z[b][:, :, m], "z_last_grouped0", copy)
+                    z_last.append(quantise(f"z_last{half}", grouped))
+            if 1 <= s <= PASSES:
+                w4_q.append(quantise(f"w4_{s - 1}", interleave(f"w4_grouped{s - 1}", w4_raw[s - 1][:], f"x2_{s}")))
             if s == PACK - 1:
-                z_q.setdefault(b, quantise(f"z_q{b}", interleave(f"z_g{b}", z[b][:])))
+                z_first.extend(quantise("z_first", interleave("z_first_grouped", z[0][:])))
 
-        for step in range(SLICES + X2_LAG):
-            if step < SLICES:
-                lead_and_domestique(step)
-            if step >= X2_LAG:
-                chaser(step - X2_LAG)
+        for s in range(SLICES + 1):
+            if s < SLICES:
+                gate(s)
+            if s >= 1:
+                chase(s - 1)
 
-        accs = [[next_bank() for j in range(N // P)] for h in range(HALVES)]
+        accs = [[next_bank() for j in range(N // P)] for half in range(HALVES)]
         for b in range(PASSES):
-            for h in range(HALVES):
-                m = slice(h * HALF, (h + 1) * HALF)
-                words, scales = (z_q[0][0][:, m], z_q[0][1][:, m]) if b == 0 else (z_last[h][0][:], z_last[h][1][:])
+            for half in range(HALVES):
+                m = slice(half * HALF, (half + 1) * HALF)
+                words, scales = (z_first[0][:, m], z_first[1][:, m]) if b == 0 else (z_last[half][0][:], z_last[half][1][:])
                 for j in range(N // P):
-                    c = slice(j * P, (j + 1) * P)
-                    nc.tensor.matmul_mx(accs[h][j][:, 0:HALF], lhsT=w4_q[b][0][:, c].bitcast(FP8X4), lhsT_scale=w4_q[b][1][:, c],
-                                        rhs=words.bitcast(FP8X4), rhs_scale=scales, start=(b == 0), stop=(b == PASSES - 1))
+                    cols = slice(j * P, (j + 1) * P)
+                    nc.tensor.matmul_mx(
+                        accs[half][j][:, 0:HALF], lhsT=w4_q[b][0][:, cols].bitcast(FP8X4), lhsT_scale=w4_q[b][1][:, cols],
+                        rhs=words.bitcast(FP8X4), rhs_scale=scales, start=(b == 0), stop=(b == PASSES - 1),
+                    )
+
         out_rows = out.rearrange("(j p) m -> p j m", p=P)
-        for h in range(HALVES):
+        for half in range(HALVES):
             for pair in range(2):
-                res = kept([P, 2, HALF], F32, f"res{h}_{pair}")
-                copy = nc.vector.tensor_copy if (h, pair) == (1, 1) else nc.scalar.copy
+                res = kept([P, 2, HALF], F32, f"res{half}_{pair}")
+                copy = nc.vector.tensor_copy if (half, pair) == (HALVES - 1, 1) else nc.scalar.copy
                 for j in range(2):
-                    copy(res[:, j, :], accs[h][2 * pair + j][:, 0:HALF])
-                nc.sync.dma_start(out_rows[:, 2 * pair : 2 * pair + 2, h * HALF : (h + 1) * HALF], res[:])
+                    copy(res[:, j, :], accs[half][2 * pair + j][:, 0:HALF])
+                nc.sync.dma_start(out_rows[:, 2 * pair : 2 * pair + 2, half * HALF : (half + 1) * HALF], res[:])

@@ -47,9 +47,8 @@ def tile_list_breakaway_gap_scores_kernel(
             return keep.tile(shape, dtype, name=name, tag=after or name, align_bytes=64)
 
         def load_scale_rows(plane, scales):
-            for quadrant in range(4):
-                rows = plane[32 * quadrant : 32 * quadrant + 4, :]
-                nc.sync.dma_start(rows.bitcast(I32), scales[0, 4 * quadrant : 4 * quadrant + 4, :].bitcast(I32))
+            for r in range(4):
+                nc.sync.dma_start(plane[r:P:32, :].bitcast(I32), scales[0, r:BLOCKS:4, :].bitcast(I32))
 
         def load_w2(b, after):
             raw = kept([P, PACK, PASS], F32, f"w2_raw{b}", after)

@@ -28,10 +28,12 @@ BANKS = 8
 PARTS = S // BANK
 PER_COLUMN = 16
 LINE = 4
-HALVES = 2
-HALF = M // HALVES
+CHUNKS = (slice(0, 256), slice(256, 384), slice(384, 512))
 GPSIMD_CLEARS = T // 4
-VECTOR_EMPTIES = 3
+VECTOR_BANKS = 2
+LAG = 3
+EARLY = 3
+LATE_ON_VECTOR = 2
 
 
 def tile_list_breakaway_gap_scores_kernel(
@@ -77,8 +79,8 @@ def tile_list_breakaway_gap_scores_kernel(
             )
             return grouped
 
-        def quantise(name, grouped):
-            words = kept([P, grouped.shape[1]], I32, name + "_words")
+        def quantise(name, grouped, after=""):
+            words = kept([P, grouped.shape[1]], I32, name + "_words", after)
             scales = kept([P, grouped.shape[1]], U8, name + "_scales")
             nc.vector.quantize_mx(words[:].bitcast(FP8X4), scales[:], grouped[:].rearrange("p c j -> p (c j)"))
             return words, scales
@@ -91,11 +93,13 @@ def tile_list_breakaway_gap_scores_kernel(
                 nc.vector.tensor_copy(dst[:, t], src[:, t])
             return quantise(f"w2_{b}", grouped)
 
-        taken = []
+        taken = {True: [], False: []}
 
-        def next_bank():
-            taken.append(psum.tile([P, BANK], F32, name=f"acc{len(taken)}", tag=f"bank{len(taken) % BANKS}"))
-            return taken[-1]
+        def next_bank(on_vector):
+            mine = taken[on_vector]
+            bank = len(mine) % VECTOR_BANKS if on_vector else VECTOR_BANKS + len(mine) % (BANKS - VECTOR_BANKS)
+            mine.append(psum.tile([P, BANK], F32, name=f"acc{bank}_{len(mine)}", tag=f"bank{bank}"))
+            return mine[-1]
 
         offs_sb = keep.tile([P, S // PER_COLUMN], U16, name="offs_sb")
         pos1_sb = keep.tile([P, M // PER_COLUMN], U16, name="pos1_sb")
@@ -142,76 +146,115 @@ def tile_list_breakaway_gap_scores_kernel(
         w3_s = in_slice_order("w3_s", w3s_raw)
         w4_raw = [load_w4(0, after="warm_bias")]
 
-        def project(x, s, lhs, lhs_scale, banks_on_vector=0):
-            for h in range(PARTS):
-                acc = next_bank()
-                nc.tensor.matmul_mx(
-                    acc[:], lhsT=lhs, lhsT_scale=lhs_scale, rhs=v_w[h][:].bitcast(FP8X4), rhs_scale=v_s[h][:],
-                    start=True, stop=True,
-                )
-                copy = nc.vector.tensor_copy if s * PARTS + h < banks_on_vector else nc.scalar.copy
-                copy(x[:, h * BANK : (h + 1) * BANK], acc[:])
+        def project(x, h, lhs, lhs_scale, on_vector=False):
+            acc = next_bank(on_vector)
+            nc.tensor.matmul_mx(
+                acc[:], lhsT=lhs, lhsT_scale=lhs_scale, rhs=v_w[h][:].bitcast(FP8X4), rhs_scale=v_s[h][:],
+                start=True, stop=True,
+            )
+            copy = nc.vector.tensor_copy if on_vector else nc.scalar.copy
+            copy(x[:, h * BANK : (h + 1) * BANK], acc[:])
 
-        z = [kept([P, PACK, M], F32, f"z{b}") for b in range(PASSES)]
-        gated, w2_q, w4_q, z_first, z_last = [], [], [], [], []
+        x1 = [kept([P, S], F32, f"x1_{s}") for s in range(SLICES)]
+
+        def project_x1(s, h):
+            cols = slice(s * P, (s + 1) * P)
+            project(x1[s], h, w1_w[:, 2 * s * P : 2 * (s + 1) * P].bitcast(FP4X4), w1_s[:, cols], s == 1)
+
+        z = kept([P, PACK, M], F32, "z")
+        z_lead = kept([P, PACK, CHUNKS[0].stop], F32, "z_lead")
+        gated, x2, w2_q, w4_q, z_first = [], [], [], [], []
+
+        def columns(picks_sb, m):
+            return picks_sb[:, m.start // PER_COLUMN : m.stop // PER_COLUMN]
 
         def gate(s):
             cols = slice(s * P, (s + 1) * P)
-            x1 = ring.tile([P, S], F32, name=f"x1_{s}", tag="x1", bufs=3)
-            project(x1, s, w1_w[:, 2 * s * P : 2 * (s + 1) * P].bitcast(FP4X4), w1_s[:, cols])
+            for h in range(1 if s < EARLY else 0, PARTS):
+                project_x1(s, h)
             lead = ring.tile([P, M], F32, name=f"lead{s}", tag="lead")
-            nc.scalar.activation(lead[:], x1[:].indirect(pos1_sb[:]), SIGMOID)
+            nc.scalar.activation(lead[:], x1[s][:].indirect(pos1_sb[:]), SIGMOID)
             x3 = kept([P, S], F32, f"x3_{s}")
-            project(x3, s, w3_w[:, PACK * s * P : PACK * (s + 1) * P].bitcast(FP8X4), w3_s[:, cols], VECTOR_EMPTIES)
-            gated.append(ring.tile([P, M], F32, name=f"gated{s}", tag="gated"))
-            nc.vector.tensor_tensor(gated[s][:], x3[:].indirect(pos3_sb[:]), lead[:], MULT)
+            for h in range(PARTS):
+                on_vector = s == 0 or (h == 0 and s >= SLICES - LATE_ON_VECTOR)
+                project(x3, h, w3_w[:, PACK * s * P : PACK * (s + 1) * P].bitcast(FP8X4), w3_s[:, cols], on_vector)
+            if s < SLICES - 1:
+                whole = kept([P, M], F32, f"gated{s}")
+                nc.vector.tensor_tensor(whole[:], x3[:].indirect(pos3_sb[:]), lead[:], MULT)
+                gated.append([whole[:, m] for m in CHUNKS] + [whole[:]])
+            else:
+                split = CHUNKS[0].stop
+                first, rest = kept([P, split], F32, "gated_first"), kept([P, M - split], F32, "gated_rest")
+                for part, m in ((first, CHUNKS[0]), (rest, slice(split, M))):
+                    nc.vector.tensor_tensor(part[:], x3[:].indirect(columns(pos3_sb, m)), lead[:, m], MULT)
+                gated.append([first[:]] + [rest[:, m.start - split : m.stop - split] for m in CHUNKS[1:]])
+            if s == 0:
+                w2_q.append(quantise_w2(0, after=""))
+                w4_raw.append(load_w4(1, after="tab_s"))
+            elif s == 1:
+                w2_q.append(quantise_w2(1, after="x3_1"))
+            elif s < 2 + PASSES:
+                w4_q.append(quantise(f"w4_{s - 2}", interleave(f"w4_grouped{s - 2}", w4_raw[s - 2][:], f"x3_{s}")))
 
         def chase(s):
             b, t = divmod(s, PACK)
-            if t == 0:
-                w2_q.append(quantise_w2(b, after="x2_0" if b else ""))
-            if s == 0:
-                w4_raw.append(load_w4(1, after="tab_s"))
             cols = slice(t * P, (t + 1) * P)
-            x2 = kept([P, S], F32, f"x2_{s}")
-            project(x2, s, w2_q[b][0][:, cols].bitcast(FP8X4), w2_q[b][1][:, cols])
-            if s < SLICES - 1:
-                nc.vector.tensor_tensor(z[b][:, t, :], x2[:].indirect(pos2_sb[:]), gated[s][:], MULT)
+            x2.append(kept([P, S], F32, f"x2_{s}", after=f"x1_{s}"))
+            for h in range(PARTS):
+                project(x2[s], h, w2_q[b][0][:, cols].bitcast(FP8X4), w2_q[b][1][:, cols])
+            if b == 0:
+                nc.vector.tensor_tensor(z[:, t, :], x2[s][:].indirect(pos2_sb[:]), gated[s][-1], MULT)
             else:
-                for half, copy in enumerate((nc.scalar.copy, nc.vector.tensor_copy)):
-                    m = slice(half * HALF, (half + 1) * HALF)
-                    picks = pos2_sb[:, half * HALF // PER_COLUMN : (half + 1) * HALF // PER_COLUMN]
-                    nc.vector.tensor_tensor(z[b][:, t, m], x2[:].indirect(picks), gated[s][:, m], MULT)
-                    grouped = interleave(f"z_last_grouped{half}", z[b][:, :, m], "z_last_grouped0", copy)
-                    z_last.append(quantise(f"z_last{half}", grouped))
-            if 1 <= s <= PASSES:
-                w4_q.append(quantise(f"w4_{s - 1}", interleave(f"w4_grouped{s - 1}", w4_raw[s - 1][:], f"x2_{s}")))
+                nc.vector.tensor_tensor(z_lead[:, t, :], x2[s][:].indirect(columns(pos2_sb, CHUNKS[0])), gated[s][0], MULT)
             if s == PACK - 1:
-                z_first.extend(quantise("z_first", interleave("z_first_grouped", z[0][:])))
+                z_first.extend(quantise("z_first", interleave("z_first_grouped", z[:])))
 
-        for s in range(SLICES + 1):
+        for s in range(EARLY):
+            project_x1(s, 0)
+        for s in range(SLICES + LAG):
             if s < SLICES:
                 gate(s)
-            if s >= 1:
-                chase(s - 1)
+            if s >= LAG:
+                chase(s - LAG)
 
-        accs = [[next_bank() for j in range(N // P)] for half in range(HALVES)]
-        for b in range(PASSES):
-            for half in range(HALVES):
-                m = slice(half * HALF, (half + 1) * HALF)
-                words, scales = (z_first[0][:, m], z_first[1][:, m]) if b == 0 else (z_last[half][0][:], z_last[half][1][:])
-                for j in range(N // P):
-                    cols = slice(j * P, (j + 1) * P)
-                    nc.tensor.matmul_mx(
-                        accs[half][j][:, 0:HALF], lhsT=w4_q[b][0][:, cols].bitcast(FP8X4), lhsT_scale=w4_q[b][1][:, cols],
-                        rhs=words.bitcast(FP8X4), rhs_scale=scales, start=(b == 0), stop=(b == PASSES - 1),
-                    )
+        accs = [[next_bank(False) for pair in range(2)] for m in CHUNKS]
+
+        def product(c, b, words, scales):
+            width = CHUNKS[c].stop - CHUNKS[c].start
+            for j in range(N // P):
+                cols = slice(j * P, (j + 1) * P)
+                nc.tensor.matmul_mx(
+                    accs[c][j // 2][:, j % 2 * width : (j % 2 + 1) * width],
+                    lhsT=w4_q[b][0][:, cols].bitcast(FP8X4), lhsT_scale=w4_q[b][1][:, cols],
+                    rhs=words.bitcast(FP8X4), rhs_scale=scales,
+                    start=(b == 0 and j % 2 == 0), stop=(b == PASSES - 1 and j % 2 == 1),
+                )
+
+        for c, m in enumerate(CHUNKS):
+            product(c, 0, z_first[0][:, m], z_first[1][:, m])
 
         out_rows = out.rearrange("(j p) m -> p j m", p=P)
-        for half in range(HALVES):
+        holds = ("", "gated_first", "z_last_grouped0")
+        grouped = []
+        for c, m in enumerate(CHUNKS):
+            width = m.stop - m.start
+            last = c == len(CHUNKS) - 1
+            planes = z_lead
+            if c:
+                planes = kept([P, PACK, width], F32, f"z_last{c}", holds[c])
+                for t in range(PACK):
+                    nc.vector.tensor_tensor(planes[:, t, :], x2[PACK + t][:].indirect(columns(pos2_sb, m)), gated[PACK + t][c], MULT)
+            if c == 1:
+                words, scales = quantise("z_last0", grouped[0])
+                product(0, 1, words[:], scales[:])
+            grouped.append(interleave(f"z_last_grouped{c}", planes[:], copy=nc.vector.tensor_copy if last else nc.scalar.copy))
+        for c in range(1, len(CHUNKS)):
+            words, scales = quantise(f"z_last{c}", grouped[c])
+            product(c, 1, words[:], scales[:])
+        for c, m in enumerate(CHUNKS):
+            width = m.stop - m.start
             for pair in range(2):
-                res = kept([P, 2, HALF], F32, f"res{half}_{pair}")
-                copy = nc.vector.tensor_copy if (half, pair) == (HALVES - 1, 1) else nc.scalar.copy
-                for j in range(2):
-                    copy(res[:, j, :], accs[half][2 * pair + j][:, 0:HALF])
-                nc.sync.dma_start(out_rows[:, 2 * pair : 2 * pair + 2, half * HALF : (half + 1) * HALF], res[:])
+                res = kept([P, 2, width], F32, f"res{c}_{pair}")
+                copy = nc.vector.tensor_copy if pair and c == len(CHUNKS) - 1 else nc.scalar.copy
+                copy(res[:].rearrange("p j m -> p (j m)"), accs[c][pair][:, 0 : 2 * width])
+                nc.sync.dma_start(out_rows[:, 2 * pair : 2 * pair + 2, m], res[:])

@@ -29,8 +29,13 @@ PARTS = S // BANK
 PER_COLUMN = 16
 LINE = 4
 CHUNKS = (slice(0, 256), slice(256, 384), slice(384, 512))
-GPSIMD_CLEARS = T // 4
 VECTOR_BANKS = 2
+RAW_BYTES = PACK * PASS * 4
+W3_AT = H + T
+W2_AT = W3_AT + PACK * H
+W4_AT = W2_AT + PASSES * RAW_BYTES
+TAB_AT = W4_AT + PASSES * RAW_BYTES
+WARM_AT = 4 * S
 LAG = 3
 EARLY = 3
 LATE_ON_VECTOR = 2
@@ -43,31 +48,34 @@ def tile_list_breakaway_gap_scores_kernel(
     with ExitStack() as ctx:
         keep = ctx.enter_context(tc.tile_pool(name="keep", bufs=1))
         ring = ctx.enter_context(tc.tile_pool(name="ring", bufs=4))
+        placed = ctx.enter_context(tc.tile_pool(name="placed", bufs=1))
         psum = ctx.enter_context(tc.psum_pool(name="psum", bufs=1))
 
         def kept(shape, dtype, name, after=""):
             return keep.tile(shape, dtype, name=name, tag=after or name, align_bytes=64)
 
-        def load_scale_rows(plane, scales):
-            for r in range(4):
-                nc.sync.dma_start(plane[r:P:32, :].bitcast(I32), scales[0, r:BLOCKS:4, :].bitcast(I32))
+        def at(offset, shape, dtype, name):
+            return placed.tile(shape, dtype, name=name, offset=offset, align_bytes=64)
 
-        def load_w2(b, after):
-            raw = kept([P, PACK, PASS], F32, f"w2_raw{b}", after)
+        def load_scale_rows(plane, scales, queue):
+            for r in range(4):
+                queue.dma_start(plane[r:P:32, :].bitcast(I32), scales[0, r:BLOCKS:4, :].bitcast(I32))
+
+        def load_w2(b):
+            raw = at(W2_AT + b * RAW_BYTES, [P, PACK, PASS], F32, f"w2_raw{b}")
             nc.sync.dma_start(raw[:], w2[:, b * PASS : (b + 1) * PASS].rearrange("(p j) c -> p j c", j=PACK))
             return raw
 
-        def load_w4(b, after):
-            raw = kept([P, PACK, N], F32, f"w4_raw{b}", after)
+        def load_w4(b):
+            raw = at(W4_AT + b * RAW_BYTES, [P, PACK, N], F32, f"w4_raw{b}")
             rows = w4[b * PASS : (b + 1) * PASS, :].rearrange("(q t i) n -> t q i n", t=PACK, i=RUN)
             for t in range(PACK):
                 nc.sync.dma_start(raw[:, t, :], rows[t])
             return raw
 
-        def in_slice_order(name, raw):
-            ordered = kept(raw.shape, U8, name)
-            src = raw[:].bitcast(I32).rearrange("p (b q t w) -> p b q t w", b=PASSES, q=BLOCKS, t=PACK)
-            dst = ordered[:].bitcast(I32).rearrange("p (b t q w) -> p b q t w", b=PASSES, q=BLOCKS, t=PACK)
+        def in_slice_order(ordered, raw, rows=slice(0, P)):
+            src = raw[rows, :].bitcast(I32).rearrange("p (b q t w) -> p b q t w", b=PASSES, q=BLOCKS, t=PACK)
+            dst = ordered[rows, :].bitcast(I32).rearrange("p (b t q w) -> p b q t w", b=PASSES, q=BLOCKS, t=PACK)
             nc.vector.tensor_copy(dst, src)
             return ordered
 
@@ -79,18 +87,18 @@ def tile_list_breakaway_gap_scores_kernel(
             )
             return grouped
 
-        def quantise(name, grouped, after=""):
-            words = kept([P, grouped.shape[1]], I32, name + "_words", after)
+        def quantise(name, grouped):
+            words = kept([P, grouped.shape[1]], I32, name + "_words")
             scales = kept([P, grouped.shape[1]], U8, name + "_scales")
             nc.vector.quantize_mx(words[:].bitcast(FP8X4), scales[:], grouped[:].rearrange("p c j -> p (c j)"))
             return words, scales
 
         def quantise_w2(b, after):
             grouped = kept([P, PASS, PACK], BF16, f"w2_grouped{b}", after)
-            src = w2_raw[b][:].rearrange("p j (q t u i) -> p t q u j i", q=BLOCKS, t=PACK, i=LINE)
-            dst = grouped[:].rearrange("p (t q u i) j -> p t q u j i", q=BLOCKS, t=PACK, i=LINE)
-            for t in range(PACK):
-                nc.vector.tensor_copy(dst[:, t], src[:, t])
+            nc.vector.tensor_copy(
+                grouped[:].rearrange("p (t q i) j -> p t q j i", q=BLOCKS, t=PACK),
+                w2_raw[b][:].rearrange("p j (q t i) -> p t q j i", q=BLOCKS, t=PACK),
+            )
             return quantise(f"w2_{b}", grouped)
 
         taken = {True: [], False: []}
@@ -105,51 +113,56 @@ def tile_list_breakaway_gap_scores_kernel(
         pos1_sb = keep.tile([P, M // PER_COLUMN], U16, name="pos1_sb")
         pos2_sb = keep.tile([P, M // PER_COLUMN], U16, name="pos2_sb")
         pos3_sb = keep.tile([P, M // PER_COLUMN], U16, name="pos3_sb")
-        tab_s = kept([P, T], U8, "tab_s")
-        w1_raw = kept([P, 2 * H], U8, "w1_raw")
-        w1s_raw = kept([P, H], U8, "w1s_raw")
+        w1s_raw = at(0, [P, H], U8, "w1s_raw")
+        tab_s = at(H, [P, T], U8, "tab_s")
+        tab_w = at(TAB_AT, [P, T], I32, "tab_w")
+        picked_s = kept([P, S], U8, "picked_s")
         w3s_raw = kept([P, H], U8, "w3s_raw")
-        warm_bias = kept([P, 1], F32, "warm_bias")
-        warm_out = kept([P, 1], F32, "warm_out")
-        nc.gpsimd.memset(tab_s[:, 0:GPSIMD_CLEARS].bitcast(I32), 0)
-        nc.vector.memset(tab_s[:, GPSIMD_CLEARS:T].bitcast(I32), 0)
-        nc.gpsimd.memset(w1s_raw[:].bitcast(I32), 0)
+        w1_raw = kept([P, 2 * H], U8, "w1_raw")
+        w1_s = kept([P, H], U8, "w1_s")
+        v_s_all = kept([P, S], U8, "v_s")
+        nc.vector.memset(tab_s[0 : P - BLOCKS, :].bitcast(I32), 0)
         nc.gpsimd.memset(w3s_raw[:].bitcast(I32), 0)
-        nc.gpsimd.memset(warm_bias[:], 0.0)
+        nc.gpsimd.memset(w1_s[:].bitcast(I32), 0)
+        nc.gpsimd.memset(v_s_all[:].bitcast(I32), 0)
 
-        nc.scalar.activation(
-            warm_out[:], w1s_raw[:, 0:4].bitcast(F32), SIGMOID, bias=warm_bias[:], scale=w3s_raw[:, 0:4].bitcast(F32)
-        )
-        for picks_sb, picks in ((offs_sb, offs), (pos1_sb, pos1), (pos3_sb, pos3), (pos2_sb, pos2)):
-            nc.sync.dma_start(picks_sb[:], picks)
+        nc.sync.dma_start(offs_sb[:], offs)
+        nc.sync.dma_start(tab_s[P - BLOCKS : P, :].bitcast(I32), tab_scales[0].bitcast(I32))
         nc.sync.dma_start(w1_raw[:].bitcast(I32), w1_words[0].bitcast(I32))
-        load_scale_rows(tab_s, tab_scales)
-        tab_w = kept([P, T], I32, "tab_w", after="warm_out")
+        load_scale_rows(w1s_raw, w1_scales, nc.sync)
         nc.sync.dma_start(tab_w[:], tab_words[0].rearrange("p t i -> p (t i)").bitcast(I32))
-        load_scale_rows(w1s_raw, w1_scales)
-        w3_raw = kept([P, PACK * H], U8, "w3_raw", after="warm_bias")
-        nc.sync.dma_start(w3_raw[:].bitcast(I32), w3_words[0].rearrange("p c i -> p (c i)").bitcast(I32))
-        load_scale_rows(w3s_raw, w3_scales)
+        for picks_sb, picks in ((pos1_sb, pos1), (pos3_sb, pos3), (pos2_sb, pos2)):
+            nc.sync.dma_start(picks_sb[:], picks)
 
         part_offs = [offs_sb[:, h * BANK // PER_COLUMN : (h + 1) * BANK // PER_COLUMN] for h in range(PARTS)]
-        w1_w = in_slice_order("w1_w", w1_raw)
-        v_s = [kept([P, BANK], U8, f"v_s{h}") for h in range(PARTS)]
-        for h in range(PARTS):
-            nc.vector.tensor_copy(v_s[h][:], tab_s[:].indirect(part_offs[h]))
-        w2_raw = [load_w2(0, after="tab_s")]
-        w1_s = in_slice_order("w1_s", w1s_raw)
-        v_w = [kept([P, BANK], I32, "v_w0"), kept([P, BANK], I32, "v_w1", after="w1s_raw")]
+        nc.vector.tensor_copy(picked_s[:, 0:S], tab_s[:].indirect(offs_sb[:]))
+        for r in range(4):
+            nc.scalar.dma_start(v_s_all[r:P:32, :].bitcast(I32), picked_s[P - BLOCKS + r : P : 4, 0:S].bitcast(I32))
+
+        warm = at(WARM_AT, [P, (TAB_AT - WARM_AT) // 4], F32, "warm")
+        nc.vector.memset(warm[:, 0:1], 0.0)
+        nc.scalar.activation(warm[:, 8:9], warm[:, 0:1], SIGMOID, scale=w3s_raw[:, 0:4].bitcast(F32))
+        v_s = [v_s_all[:, h * BANK : (h + 1) * BANK] for h in range(PARTS)]
+        w1_w = in_slice_order(kept([P, 2 * H], U8, "w1_w"), w1_raw)
+        for quadrant in range(0, P, 32):
+            in_slice_order(w1_s, w1s_raw, slice(quadrant, quadrant + 4))
+
+        w3_raw = at(W3_AT, [P, PACK * H], U8, "w3_raw")
+        nc.sync.dma_start(w3_raw[:].bitcast(I32), w3_words[0].rearrange("p c i -> p (c i)").bitcast(I32))
+        load_scale_rows(w3s_raw, w3_scales, nc.sync)
+        w2_raw = [load_w2(b) for b in range(PASSES)]
+        w4_raw = [load_w4(b) for b in range(PASSES)]
+
+        v_w = [at(h * 4 * BANK, [P, BANK], I32, f"v_w{h}") for h in range(PARTS)]
         for h in range(PARTS):
             nc.vector.tensor_copy(v_w[h][:].bitcast(U32), tab_w[:].bitcast(U32).indirect(part_offs[h]))
-        w2_raw.append(load_w2(1, after="warm_out"))
-        w3_w = in_slice_order("w3_w", w3_raw)
-        w3_s = in_slice_order("w3_s", w3s_raw)
-        w4_raw = [load_w4(0, after="warm_bias")]
+        w3_w = in_slice_order(at(TAB_AT, [P, PACK * H], U8, "w3_w"), w3_raw)
+        w3_s = in_slice_order(at(TAB_AT + PACK * H, [P, H], U8, "w3_s"), w3s_raw)
 
         def project(x, h, lhs, lhs_scale, on_vector=False):
             acc = next_bank(on_vector)
             nc.tensor.matmul_mx(
-                acc[:], lhsT=lhs, lhsT_scale=lhs_scale, rhs=v_w[h][:].bitcast(FP8X4), rhs_scale=v_s[h][:],
+                acc[:], lhsT=lhs, lhsT_scale=lhs_scale, rhs=v_w[h][:].bitcast(FP8X4), rhs_scale=v_s[h],
                 start=True, stop=True,
             )
             copy = nc.vector.tensor_copy if on_vector else nc.scalar.copy
@@ -190,7 +203,6 @@ def tile_list_breakaway_gap_scores_kernel(
                 gated.append([first[:]] + [rest[:, m.start - split : m.stop - split] for m in CHUNKS[1:]])
             if s == 0:
                 w2_q.append(quantise_w2(0, after=""))
-                w4_raw.append(load_w4(1, after="tab_s"))
             elif s == 1:
                 w2_q.append(quantise_w2(1, after="x3_1"))
             elif s < 2 + PASSES:

@@ -38,7 +38,6 @@ TAB_AT = W4_AT + PASSES * RAW_BYTES
 WARM_AT = 4 * S
 LAG = 3
 EARLY = 3
-LATE_ON_VECTOR = 2
 
 
 def tile_list_breakaway_gap_scores_kernel(
@@ -87,19 +86,19 @@ def tile_list_breakaway_gap_scores_kernel(
             )
             return grouped
 
-        def quantise(name, grouped):
-            words = kept([P, grouped.shape[1]], I32, name + "_words")
+        def quantise(name, grouped, after=""):
+            words = kept([P, grouped.shape[1]], I32, name + "_words", after)
             scales = kept([P, grouped.shape[1]], U8, name + "_scales")
             nc.vector.quantize_mx(words[:].bitcast(FP8X4), scales[:], grouped[:].rearrange("p c j -> p (c j)"))
             return words, scales
 
-        def quantise_w2(b, after):
-            grouped = kept([P, PASS, PACK], BF16, f"w2_grouped{b}", after)
+        def interleave_w2(b):
+            grouped = kept([P, PASS, PACK], BF16, f"w2_grouped{b}", "staged")
             nc.vector.tensor_copy(
                 grouped[:].rearrange("p (t q i) j -> p t q j i", q=BLOCKS, t=PACK),
                 w2_raw[b][:].rearrange("p j (q t i) -> p t q j i", q=BLOCKS, t=PACK),
             )
-            return quantise(f"w2_{b}", grouped)
+            return grouped
 
         taken = {True: [], False: []}
 
@@ -168,7 +167,7 @@ def tile_list_breakaway_gap_scores_kernel(
             copy = nc.vector.tensor_copy if on_vector else nc.scalar.copy
             copy(x[:, h * BANK : (h + 1) * BANK], acc[:])
 
-        x1 = [kept([P, S], F32, f"x1_{s}") for s in range(SLICES)]
+        x1 = [kept([P, S], F32, f"x1_{s}") for s in range(EARLY)]
 
         def project_x1(s, h):
             cols = slice(s * P, (s + 1) * P)
@@ -176,24 +175,26 @@ def tile_list_breakaway_gap_scores_kernel(
 
         z = kept([P, PACK, M], F32, "z")
         z_lead = kept([P, PACK, CHUNKS[0].stop], F32, "z_lead")
-        gated, x2, w2_q, w4_q, z_first = [], [], [], [], []
+        gated, x2, w2_q, w4_q, z_first, staged = [], [], [], [], [], []
 
         def columns(picks_sb, m):
             return picks_sb[:, m.start // PER_COLUMN : m.stop // PER_COLUMN]
 
         def gate(s):
             cols = slice(s * P, (s + 1) * P)
+            if s >= EARLY:
+                x1.append(kept([P, S], F32, f"x1_{s}", after=f"x3_{s - EARLY}"))
             for h in range(1 if s < EARLY else 0, PARTS):
                 project_x1(s, h)
-            lead = ring.tile([P, M], F32, name=f"lead{s}", tag="lead")
-            nc.scalar.activation(lead[:], x1[s][:].indirect(pos1_sb[:]), SIGMOID)
+            lead = kept([P, M], F32, f"lead{s}")[:]
+            nc.scalar.activation(lead, x1[s][:].indirect(pos1_sb[:]), SIGMOID)
             x3 = kept([P, S], F32, f"x3_{s}")
             for h in range(PARTS):
-                on_vector = s == 0 or (h == 0 and s >= SLICES - LATE_ON_VECTOR)
+                on_vector = s == 0 or s == 5 or (h == 0 and s in (4, 6))
                 project(x3, h, w3_w[:, PACK * s * P : PACK * (s + 1) * P].bitcast(FP8X4), w3_s[:, cols], on_vector)
             if s < SLICES - 1:
                 whole = kept([P, M], F32, f"gated{s}")
-                nc.vector.tensor_tensor(whole[:], x3[:].indirect(pos3_sb[:]), lead[:], MULT)
+                nc.vector.tensor_tensor(whole[:], x3[:].indirect(pos3_sb[:]), lead, MULT)
                 gated.append([whole[:, m] for m in CHUNKS] + [whole[:]])
             else:
                 split = CHUNKS[0].stop
@@ -201,17 +202,19 @@ def tile_list_breakaway_gap_scores_kernel(
                 for part, m in ((first, CHUNKS[0]), (rest, slice(split, M))):
                     nc.vector.tensor_tensor(part[:], x3[:].indirect(columns(pos3_sb, m)), lead[:, m], MULT)
                 gated.append([first[:]] + [rest[:, m.start - split : m.stop - split] for m in CHUNKS[1:]])
-            if s == 0:
-                w2_q.append(quantise_w2(0, after=""))
-            elif s == 1:
-                w2_q.append(quantise_w2(1, after="x3_1"))
-            elif s < 2 + PASSES:
-                w4_q.append(quantise(f"w4_{s - 2}", interleave(f"w4_grouped{s - 2}", w4_raw[s - 2][:], f"x3_{s}")))
+            if staged:
+                name, grouped, done = staged.pop()
+                done.append(quantise(name, grouped, after=f"lead{s}"))
+            if s < PASSES:
+                staged.append((f"w2_{s}", interleave_w2(s), w2_q))
+            elif s < 2 * PASSES:
+                b = s - PASSES
+                staged.append((f"w4_{b}", interleave(f"w4_grouped{b}", w4_raw[b][:], "staged"), w4_q))
 
         def chase(s):
             b, t = divmod(s, PACK)
             cols = slice(t * P, (t + 1) * P)
-            x2.append(kept([P, S], F32, f"x2_{s}", after=f"x1_{s}"))
+            x2.append(kept([P, S], F32, f"x2_{s}", after=f"x1_{s}" if s < EARLY else ""))
             for h in range(PARTS):
                 project(x2[s], h, w2_q[b][0][:, cols].bitcast(FP8X4), w2_q[b][1][:, cols])
             if b == 0:
@@ -219,7 +222,7 @@ def tile_list_breakaway_gap_scores_kernel(
             else:
                 nc.vector.tensor_tensor(z_lead[:, t, :], x2[s][:].indirect(columns(pos2_sb, CHUNKS[0])), gated[s][0], MULT)
             if s == PACK - 1:
-                z_first.extend(quantise("z_first", interleave("z_first_grouped", z[:])))
+                staged.append(("z_first", interleave("z_first_grouped", z[:], "staged"), z_first))
 
         for s in range(EARLY):
             project_x1(s, 0)
@@ -243,7 +246,7 @@ def tile_list_breakaway_gap_scores_kernel(
                 )
 
         for c, m in enumerate(CHUNKS):
-            product(c, 0, z_first[0][:, m], z_first[1][:, m])
+            product(c, 0, z_first[0][0][:, m], z_first[0][1][:, m])
 
         out_rows = out.rearrange("(j p) m -> p j m", p=P)
         holds = ("", "gated_first", "z_last_grouped0")

@@ -31,11 +31,13 @@ LINE = 4
 CHUNKS = (slice(0, 256), slice(256, 384), slice(384, 512))
 VECTOR_BANKS = 2
 RAW_BYTES = PACK * PASS * 4
-W3_AT = H + T
-W2_AT = W3_AT + PACK * H
+W2_AT = H + T
 W4_AT = W2_AT + PASSES * RAW_BYTES
 TAB_AT = W4_AT + PASSES * RAW_BYTES
-WARM_AT = 4 * S
+W3S_AT = 4 * S
+W1_AT = TAB_AT + 4 * T
+W3_AT = W1_AT + 2 * H
+LAST_QUADRANT = slice(96, P)
 LAG = 3
 EARLY = 3
 
@@ -72,9 +74,9 @@ def tile_list_breakaway_gap_scores_kernel(
                 nc.sync.dma_start(raw[:, t, :], rows[t])
             return raw
 
-        def in_slice_order(ordered, raw, rows=slice(0, P)):
-            src = raw[rows, :].bitcast(I32).rearrange("p (b q t w) -> p b q t w", b=PASSES, q=BLOCKS, t=PACK)
-            dst = ordered[rows, :].bitcast(I32).rearrange("p (b t q w) -> p b q t w", b=PASSES, q=BLOCKS, t=PACK)
+        def in_slice_order(ordered, raw):
+            src = raw.bitcast(I32).rearrange("p (b q t w) -> p b q t w", b=PASSES, q=BLOCKS, t=PACK)
+            dst = ordered.bitcast(I32).rearrange("p (b t q w) -> p b q t w", b=PASSES, q=BLOCKS, t=PACK)
             nc.vector.tensor_copy(dst, src)
             return ordered
 
@@ -115,36 +117,38 @@ def tile_list_breakaway_gap_scores_kernel(
         w1s_raw = at(0, [P, H], U8, "w1s_raw")
         tab_s = at(H, [P, T], U8, "tab_s")
         tab_w = at(TAB_AT, [P, T], I32, "tab_w")
-        picked_s = kept([P, S], U8, "picked_s")
-        w3s_raw = kept([P, H], U8, "w3s_raw")
-        w1_raw = kept([P, 2 * H], U8, "w1_raw")
-        w1_s = kept([P, H], U8, "w1_s")
-        v_s_all = kept([P, S], U8, "v_s")
+        picked_s = at(W3_AT - S // 2, [P, S], U8, "picked_s")
+        w1_raw = at(W2_AT, [P, TAB_AT - W2_AT], U8, "w1_raw")[:, 0 : 2 * H]
+        warm = kept([P, 16], F32, "warm")
+        nc.gpsimd.memset(warm[:, 0:1], 0.0)
+        rows = kept([P, S + H], U8, "rows")
+        planes_s = kept([P, S + H], U8, "planes_s")
         nc.vector.memset(tab_s[0 : P - BLOCKS, :].bitcast(I32), 0)
-        nc.gpsimd.memset(w3s_raw[:].bitcast(I32), 0)
-        nc.gpsimd.memset(w1_s[:].bitcast(I32), 0)
-        nc.gpsimd.memset(v_s_all[:].bitcast(I32), 0)
+        nc.gpsimd.memset(w1s_raw[LAST_QUADRANT.start : P - BLOCKS, :].bitcast(I32), 0)
+        nc.gpsimd.memset(planes_s[:].bitcast(I32), 0)
 
         nc.sync.dma_start(offs_sb[:], offs)
         nc.sync.dma_start(tab_s[P - BLOCKS : P, :].bitcast(I32), tab_scales[0].bitcast(I32))
-        nc.sync.dma_start(w1_raw[:].bitcast(I32), w1_words[0].bitcast(I32))
-        load_scale_rows(w1s_raw, w1_scales, nc.sync)
-        nc.sync.dma_start(tab_w[:], tab_words[0].rearrange("p t i -> p (t i)").bitcast(I32))
+        nc.sync.dma_start(w1s_raw[P - BLOCKS : P, :].bitcast(I32), w1_scales[0].bitcast(I32))
+        nc.sync.dma_start(w1_raw.bitcast(I32), w1_words[0].bitcast(I32))
         for picks_sb, picks in ((pos1_sb, pos1), (pos3_sb, pos3), (pos2_sb, pos2)):
             nc.sync.dma_start(picks_sb[:], picks)
+        nc.sync.dma_start(tab_w[:], tab_words[0].rearrange("p t i -> p (t i)").bitcast(I32))
+
+        nc.scalar.activation(warm[:, 8:9], warm[:, 0:1], SIGMOID)
 
         part_offs = [offs_sb[:, h * BANK // PER_COLUMN : (h + 1) * BANK // PER_COLUMN] for h in range(PARTS)]
         nc.vector.tensor_copy(picked_s[:, 0:S], tab_s[:].indirect(offs_sb[:]))
+        in_slice_order(rows[LAST_QUADRANT, S:], w1s_raw[LAST_QUADRANT, :])
+        nc.vector.tensor_copy(rows[LAST_QUADRANT, 0:S].bitcast(I32), picked_s[LAST_QUADRANT, :].bitcast(I32))
         for r in range(4):
-            nc.scalar.dma_start(v_s_all[r:P:32, :].bitcast(I32), picked_s[P - BLOCKS + r : P : 4, 0:S].bitcast(I32))
+            nc.scalar.dma_start(planes_s[r:P:32, :].bitcast(I32), rows[P - BLOCKS + r : P : 4, :].bitcast(I32))
 
-        warm = at(WARM_AT, [P, (TAB_AT - WARM_AT) // 4], F32, "warm")
-        nc.vector.memset(warm[:, 0:1], 0.0)
-        nc.scalar.activation(warm[:, 8:9], warm[:, 0:1], SIGMOID, scale=w3s_raw[:, 0:4].bitcast(F32))
-        v_s = [v_s_all[:, h * BANK : (h + 1) * BANK] for h in range(PARTS)]
-        w1_w = in_slice_order(kept([P, 2 * H], U8, "w1_w"), w1_raw)
-        for quadrant in range(0, P, 32):
-            in_slice_order(w1_s, w1s_raw, slice(quadrant, quadrant + 4))
+        w3s_raw = at(W3S_AT, [P, H], U8, "w3s_raw")
+        nc.vector.memset(w3s_raw[:].bitcast(I32), 0)
+        v_s = [planes_s[:, h * BANK : (h + 1) * BANK] for h in range(PARTS)]
+        w1_s = planes_s[:, S:]
+        w1_w = in_slice_order(at(W1_AT, [P, 2 * H], U8, "w1_w")[:], w1_raw)
 
         w3_raw = at(W3_AT, [P, PACK * H], U8, "w3_raw")
         nc.sync.dma_start(w3_raw[:].bitcast(I32), w3_words[0].rearrange("p c i -> p (c i)").bitcast(I32))
@@ -155,8 +159,8 @@ def tile_list_breakaway_gap_scores_kernel(
         v_w = [at(h * 4 * BANK, [P, BANK], I32, f"v_w{h}") for h in range(PARTS)]
         for h in range(PARTS):
             nc.vector.tensor_copy(v_w[h][:].bitcast(U32), tab_w[:].bitcast(U32).indirect(part_offs[h]))
-        w3_w = in_slice_order(at(TAB_AT, [P, PACK * H], U8, "w3_w"), w3_raw)
-        w3_s = in_slice_order(at(TAB_AT + PACK * H, [P, H], U8, "w3_s"), w3s_raw)
+        w3_w = in_slice_order(at(TAB_AT, [P, PACK * H], U8, "w3_w")[:], w3_raw[:])
+        w3_s = in_slice_order(at(TAB_AT + PACK * H, [P, H], U8, "w3_s")[:], w3s_raw[:])
 
         def project(x, h, lhs, lhs_scale, on_vector=False):
             acc = next_bank(on_vector)

@@ -31,12 +31,12 @@ LINE = 4
 CHUNKS = (slice(0, 256), slice(256, 384), slice(384, 512))
 VECTOR_BANKS = 2
 RAW_BYTES = PACK * PASS * 4
-W2_AT = H + T
+W3_AT = H + T
+W2_AT = W3_AT + PACK * H
 W4_AT = W2_AT + PASSES * RAW_BYTES
 TAB_AT = W4_AT + PASSES * RAW_BYTES
 W3S_AT = 4 * S
-W1_AT = TAB_AT + 4 * T
-W3_AT = W1_AT + 2 * H
+W1_AT = 4 * BANK
 LAST_QUADRANT = slice(96, P)
 LAG = 3
 EARLY = 3
@@ -117,15 +117,16 @@ def tile_list_breakaway_gap_scores_kernel(
         w1s_raw = at(0, [P, H], U8, "w1s_raw")
         tab_s = at(H, [P, T], U8, "tab_s")
         tab_w = at(TAB_AT, [P, T], I32, "tab_w")
-        picked_s = at(W3_AT - S // 2, [P, S], U8, "picked_s")
-        w1_raw = at(W2_AT, [P, TAB_AT - W2_AT], U8, "w1_raw")[:, 0 : 2 * H]
+        w1_raw = at(W3_AT, [P, TAB_AT - W3_AT], U8, "w1_raw")[:, 0 : 2 * H]
         warm = kept([P, 16], F32, "warm")
         nc.gpsimd.memset(warm[:, 0:1], 0.0)
-        rows = kept([P, S + H], U8, "rows")
-        planes_s = kept([P, S + H], U8, "planes_s")
+        rows = kept([P, BANK + H], U8, "rows")
+        first_s = kept([P, BANK + H], U8, "first_s")
+        second_s = kept([P, BANK], U8, "second_s")
         nc.vector.memset(tab_s[0 : P - BLOCKS, :].bitcast(I32), 0)
         nc.gpsimd.memset(w1s_raw[LAST_QUADRANT.start : P - BLOCKS, :].bitcast(I32), 0)
-        nc.gpsimd.memset(planes_s[:].bitcast(I32), 0)
+        nc.gpsimd.memset(first_s[:].bitcast(I32), 0)
+        nc.gpsimd.memset(second_s[:].bitcast(I32), 0)
 
         nc.sync.dma_start(offs_sb[:], offs)
         nc.sync.dma_start(tab_s[P - BLOCKS : P, :].bitcast(I32), tab_scales[0].bitcast(I32))
@@ -138,17 +139,20 @@ def tile_list_breakaway_gap_scores_kernel(
         nc.scalar.activation(warm[:, 8:9], warm[:, 0:1], SIGMOID)
 
         part_offs = [offs_sb[:, h * BANK // PER_COLUMN : (h + 1) * BANK // PER_COLUMN] for h in range(PARTS)]
-        nc.vector.tensor_copy(picked_s[:, 0:S], tab_s[:].indirect(offs_sb[:]))
-        in_slice_order(rows[LAST_QUADRANT, S:], w1s_raw[LAST_QUADRANT, :])
-        nc.vector.tensor_copy(rows[LAST_QUADRANT, 0:S].bitcast(I32), picked_s[LAST_QUADRANT, :].bitcast(I32))
-        for r in range(4):
-            nc.scalar.dma_start(planes_s[r:P:32, :].bitcast(I32), rows[P - BLOCKS + r : P : 4, :].bitcast(I32))
-
+        picked_s = [kept([P, BANK], U8, "picked_s0")]
+        in_slice_order(rows[LAST_QUADRANT, BANK:], w1s_raw[LAST_QUADRANT, :])
+        nc.vector.tensor_copy(picked_s[0][:], tab_s[:].indirect(part_offs[0]))
+        nc.vector.tensor_copy(rows[LAST_QUADRANT, 0:BANK].bitcast(I32), picked_s[0][LAST_QUADRANT, :].bitcast(I32))
+        picked_s.append(kept([P, BANK], U8, "picked_s1", after="picked_s0"))
+        nc.vector.tensor_copy(picked_s[1][:], tab_s[:].indirect(part_offs[1]))
+        for plane, source in ((first_s, rows), (second_s, picked_s[1])):
+            for r in range(4):
+                nc.scalar.dma_start(plane[r:P:32, :].bitcast(I32), source[P - BLOCKS + r : P : 4, :].bitcast(I32))
+        v_s = [first_s[:, 0:BANK], second_s[:]]
+        w1_s = first_s[:, BANK:]
+        w1_w = in_slice_order(at(W1_AT, [P, 2 * H], U8, "w1_w")[:], w1_raw)
         w3s_raw = at(W3S_AT, [P, H], U8, "w3s_raw")
         nc.vector.memset(w3s_raw[:].bitcast(I32), 0)
-        v_s = [planes_s[:, h * BANK : (h + 1) * BANK] for h in range(PARTS)]
-        w1_s = planes_s[:, S:]
-        w1_w = in_slice_order(at(W1_AT, [P, 2 * H], U8, "w1_w")[:], w1_raw)
 
         w3_raw = at(W3_AT, [P, PACK * H], U8, "w3_raw")
         nc.sync.dma_start(w3_raw[:].bitcast(I32), w3_words[0].rearrange("p c i -> p (c i)").bitcast(I32))
@@ -156,7 +160,7 @@ def tile_list_breakaway_gap_scores_kernel(
         w2_raw = [load_w2(b) for b in range(PASSES)]
         w4_raw = [load_w4(b) for b in range(PASSES)]
 
-        v_w = [at(h * 4 * BANK, [P, BANK], I32, f"v_w{h}") for h in range(PARTS)]
+        v_w = [at(0, [P, BANK], I32, "v_w0"), kept([P, BANK], I32, "v_w1")]
         for h in range(PARTS):
             nc.vector.tensor_copy(v_w[h][:].bitcast(U32), tab_w[:].bitcast(U32).indirect(part_offs[h]))
         w3_w = in_slice_order(at(TAB_AT, [P, PACK * H], U8, "w3_w")[:], w3_raw[:])

@@ -48,7 +48,6 @@ def tile_list_breakaway_gap_scores_kernel(
     nc = tc.nc
     with ExitStack() as ctx:
         keep = ctx.enter_context(tc.tile_pool(name="keep", bufs=1))
-        ring = ctx.enter_context(tc.tile_pool(name="ring", bufs=4))
         placed = ctx.enter_context(tc.tile_pool(name="placed", bufs=1))
         psum = ctx.enter_context(tc.psum_pool(name="psum", bufs=1))
 
@@ -127,6 +126,9 @@ def tile_list_breakaway_gap_scores_kernel(
         nc.gpsimd.memset(w1s_raw[LAST_QUADRANT.start : P - BLOCKS, :].bitcast(I32), 0)
         nc.gpsimd.memset(first_s[:].bitcast(I32), 0)
         nc.gpsimd.memset(second_s[:].bitcast(I32), 0)
+        w3s_raw = kept([P, H], U8, "w3s_raw")
+        nc.gpsimd.memset(w3s_raw[:].bitcast(I32), 0)
+        load_scale_rows(w3s_raw, w3_scales, nc.gpsimd)
 
         nc.sync.dma_start(offs_sb[:], offs)
         nc.sync.dma_start(tab_s[P - BLOCKS : P, :].bitcast(I32), tab_scales[0].bitcast(I32))
@@ -151,12 +153,9 @@ def tile_list_breakaway_gap_scores_kernel(
         v_s = [first_s[:, 0:BANK], second_s[:]]
         w1_s = first_s[:, BANK:]
         w1_w = in_slice_order(at(W1_AT, [P, 2 * H], U8, "w1_w")[:], w1_raw)
-        w3s_raw = at(W3S_AT, [P, H], U8, "w3s_raw")
-        nc.vector.memset(w3s_raw[:].bitcast(I32), 0)
 
         w3_raw = at(W3_AT, [P, PACK * H], U8, "w3_raw")
         nc.sync.dma_start(w3_raw[:].bitcast(I32), w3_words[0].rearrange("p c i -> p (c i)").bitcast(I32))
-        load_scale_rows(w3s_raw, w3_scales, nc.sync)
         w2_raw = [load_w2(b) for b in range(PASSES)]
         w4_raw = [load_w4(b) for b in range(PASSES)]
 

@@ -197,7 +197,7 @@ def tile_list_breakaway_gap_scores_kernel(
             nc.scalar.activation(lead, x1[s][:].indirect(pos1_sb[:]), SIGMOID)
             x3 = kept([P, S], F32, f"x3_{s}")
             for h in range(PARTS):
-                on_vector = s == 0 or s == 5 or (h == 0 and s in (4, 6))
+                on_vector = s == 0 or s == 5 or (h == 0 and s == 4)
                 project(x3, h, w3_w[:, PACK * s * P : PACK * (s + 1) * P].bitcast(FP8X4), w3_s[:, cols], on_vector)
             if s < SLICES - 1:
                 whole = kept([P, M], F32, f"gated{s}")

@@ -35,8 +35,7 @@ W3_AT = H + T
 W2_AT = W3_AT + PACK * H
 W4_AT = W2_AT + PASSES * RAW_BYTES
 TAB_AT = W4_AT + PASSES * RAW_BYTES
-W3S_AT = 4 * S
-W1_AT = 4 * BANK
+W1_AT = TAB_AT + 4 * T
 LAST_QUADRANT = slice(96, P)
 LAG = 3
 EARLY = 3
@@ -116,16 +115,15 @@ def tile_list_breakaway_gap_scores_kernel(
         w1s_raw = at(0, [P, H], U8, "w1s_raw")
         tab_s = at(H, [P, T], U8, "tab_s")
         tab_w = at(TAB_AT, [P, T], I32, "tab_w")
-        w1_raw = at(W3_AT, [P, TAB_AT - W3_AT], U8, "w1_raw")[:, 0 : 2 * H]
+        w1_raw = at(W1_AT, [P, 2 * H], U8, "w1_raw")[:]
+        w3_raw = at(W3_AT, [P, PACK * H], U8, "w3_raw")
         warm = kept([P, 16], F32, "warm")
         nc.gpsimd.memset(warm[:, 0:1], 0.0)
-        rows = kept([P, BANK + H], U8, "rows")
-        first_s = kept([P, BANK + H], U8, "first_s")
-        second_s = kept([P, BANK], U8, "second_s")
+        rows = at(W2_AT, [P, TAB_AT - W2_AT], U8, "rows")[:, 0 : S + H]
+        first_s = kept([P, S + H], U8, "first_s")
         nc.vector.memset(tab_s[0 : P - BLOCKS, :].bitcast(I32), 0)
         nc.gpsimd.memset(w1s_raw[LAST_QUADRANT.start : P - BLOCKS, :].bitcast(I32), 0)
         nc.gpsimd.memset(first_s[:].bitcast(I32), 0)
-        nc.gpsimd.memset(second_s[:].bitcast(I32), 0)
         w3s_raw = kept([P, H], U8, "w3s_raw")
         nc.gpsimd.memset(w3s_raw[:].bitcast(I32), 0)
         load_scale_rows(w3s_raw, w3_scales, nc.gpsimd)
@@ -133,35 +131,33 @@ def tile_list_breakaway_gap_scores_kernel(
         nc.sync.dma_start(offs_sb[:], offs)
         nc.sync.dma_start(tab_s[P - BLOCKS : P, :].bitcast(I32), tab_scales[0].bitcast(I32))
         nc.sync.dma_start(w1s_raw[P - BLOCKS : P, :].bitcast(I32), w1_scales[0].bitcast(I32))
-        nc.sync.dma_start(w1_raw.bitcast(I32), w1_words[0].bitcast(I32))
-        for picks_sb, picks in ((pos1_sb, pos1), (pos3_sb, pos3), (pos2_sb, pos2)):
-            nc.sync.dma_start(picks_sb[:], picks)
+        nc.sync.dma_start(pos1_sb[:], pos1)
+        nc.sync.dma_start(pos3_sb[:], pos3)
         nc.sync.dma_start(tab_w[:], tab_words[0].rearrange("p t i -> p (t i)").bitcast(I32))
+        nc.sync.dma_start(pos2_sb[:], pos2)
+        nc.sync.dma_start(w1_raw.bitcast(I32), w1_words[0].bitcast(I32))
+        nc.sync.dma_start(w3_raw[:].bitcast(I32), w3_words[0].rearrange("p c i -> p (c i)").bitcast(I32))
 
         nc.scalar.activation(warm[:, 8:9], warm[:, 0:1], SIGMOID)
 
         part_offs = [offs_sb[:, h * BANK // PER_COLUMN : (h + 1) * BANK // PER_COLUMN] for h in range(PARTS)]
-        picked_s = [kept([P, BANK], U8, "picked_s0")]
-        in_slice_order(rows[LAST_QUADRANT, BANK:], w1s_raw[LAST_QUADRANT, :])
-        nc.vector.tensor_copy(picked_s[0][:], tab_s[:].indirect(part_offs[0]))
-        nc.vector.tensor_copy(rows[LAST_QUADRANT, 0:BANK].bitcast(I32), picked_s[0][LAST_QUADRANT, :].bitcast(I32))
-        picked_s.append(kept([P, BANK], U8, "picked_s1", after="picked_s0"))
-        nc.vector.tensor_copy(picked_s[1][:], tab_s[:].indirect(part_offs[1]))
-        for plane, source in ((first_s, rows), (second_s, picked_s[1])):
-            for r in range(4):
-                nc.scalar.dma_start(plane[r:P:32, :].bitcast(I32), source[P - BLOCKS + r : P : 4, :].bitcast(I32))
-        v_s = [first_s[:, 0:BANK], second_s[:]]
-        w1_s = first_s[:, BANK:]
-        w1_w = in_slice_order(at(W1_AT, [P, 2 * H], U8, "w1_w")[:], w1_raw)
+        picked_s = kept([P, S], U8, "picked_s")
+        in_slice_order(rows[LAST_QUADRANT, S:], w1s_raw[LAST_QUADRANT, :])
+        nc.vector.tensor_copy(picked_s[:], tab_s[:].indirect(offs_sb[:]))
+        nc.vector.tensor_copy(rows[LAST_QUADRANT, 0:S].bitcast(I32), picked_s[LAST_QUADRANT, :].bitcast(I32))
+        for r in range(4):
+            nc.scalar.dma_start(first_s[r:P:32, :].bitcast(I32), rows[P - BLOCKS + r : P : 4, :].bitcast(I32))
+        v_s = [first_s[:, h * BANK : (h + 1) * BANK] for h in range(PARTS)]
+        w1_s = first_s[:, S:]
 
-        w3_raw = at(W3_AT, [P, PACK * H], U8, "w3_raw")
-        nc.sync.dma_start(w3_raw[:].bitcast(I32), w3_words[0].rearrange("p c i -> p (c i)").bitcast(I32))
         w2_raw = [load_w2(b) for b in range(PASSES)]
         w4_raw = [load_w4(b) for b in range(PASSES)]
 
-        v_w = [at(0, [P, BANK], I32, "v_w0"), kept([P, BANK], I32, "v_w1")]
-        for h in range(PARTS):
-            nc.vector.tensor_copy(v_w[h][:].bitcast(U32), tab_w[:].bitcast(U32).indirect(part_offs[h]))
+        v_w = [at(0, [P, BANK], I32, "v_w0")]
+        nc.vector.tensor_copy(v_w[0][:].bitcast(U32), tab_w[:].bitcast(U32).indirect(part_offs[0]))
+        w1_w = in_slice_order(kept([P, 2 * H], U8, "w1_w")[:], w1_raw)
+        v_w.append(at(W1_AT, [P, BANK], I32, "v_w1"))
+        nc.vector.tensor_copy(v_w[1][:].bitcast(U32), tab_w[:].bitcast(U32).indirect(part_offs[1]))
         w3_w = in_slice_order(at(TAB_AT, [P, PACK * H], U8, "w3_w")[:], w3_raw[:])
         w3_s = in_slice_order(at(TAB_AT + PACK * H, [P, H], U8, "w3_s")[:], w3s_raw[:])
 

@@ -29,14 +29,15 @@ PARTS = S // BANK
 PER_COLUMN = 16
 LINE = 4
 CHUNKS = (slice(0, 256), slice(256, 384), slice(384, 512))
-VECTOR_BANKS = 2
+VECTOR_BANKS = 3
 RAW_BYTES = PACK * PASS * 4
-W3_AT = H + T
+W3_AT = 2 * H + T
 W2_AT = W3_AT + PACK * H
 W4_AT = W2_AT + PASSES * RAW_BYTES
 TAB_AT = W4_AT + PASSES * RAW_BYTES
 W1_AT = TAB_AT + 4 * T
 LAST_QUADRANT = slice(96, P)
+WARM_PASSES = 3
 LAG = 3
 EARLY = 3
 
@@ -56,10 +57,6 @@ def tile_list_breakaway_gap_scores_kernel(
         def at(offset, shape, dtype, name):
             return placed.tile(shape, dtype, name=name, offset=offset, align_bytes=64)
 
-        def load_scale_rows(plane, scales, queue):
-            for r in range(4):
-                queue.dma_start(plane[r:P:32, :].bitcast(I32), scales[0, r:BLOCKS:4, :].bitcast(I32))
-
         def load_w2(b):
             raw = at(W2_AT + b * RAW_BYTES, [P, PACK, PASS], F32, f"w2_raw{b}")
             nc.sync.dma_start(raw[:], w2[:, b * PASS : (b + 1) * PASS].rearrange("(p j) c -> p j c", j=PACK))
@@ -72,10 +69,10 @@ def tile_list_breakaway_gap_scores_kernel(
                 nc.sync.dma_start(raw[:, t, :], rows[t])
             return raw
 
-        def in_slice_order(ordered, raw):
-            src = raw.bitcast(I32).rearrange("p (b q t w) -> p b q t w", b=PASSES, q=BLOCKS, t=PACK)
-            dst = ordered.bitcast(I32).rearrange("p (b t q w) -> p b q t w", b=PASSES, q=BLOCKS, t=PACK)
-            nc.vector.tensor_copy(dst, src)
+        def in_slice_order(ordered, raw, passes=PASSES, copy=nc.vector.tensor_copy):
+            src = raw.bitcast(I32).rearrange("p (b q t w) -> p b t q w", b=passes, q=BLOCKS, t=PACK)
+            dst = ordered.bitcast(I32).rearrange("p (b t q w) -> p b t q w", b=passes, q=BLOCKS, t=PACK)
+            copy(dst, src)
             return ordered
 
         def interleave(name, planes, after="", copy=nc.vector.tensor_copy):
@@ -112,25 +109,23 @@ def tile_list_breakaway_gap_scores_kernel(
         pos1_sb = keep.tile([P, M // PER_COLUMN], U16, name="pos1_sb")
         pos2_sb = keep.tile([P, M // PER_COLUMN], U16, name="pos2_sb")
         pos3_sb = keep.tile([P, M // PER_COLUMN], U16, name="pos3_sb")
-        w1s_raw = at(0, [P, H], U8, "w1s_raw")
-        tab_s = at(H, [P, T], U8, "tab_s")
+        ws_raw = at(0, [P, 2 * H], U8, "ws_raw")
+        tab_s = at(2 * H, [P, T], U8, "tab_s")
         tab_w = at(TAB_AT, [P, T], I32, "tab_w")
         w1_raw = at(W1_AT, [P, 2 * H], U8, "w1_raw")[:]
         w3_raw = at(W3_AT, [P, PACK * H], U8, "w3_raw")
         warm = kept([P, 16], F32, "warm")
         nc.gpsimd.memset(warm[:, 0:1], 0.0)
-        rows = at(W2_AT, [P, TAB_AT - W2_AT], U8, "rows")[:, 0 : S + H]
-        first_s = kept([P, S + H], U8, "first_s")
+        rows = at(W2_AT, [P, TAB_AT - W2_AT], U8, "rows")[:, 0 : S + 2 * H]
+        first_s = kept([P, S + 2 * H], U8, "first_s")
         nc.vector.memset(tab_s[0 : P - BLOCKS, :].bitcast(I32), 0)
-        nc.gpsimd.memset(w1s_raw[LAST_QUADRANT.start : P - BLOCKS, :].bitcast(I32), 0)
+        nc.gpsimd.memset(ws_raw[LAST_QUADRANT.start : P - BLOCKS, :].bitcast(I32), 0)
         nc.gpsimd.memset(first_s[:].bitcast(I32), 0)
-        w3s_raw = kept([P, H], U8, "w3s_raw")
-        nc.gpsimd.memset(w3s_raw[:].bitcast(I32), 0)
-        load_scale_rows(w3s_raw, w3_scales, nc.gpsimd)
 
         nc.sync.dma_start(offs_sb[:], offs)
         nc.sync.dma_start(tab_s[P - BLOCKS : P, :].bitcast(I32), tab_scales[0].bitcast(I32))
-        nc.sync.dma_start(w1s_raw[P - BLOCKS : P, :].bitcast(I32), w1_scales[0].bitcast(I32))
+        nc.sync.dma_start(ws_raw[P - BLOCKS : P, 0:H].bitcast(I32), w1_scales[0].bitcast(I32))
+        nc.sync.dma_start(ws_raw[P - BLOCKS : P, H:].bitcast(I32), w3_scales[0].bitcast(I32))
         nc.sync.dma_start(pos1_sb[:], pos1)
         nc.sync.dma_start(pos3_sb[:], pos3)
         nc.sync.dma_start(tab_w[:], tab_words[0].rearrange("p t i -> p (t i)").bitcast(I32))
@@ -142,24 +137,31 @@ def tile_list_breakaway_gap_scores_kernel(
 
         part_offs = [offs_sb[:, h * BANK // PER_COLUMN : (h + 1) * BANK // PER_COLUMN] for h in range(PARTS)]
         picked_s = kept([P, S], U8, "picked_s")
-        in_slice_order(rows[LAST_QUADRANT, S:], w1s_raw[LAST_QUADRANT, :])
+        in_slice_order(rows[LAST_QUADRANT, S:], ws_raw[LAST_QUADRANT, :], 2 * PASSES)
         nc.vector.tensor_copy(picked_s[:], tab_s[:].indirect(offs_sb[:]))
         nc.vector.tensor_copy(rows[LAST_QUADRANT, 0:S].bitcast(I32), picked_s[LAST_QUADRANT, :].bitcast(I32))
         for r in range(4):
             nc.scalar.dma_start(first_s[r:P:32, :].bitcast(I32), rows[P - BLOCKS + r : P : 4, :].bitcast(I32))
         v_s = [first_s[:, h * BANK : (h + 1) * BANK] for h in range(PARTS)]
-        w1_s = first_s[:, S:]
+        w1_s, w3_s = first_s[:, S : S + H], first_s[:, S + H :]
 
         w2_raw = [load_w2(b) for b in range(PASSES)]
         w4_raw = [load_w4(b) for b in range(PASSES)]
 
+        idle_bank = psum.tile([P, BANK], F32, name="idle_bank", tag=f"bank{BANKS - 1}")
+        for k in range(WARM_PASSES):
+            nc.tensor.matmul_mx(
+                idle_bank[:], lhsT=tab_w[:, 0:P].bitcast(FP8X4), lhsT_scale=tab_s[:, 0:P],
+                rhs=tab_w[:, 0:BANK].bitcast(FP8X4), rhs_scale=tab_s[:, 0:BANK], start=True, stop=True,
+            )
+
         v_w = [at(0, [P, BANK], I32, "v_w0")]
         nc.vector.tensor_copy(v_w[0][:].bitcast(U32), tab_w[:].bitcast(U32).indirect(part_offs[0]))
-        w1_w = in_slice_order(kept([P, 2 * H], U8, "w1_w")[:], w1_raw)
-        v_w.append(at(W1_AT, [P, BANK], I32, "v_w1"))
+        w1_w = in_slice_order(kept([P, 2 * H], U8, "w1_w")[:], w1_raw, copy=nc.gpsimd.tensor_copy)
+        v_w.append(kept([P, BANK], I32, "v_w1"))
         nc.vector.tensor_copy(v_w[1][:].bitcast(U32), tab_w[:].bitcast(U32).indirect(part_offs[1]))
-        w3_w = in_slice_order(at(TAB_AT, [P, PACK * H], U8, "w3_w")[:], w3_raw[:])
-        w3_s = in_slice_order(at(TAB_AT + PACK * H, [P, H], U8, "w3_s")[:], w3s_raw[:])
+        w3_w = in_slice_order(kept([P, PACK * H], U8, "w3_w")[:], w3_raw[:], copy=nc.gpsimd.tensor_copy)
+
 
         def project(x, h, lhs, lhs_scale, on_vector=False):
             acc = next_bank(on_vector)
@@ -174,7 +176,7 @@ def tile_list_breakaway_gap_scores_kernel(
 
         def project_x1(s, h):
             cols = slice(s * P, (s + 1) * P)
-            project(x1[s], h, w1_w[:, 2 * s * P : 2 * (s + 1) * P].bitcast(FP4X4), w1_s[:, cols], s == 1)
+            project(x1[s], h, w1_w[:, 2 * s * P : 2 * (s + 1) * P].bitcast(FP4X4), w1_s[:, cols], s == 1 or (s == 2 and h == 0))
 
         z = kept([P, PACK, M], F32, "z")
         z_lead = kept([P, PACK, CHUNKS[0].stop], F32, "z_lead")
@@ -189,11 +191,11 @@ def tile_list_breakaway_gap_scores_kernel(
                 x1.append(kept([P, S], F32, f"x1_{s}", after=f"x3_{s - EARLY}"))
             for h in range(1 if s < EARLY else 0, PARTS):
                 project_x1(s, h)
-            lead = kept([P, M], F32, f"lead{s}")[:]
+            lead = kept([P, M], F32, f"lead{s}", after="staged" if s == 0 else "")[:]
             nc.scalar.activation(lead, x1[s][:].indirect(pos1_sb[:]), SIGMOID)
             x3 = kept([P, S], F32, f"x3_{s}")
             for h in range(PARTS):
-                on_vector = s == 0 or s == 5 or (h == 0 and s == 4)
+                on_vector = s in (0, 4, 5)
                 project(x3, h, w3_w[:, PACK * s * P : PACK * (s + 1) * P].bitcast(FP8X4), w3_s[:, cols], on_vector)
             if s < SLICES - 1:
                 whole = kept([P, M], F32, f"gated{s}")
@@ -217,7 +219,7 @@ def tile_list_breakaway_gap_scores_kernel(
         def chase(s):
             b, t = divmod(s, PACK)
             cols = slice(t * P, (t + 1) * P)
-            x2.append(kept([P, S], F32, f"x2_{s}", after=f"x1_{s}" if s < EARLY else ""))
+            x2.append(kept([P, S], F32, f"x2_{s}", after=f"x1_{s}" if s in (0, 2) else ""))
             for h in range(PARTS):
                 project(x2[s], h, w2_q[b][0][:, cols].bitcast(FP8X4), w2_q[b][1][:, cols])
             if b == 0:

@@ -29,7 +29,7 @@ PARTS = S // BANK
 PER_COLUMN = 16
 LINE = 4
 CHUNKS = (slice(0, 256), slice(256, 384), slice(384, 512))
-VECTOR_BANKS = 3
+VECTOR_BANKS = 5
 RAW_BYTES = PACK * PASS * 4
 W3_AT = 2 * H + T
 W2_AT = W3_AT + PACK * H
@@ -38,6 +38,7 @@ TAB_AT = W4_AT + PASSES * RAW_BYTES
 W1_AT = TAB_AT + 4 * T
 LAST_QUADRANT = slice(96, P)
 WARM_PASSES = 3
+AHEAD = 5
 LAG = 3
 EARLY = 3
 
@@ -91,6 +92,12 @@ def tile_list_breakaway_gap_scores_kernel(
 
         def interleave_w2(b):
             grouped = kept([P, PASS, PACK], BF16, f"w2_grouped{b}", "staged")
+            if b == 0:
+                nc.gpsimd.tensor_copy(
+                    grouped[:].rearrange("p (t q i) j -> p t q i j", q=BLOCKS, t=PACK),
+                    w2_raw[b][:].rearrange("p j (q t i) -> p t q i j", q=BLOCKS, t=PACK),
+                )
+                return grouped
             nc.vector.tensor_copy(
                 grouped[:].rearrange("p (t q i) j -> p t q j i", q=BLOCKS, t=PACK),
                 w2_raw[b][:].rearrange("p j (q t i) -> p t q j i", q=BLOCKS, t=PACK),
@@ -101,7 +108,7 @@ def tile_list_breakaway_gap_scores_kernel(
 
         def next_bank(on_vector):
             mine = taken[on_vector]
-            bank = len(mine) % VECTOR_BANKS if on_vector else VECTOR_BANKS + len(mine) % (BANKS - VECTOR_BANKS)
+            bank = len(mine) % VECTOR_BANKS if on_vector else (VECTOR_BANKS + len(mine)) % BANKS
             mine.append(psum.tile([P, BANK], F32, name=f"acc{bank}_{len(mine)}", tag=f"bank{bank}"))
             return mine[-1]
 
@@ -180,25 +187,29 @@ def tile_list_breakaway_gap_scores_kernel(
 
         z = kept([P, PACK, M], F32, "z")
         z_lead = kept([P, PACK, CHUNKS[0].stop], F32, "z_lead")
-        gated, x2, w2_q, w4_q, z_first, staged = [], [], [], [], [], []
+        gated, x2, w2_q, w4_q, z_first, staged, fronts = [], [], [], [], [], [], []
 
         def columns(picks_sb, m):
             return picks_sb[:, m.start // PER_COLUMN : m.stop // PER_COLUMN]
 
-        def gate(s):
+        def front(s):
             cols = slice(s * P, (s + 1) * P)
             if s >= EARLY:
-                x1.append(kept([P, S], F32, f"x1_{s}", after=f"x3_{s - EARLY}"))
+                x1.append(kept([P, S], F32, f"x1_{s}", after=f"x3_{s - AHEAD}" if s >= AHEAD else ""))
             for h in range(1 if s < EARLY else 0, PARTS):
                 project_x1(s, h)
-            lead = kept([P, M], F32, f"lead{s}", after="staged" if s == 0 else "")[:]
+            lead = kept([P, M], F32, f"lead{s}")[:]
             nc.scalar.activation(lead, x1[s][:].indirect(pos1_sb[:]), SIGMOID)
             x3 = kept([P, S], F32, f"x3_{s}")
             for h in range(PARTS):
-                on_vector = s in (0, 4, 5)
+                on_vector = s < EARLY or (s == EARLY and h == 0)
                 project(x3, h, w3_w[:, PACK * s * P : PACK * (s + 1) * P].bitcast(FP8X4), w3_s[:, cols], on_vector)
+            fronts.append((x3, lead))
+
+        def gate(s):
+            x3, lead = fronts[s]
             if s < SLICES - 1:
-                whole = kept([P, M], F32, f"gated{s}")
+                whole = at(W2_AT + 4 * M * s, [P, M], F32, f"gated{s}") if s <= EARLY else kept([P, M], F32, f"gated{s}")
                 nc.vector.tensor_tensor(whole[:], x3[:].indirect(pos3_sb[:]), lead, MULT)
                 gated.append([whole[:, m] for m in CHUNKS] + [whole[:]])
             else:
@@ -210,10 +221,10 @@ def tile_list_breakaway_gap_scores_kernel(
             if staged:
                 name, grouped, done = staged.pop()
                 done.append(quantise(name, grouped, after=f"lead{s}"))
-            if s < PASSES:
-                staged.append((f"w2_{s}", interleave_w2(s), w2_q))
-            elif s < 2 * PASSES:
-                b = s - PASSES
+            if s == 0:
+                staged.append(("w2_1", interleave_w2(1), w2_q))
+            elif s <= PASSES:
+                b = s - 1
                 staged.append((f"w4_{b}", interleave(f"w4_grouped{b}", w4_raw[b][:], "staged"), w4_q))
 
         def chase(s):
@@ -231,7 +242,13 @@ def tile_list_breakaway_gap_scores_kernel(
 
         for s in range(EARLY):
             project_x1(s, 0)
+        w2_first = interleave_w2(0)
+        for s in range(EARLY + 1):
+            front(s)
+        w2_q.append(quantise("w2_0", w2_first))
         for s in range(SLICES + LAG):
+            if EARLY < s < SLICES:
+                front(s)
             if s < SLICES:
                 gate(s)
             if s >= LAG:

@@ -33,14 +33,14 @@ VECTOR_BANKS = 5
 RAW_BYTES = PACK * PASS * 4
 W3_AT = 2 * H + T
 W2_AT = W3_AT + PACK * H
-W4_AT = W2_AT + PASSES * RAW_BYTES
+W4_AT = W2_AT + PASSES * RAW_BYTES + RAW_BYTES // 2
 TAB_AT = W4_AT + PASSES * RAW_BYTES
 W1_AT = TAB_AT + 4 * T
 LAST_QUADRANT = slice(96, P)
 WARM_PASSES = 3
 AHEAD = 5
 LAG = 3
-EARLY = 3
+EARLY = 5
 
 
 def tile_list_breakaway_gap_scores_kernel(
@@ -58,9 +58,9 @@ def tile_list_breakaway_gap_scores_kernel(
         def at(offset, shape, dtype, name):
             return placed.tile(shape, dtype, name=name, offset=offset, align_bytes=64)
 
-        def load_w2(b):
-            raw = at(W2_AT + b * RAW_BYTES, [P, PACK, PASS], F32, f"w2_raw{b}")
-            nc.sync.dma_start(raw[:], w2[:, b * PASS : (b + 1) * PASS].rearrange("(p j) c -> p j c", j=PACK))
+        def load_w2(first, width, offset, planes=PACK):
+            raw = at(W2_AT + offset, [P, planes, width], F32, f"w2_raw{first}")[:, 0:PACK, :]
+            nc.sync.dma_start(raw, w2[:, first : first + width].rearrange("(p j) c -> p j c", j=PACK))
             return raw
 
         def load_w4(b):
@@ -93,14 +93,15 @@ def tile_list_breakaway_gap_scores_kernel(
         def interleave_w2(b):
             grouped = kept([P, PASS, PACK], BF16, f"w2_grouped{b}", "staged")
             if b == 0:
-                nc.gpsimd.tensor_copy(
-                    grouped[:].rearrange("p (t q i) j -> p t q i j", q=BLOCKS, t=PACK),
-                    w2_raw[b][:].rearrange("p j (q t i) -> p t q i j", q=BLOCKS, t=PACK),
-                )
+                for u in range(2):
+                    nc.gpsimd.tensor_copy(
+                        grouped[:].rearrange("p (t q i) j -> p t q i j", q=BLOCKS, t=PACK)[:, :, 8 * u : 8 * u + 8],
+                        w2_raw[u].rearrange("p j (q t i) -> p t q i j", q=BLOCKS // 2, t=PACK),
+                    )
                 return grouped
             nc.vector.tensor_copy(
                 grouped[:].rearrange("p (t q i) j -> p t q j i", q=BLOCKS, t=PACK),
-                w2_raw[b][:].rearrange("p j (q t i) -> p t q j i", q=BLOCKS, t=PACK),
+                w2_raw[2].rearrange("p j (q t i) -> p t q j i", q=BLOCKS, t=PACK),
             )
             return grouped
 
@@ -120,10 +121,9 @@ def tile_list_breakaway_gap_scores_kernel(
         tab_s = at(2 * H, [P, T], U8, "tab_s")
         tab_w = at(TAB_AT, [P, T], I32, "tab_w")
         w1_raw = at(W1_AT, [P, 2 * H], U8, "w1_raw")[:]
-        w3_raw = at(W3_AT, [P, PACK * H], U8, "w3_raw")
         warm = kept([P, 16], F32, "warm")
         nc.gpsimd.memset(warm[:, 0:1], 0.0)
-        rows = at(W2_AT, [P, TAB_AT - W2_AT], U8, "rows")[:, 0 : S + 2 * H]
+        rows = at(W3_AT, [P, TAB_AT - W3_AT], U8, "rows")[:, 0 : S + 2 * H]
         first_s = kept([P, S + 2 * H], U8, "first_s")
         nc.vector.memset(tab_s[0 : P - BLOCKS, :].bitcast(I32), 0)
         nc.gpsimd.memset(ws_raw[LAST_QUADRANT.start : P - BLOCKS, :].bitcast(I32), 0)
@@ -134,11 +134,10 @@ def tile_list_breakaway_gap_scores_kernel(
         nc.sync.dma_start(ws_raw[P - BLOCKS : P, 0:H].bitcast(I32), w1_scales[0].bitcast(I32))
         nc.sync.dma_start(ws_raw[P - BLOCKS : P, H:].bitcast(I32), w3_scales[0].bitcast(I32))
         nc.sync.dma_start(pos1_sb[:], pos1)
-        nc.sync.dma_start(pos3_sb[:], pos3)
         nc.sync.dma_start(tab_w[:], tab_words[0].rearrange("p t i -> p (t i)").bitcast(I32))
-        nc.sync.dma_start(pos2_sb[:], pos2)
         nc.sync.dma_start(w1_raw.bitcast(I32), w1_words[0].bitcast(I32))
-        nc.sync.dma_start(w3_raw[:].bitcast(I32), w3_words[0].rearrange("p c i -> p (c i)").bitcast(I32))
+        nc.sync.dma_start(pos3_sb[:], pos3)
+        nc.sync.dma_start(pos2_sb[:], pos2)
 
         nc.scalar.activation(warm[:, 8:9], warm[:, 0:1], SIGMOID)
 
@@ -152,7 +151,9 @@ def tile_list_breakaway_gap_scores_kernel(
         v_s = [first_s[:, h * BANK : (h + 1) * BANK] for h in range(PARTS)]
         w1_s, w3_s = first_s[:, S : S + H], first_s[:, S + H :]
 
-        w2_raw = [load_w2(b) for b in range(PASSES)]
+        w3_raw = at(W3_AT, [P, PACK * H], U8, "w3_raw")
+        nc.sync.dma_start(w3_raw[:].bitcast(I32), w3_words[0].rearrange("p c i -> p (c i)").bitcast(I32))
+        w2_raw = [load_w2(0, PASS // 2, 0), load_w2(PASS // 2, PASS // 2, RAW_BYTES // 2, 2 * PACK), load_w2(PASS, PASS, 3 * RAW_BYTES // 2)]
         w4_raw = [load_w4(b) for b in range(PASSES)]
 
         idle_bank = psum.tile([P, BANK], F32, name="idle_bank", tag=f"bank{BANKS - 1}")
@@ -183,33 +184,39 @@ def tile_list_breakaway_gap_scores_kernel(
 
         def project_x1(s, h):
             cols = slice(s * P, (s + 1) * P)
-            project(x1[s], h, w1_w[:, 2 * s * P : 2 * (s + 1) * P].bitcast(FP4X4), w1_s[:, cols], s == 1 or (s == 2 and h == 0))
+            project(x1[s], h, w1_w[:, 2 * s * P : 2 * (s + 1) * P].bitcast(FP4X4), w1_s[:, cols], 0 < s < EARLY and (s, h) != (1, 0))
 
         z = kept([P, PACK, M], F32, "z")
         z_lead = kept([P, PACK, CHUNKS[0].stop], F32, "z_lead")
-        gated, x2, w2_q, w4_q, z_first, staged, fronts = [], [], [], [], [], [], []
+        gated, x2, w2_q, w4_q, z_first, staged, fronts, leads = [], [], [], [], [], [], [], []
 
         def columns(picks_sb, m):
             return picks_sb[:, m.start // PER_COLUMN : m.stop // PER_COLUMN]
 
-        def front(s):
-            cols = slice(s * P, (s + 1) * P)
+        def project_leader(s):
             if s >= EARLY:
                 x1.append(kept([P, S], F32, f"x1_{s}", after=f"x3_{s - AHEAD}" if s >= AHEAD else ""))
-            for h in range(1 if s < EARLY else 0, PARTS):
+            for h in range(1 if s < 2 else 0, PARTS):
                 project_x1(s, h)
+
+        def leader(s):
             lead = kept([P, M], F32, f"lead{s}")[:]
             nc.scalar.activation(lead, x1[s][:].indirect(pos1_sb[:]), SIGMOID)
+            leads.append(lead)
+
+        def front(s):
+            cols = slice(s * P, (s + 1) * P)
+            lead = leads[s]
             x3 = kept([P, S], F32, f"x3_{s}")
             for h in range(PARTS):
-                on_vector = s < EARLY or (s == EARLY and h == 0)
+                on_vector = s == 0 or (s, h) == (1, 0)
                 project(x3, h, w3_w[:, PACK * s * P : PACK * (s + 1) * P].bitcast(FP8X4), w3_s[:, cols], on_vector)
             fronts.append((x3, lead))
 
         def gate(s):
             x3, lead = fronts[s]
             if s < SLICES - 1:
-                whole = at(W2_AT + 4 * M * s, [P, M], F32, f"gated{s}") if s <= EARLY else kept([P, M], F32, f"gated{s}")
+                whole = at(W2_AT + RAW_BYTES // 2 + 4 * M * s, [P, M], F32, f"gated{s}") if s < 4 else kept([P, M], F32, f"gated{s}")
                 nc.vector.tensor_tensor(whole[:], x3[:].indirect(pos3_sb[:]), lead, MULT)
                 gated.append([whole[:, m] for m in CHUNKS] + [whole[:]])
             else:
@@ -240,14 +247,21 @@ def tile_list_breakaway_gap_scores_kernel(
             if s == PACK - 1:
                 staged.append(("z_first", interleave("z_first_grouped", z[:], "staged"), z_first))
 
-        for s in range(EARLY):
+        for s in range(2):
             project_x1(s, 0)
         w2_first = interleave_w2(0)
-        for s in range(EARLY + 1):
-            front(s)
+        for s in range(EARLY):
+            project_leader(s)
+        for s in range(EARLY + 2):
+            if s >= 2:
+                front(s - 2)
+            if s < EARLY:
+                leader(s)
         w2_q.append(quantise("w2_0", w2_first))
         for s in range(SLICES + LAG):
-            if EARLY < s < SLICES:
+            if EARLY <= s < SLICES:
+                project_leader(s)
+                leader(s)
                 front(s)
             if s < SLICES:
                 gate(s)

@@ -33,7 +33,7 @@ VECTOR_BANKS = 5
 RAW_BYTES = PACK * PASS * 4
 W3_AT = 2 * H + T
 W2_AT = W3_AT + PACK * H
-W4_AT = W2_AT + PASSES * RAW_BYTES + RAW_BYTES // 2
+W4_AT = W2_AT + 3 * RAW_BYTES
 TAB_AT = W4_AT + PASSES * RAW_BYTES
 W1_AT = TAB_AT + 4 * T
 LAST_QUADRANT = slice(96, P)
@@ -151,9 +151,15 @@ def tile_list_breakaway_gap_scores_kernel(
         v_s = [first_s[:, h * BANK : (h + 1) * BANK] for h in range(PARTS)]
         w1_s, w3_s = first_s[:, S : S + H], first_s[:, S + H :]
 
-        w3_raw = at(W3_AT, [P, PACK * H], U8, "w3_raw")
-        nc.sync.dma_start(w3_raw[:].bitcast(I32), w3_words[0].rearrange("p c i -> p (c i)").bitcast(I32))
-        w2_raw = [load_w2(0, PASS // 2, 0), load_w2(PASS // 2, PASS // 2, RAW_BYTES // 2, 2 * PACK), load_w2(PASS, PASS, 3 * RAW_BYTES // 2)]
+        def load_w3(b):
+            raw = at(W3_AT + b * PACK * PASS, [P, PACK * PASS], U8, f"w3_raw{b}")
+            nc.sync.dma_start(raw[:].bitcast(I32), w3_words[0][:, b * PASS : (b + 1) * PASS, :].rearrange("p c i -> p (c i)").bitcast(I32))
+            return raw
+
+        w3_raw = [load_w3(0)]
+        w2_raw = [load_w2(0, PASS // 2, 0), load_w2(PASS // 2, PASS // 2, RAW_BYTES // 2, 3 * PACK)]
+        w3_raw.append(load_w3(1))
+        w2_raw.append(load_w2(PASS, PASS, 2 * RAW_BYTES))
         w4_raw = [load_w4(b) for b in range(PASSES)]
 
         idle_bank = psum.tile([P, BANK], F32, name="idle_bank", tag=f"bank{BANKS - 1}")
@@ -168,7 +174,7 @@ def tile_list_breakaway_gap_scores_kernel(
         w1_w = in_slice_order(kept([P, 2 * H], U8, "w1_w")[:], w1_raw, copy=nc.gpsimd.tensor_copy)
         v_w.append(kept([P, BANK], I32, "v_w1"))
         nc.vector.tensor_copy(v_w[1][:].bitcast(U32), tab_w[:].bitcast(U32).indirect(part_offs[1]))
-        w3_w = in_slice_order(kept([P, PACK * H], U8, "w3_w")[:], w3_raw[:], copy=nc.gpsimd.tensor_copy)
+        w3_w = [in_slice_order(kept([P, PACK * PASS], U8, "w3_w0")[:], w3_raw[0][:], 1, nc.gpsimd.tensor_copy)]
 
 
         def project(x, h, lhs, lhs_scale, on_vector=False):
@@ -188,7 +194,7 @@ def tile_list_breakaway_gap_scores_kernel(
 
         z = kept([P, PACK, M], F32, "z")
         z_lead = kept([P, PACK, CHUNKS[0].stop], F32, "z_lead")
-        gated, x2, w2_q, w4_q, z_first, staged, fronts, leads = [], [], [], [], [], [], [], []
+        gated, x2, w2_q, w4_q, z_first, staged, fronts, leads, held = [], [], [], [], [], [], [], [], []
 
         def columns(picks_sb, m):
             return picks_sb[:, m.start // PER_COLUMN : m.stop // PER_COLUMN]
@@ -210,7 +216,7 @@ def tile_list_breakaway_gap_scores_kernel(
             x3 = kept([P, S], F32, f"x3_{s}")
             for h in range(PARTS):
                 on_vector = s == 0 or (s, h) == (1, 0)
-                project(x3, h, w3_w[:, PACK * s * P : PACK * (s + 1) * P].bitcast(FP8X4), w3_s[:, cols], on_vector)
+                project(x3, h, w3_w[s // PACK][:, PACK * (s % PACK) * P : PACK * (s % PACK + 1) * P].bitcast(FP8X4), w3_s[:, cols], on_vector)
             fronts.append((x3, lead))
 
         def gate(s):
@@ -227,7 +233,8 @@ def tile_list_breakaway_gap_scores_kernel(
                 gated.append([first[:]] + [rest[:, m.start - split : m.stop - split] for m in CHUNKS[1:]])
             if staged:
                 name, grouped, done = staged.pop()
-                done.append(quantise(name, grouped, after=f"lead{s}"))
+                done.append(quantise(name, grouped[:, 0 : CHUNKS[0].stop, :] if name == "z_first" else grouped, after=f"lead{s}"))
+                held.append(grouped)
             if s == 0:
                 staged.append(("w2_1", interleave_w2(1), w2_q))
             elif s <= PASSES:
@@ -253,11 +260,13 @@ def tile_list_breakaway_gap_scores_kernel(
         for s in range(EARLY):
             project_leader(s)
         for s in range(EARLY + 2):
+            if s - 2 == PACK:
+                w2_q.append(quantise("w2_0", w2_first))
+                w3_w.append(in_slice_order(at(W2_AT + RAW_BYTES // 2 + 8192, [P, PACK * PASS], U8, "w3_w1")[:], w3_raw[1][:], 1))
             if s >= 2:
                 front(s - 2)
             if s < EARLY:
                 leader(s)
-        w2_q.append(quantise("w2_0", w2_first))
         for s in range(SLICES + LAG):
             if EARLY <= s < SLICES:
                 project_leader(s)
@@ -281,8 +290,12 @@ def tile_list_breakaway_gap_scores_kernel(
                     start=(b == 0 and j % 2 == 0), stop=(b == PASSES - 1 and j % 2 == 1),
                 )
 
-        for c, m in enumerate(CHUNKS):
-            product(c, 0, z_first[0][0][:, m], z_first[0][1][:, m])
+        product(0, 0, z_first[0][0][:], z_first[0][1][:])
+        split = CHUNKS[0].stop
+        words, scales = quantise("z_rest", held[-1][:, split:, :], after="lead1")
+        for d in range(1, len(CHUNKS)):
+            cols = slice(CHUNKS[d].start - split, CHUNKS[d].stop - split)
+            product(d, 0, words[:, cols], scales[:, cols])
 
         out_rows = out.rearrange("(j p) m -> p j m", p=P)
         holds = ("", "gated_first", "z_last_grouped0")

@@ -109,7 +109,7 @@ def tile_list_breakaway_gap_scores_kernel(
 
         def next_bank(on_vector):
             mine = taken[on_vector]
-            bank = len(mine) % VECTOR_BANKS if on_vector else (VECTOR_BANKS + len(mine)) % BANKS
+            bank = len(mine) % VECTOR_BANKS if on_vector else (VECTOR_BANKS + len(mine) if len(mine) < 3 else VECTOR_BANKS + len(mine) - 3) % BANKS
             mine.append(psum.tile([P, BANK], F32, name=f"acc{bank}_{len(mine)}", tag=f"bank{bank}"))
             return mine[-1]
 
@@ -124,6 +124,7 @@ def tile_list_breakaway_gap_scores_kernel(
         warm = kept([P, 16], F32, "warm")
         nc.gpsimd.memset(warm[:, 0:1], 0.0)
         rows = at(W3_AT, [P, TAB_AT - W3_AT], U8, "rows")[:, 0 : S + 2 * H]
+        other_rows = kept([P, S + 2 * H], U8, "other_rows")[:]
         first_s = kept([P, S + 2 * H], U8, "first_s")
         nc.vector.memset(tab_s[0 : P - BLOCKS, :].bitcast(I32), 0)
         nc.gpsimd.memset(ws_raw[LAST_QUADRANT.start : P - BLOCKS, :].bitcast(I32), 0)
@@ -143,11 +144,14 @@ def tile_list_breakaway_gap_scores_kernel(
 
         part_offs = [offs_sb[:, h * BANK // PER_COLUMN : (h + 1) * BANK // PER_COLUMN] for h in range(PARTS)]
         picked_s = kept([P, S], U8, "picked_s")
-        in_slice_order(rows[LAST_QUADRANT, S:], ws_raw[LAST_QUADRANT, :], 2 * PASSES)
+        for staging in (rows, other_rows):
+            in_slice_order(staging[LAST_QUADRANT, S:], ws_raw[LAST_QUADRANT, :], 2 * PASSES, nc.gpsimd.tensor_copy)
         nc.vector.tensor_copy(picked_s[:], tab_s[:].indirect(offs_sb[:]))
-        nc.vector.tensor_copy(rows[LAST_QUADRANT, 0:S].bitcast(I32), picked_s[LAST_QUADRANT, :].bitcast(I32))
+        for staging in (rows, other_rows):
+            nc.vector.tensor_copy(staging[LAST_QUADRANT, 0:S].bitcast(I32), picked_s[LAST_QUADRANT, :].bitcast(I32))
         for r in range(4):
-            nc.scalar.dma_start(first_s[r:P:32, :].bitcast(I32), rows[P - BLOCKS + r : P : 4, :].bitcast(I32))
+            staging = rows if r < 2 else other_rows
+            nc.scalar.dma_start(first_s[r:P:32, :].bitcast(I32), staging[P - BLOCKS + r : P : 4, :].bitcast(I32))
         v_s = [first_s[:, h * BANK : (h + 1) * BANK] for h in range(PARTS)]
         w1_s, w3_s = first_s[:, S : S + H], first_s[:, S + H :]
 
@@ -156,9 +160,8 @@ def tile_list_breakaway_gap_scores_kernel(
             nc.sync.dma_start(raw[:].bitcast(I32), w3_words[0][:, b * PASS : (b + 1) * PASS, :].rearrange("p c i -> p (c i)").bitcast(I32))
             return raw
 
-        w3_raw = [load_w3(0)]
+        w3_raw = [load_w3(b) for b in range(PASSES)]
         w2_raw = [load_w2(0, PASS // 2, 0), load_w2(PASS // 2, PASS // 2, RAW_BYTES // 2, 3 * PACK)]
-        w3_raw.append(load_w3(1))
         w2_raw.append(load_w2(PASS, PASS, 2 * RAW_BYTES))
         w4_raw = [load_w4(b) for b in range(PASSES)]
 
@@ -174,7 +177,7 @@ def tile_list_breakaway_gap_scores_kernel(
         w1_w = in_slice_order(kept([P, 2 * H], U8, "w1_w")[:], w1_raw, copy=nc.gpsimd.tensor_copy)
         v_w.append(kept([P, BANK], I32, "v_w1"))
         nc.vector.tensor_copy(v_w[1][:].bitcast(U32), tab_w[:].bitcast(U32).indirect(part_offs[1]))
-        w3_w = [in_slice_order(kept([P, PACK * PASS], U8, "w3_w0")[:], w3_raw[0][:], 1, nc.gpsimd.tensor_copy)]
+        w3_w = [in_slice_order(kept([P, PACK * PASS], U8, f"w3_w{b}")[:], w3_raw[b][:], 1, nc.gpsimd.tensor_copy) for b in range(PASSES)]
 
 
         def project(x, h, lhs, lhs_scale, on_vector=False):
@@ -201,7 +204,7 @@ def tile_list_breakaway_gap_scores_kernel(
 
         def project_leader(s):
             if s >= EARLY:
-                x1.append(kept([P, S], F32, f"x1_{s}", after=f"x3_{s - AHEAD}" if s >= AHEAD else ""))
+                x1.append(kept([P, S], F32, f"x1_{s}", after=("x3_0", "x3_1", "x1_1")[s - AHEAD] if s >= AHEAD else ""))
             for h in range(1 if s < 2 else 0, PARTS):
                 project_x1(s, h)
 
@@ -213,7 +216,7 @@ def tile_list_breakaway_gap_scores_kernel(
         def front(s):
             cols = slice(s * P, (s + 1) * P)
             lead = leads[s]
-            x3 = kept([P, S], F32, f"x3_{s}")
+            x3 = kept([P, S], F32, f"x3_{s}", after=f"x1_{s - 1}" if 2 <= s < EARLY else "")
             for h in range(PARTS):
                 on_vector = s == 0 or (s, h) == (1, 0)
                 project(x3, h, w3_w[s // PACK][:, PACK * (s % PACK) * P : PACK * (s % PACK + 1) * P].bitcast(FP8X4), w3_s[:, cols], on_vector)
@@ -244,7 +247,7 @@ def tile_list_breakaway_gap_scores_kernel(
         def chase(s):
             b, t = divmod(s, PACK)
             cols = slice(t * P, (t + 1) * P)
-            x2.append(kept([P, S], F32, f"x2_{s}", after=f"x1_{s}" if s in (0, 2) else ""))
+            x2.append(kept([P, S], F32, f"x2_{s}", after=f"x1_{s}" if s == 0 else ""))
             for h in range(PARTS):
                 project(x2[s], h, w2_q[b][0][:, cols].bitcast(FP8X4), w2_q[b][1][:, cols])
             if b == 0:
@@ -262,7 +265,6 @@ def tile_list_breakaway_gap_scores_kernel(
         for s in range(EARLY + 2):
             if s - 2 == PACK:
                 w2_q.append(quantise("w2_0", w2_first))
-                w3_w.append(in_slice_order(at(W2_AT + RAW_BYTES // 2 + 8192, [P, PACK * PASS], U8, "w3_w1")[:], w3_raw[1][:], 1))
             if s >= 2:
                 front(s - 2)
             if s < EARLY:

@@ -15,6 +15,7 @@ FP8X4 = mybir.dt.float8_e4m3fn_x4
 FP4X4 = mybir.dt.float4_e2m1fn_x4
 MULT = mybir.AluOpType.mult
 SIGMOID = mybir.ActivationFunctionType.Sigmoid
+COPY = mybir.ActivationFunctionType.Copy
 
 P = 128
 PACK = 4
@@ -27,20 +28,19 @@ BANK = 512
 BANKS = 8
 PARTS = S // BANK
 PER_COLUMN = 16
-LINE = 4
+PAIR = 2
 CHUNKS = (slice(0, 256), slice(256, 384), slice(384, 512))
 VECTOR_BANKS = 5
 RAW_BYTES = PACK * PASS * 4
 W3_AT = 2 * H + T
 W2_AT = W3_AT + PACK * H
-W4_AT = W2_AT + 3 * RAW_BYTES
-TAB_AT = W4_AT + PASSES * RAW_BYTES
+W4_AT = W2_AT + PASSES * RAW_BYTES
+W1_ORDERED_AT = W4_AT + PASSES * RAW_BYTES
+TAB_AT = W1_ORDERED_AT + 2 * H
 W1_AT = TAB_AT + 4 * T
+LATE_AT = W1_AT + 2 * H
 LAST_QUADRANT = slice(96, P)
 WARM_PASSES = 3
-AHEAD = 5
-LAG = 3
-EARLY = 5
 
 
 def tile_list_breakaway_gap_scores_kernel(
@@ -58,9 +58,15 @@ def tile_list_breakaway_gap_scores_kernel(
         def at(offset, shape, dtype, name):
             return placed.tile(shape, dtype, name=name, offset=offset, align_bytes=64)
 
-        def load_w2(first, width, offset, planes=PACK):
-            raw = at(W2_AT + offset, [P, planes, width], F32, f"w2_raw{first}")[:, 0:PACK, :]
-            nc.sync.dma_start(raw, w2[:, first : first + width].rearrange("(p j) c -> p j c", j=PACK))
+        def load_w2(first, width):
+            raw = at(W2_AT + first * PACK * 4, [P, PACK, width], F32, f"w2_raw{first}")
+            nc.sync.dma_start(raw[:], w2[:, first : first + width].rearrange("(p j) c -> p j c", j=PACK))
+            return raw
+
+        def load_w3(b):
+            raw = at(W3_AT + b * PACK * PASS, [P, PACK * PASS], U8, f"w3_raw{b}")
+            words = w3_words[0][:, b * PASS : (b + 1) * PASS, :].rearrange("p c i -> p (c i)")
+            nc.sync.dma_start(raw[:].bitcast(I32), words.bitcast(I32))
             return raw
 
         def load_w4(b):
@@ -70,48 +76,21 @@ def tile_list_breakaway_gap_scores_kernel(
                 nc.sync.dma_start(raw[:, t, :], rows[t])
             return raw
 
-        def in_slice_order(ordered, raw, passes=PASSES, copy=nc.vector.tensor_copy):
+        def in_slice_order(ordered, raw, passes):
             src = raw.bitcast(I32).rearrange("p (b q t w) -> p b t q w", b=passes, q=BLOCKS, t=PACK)
             dst = ordered.bitcast(I32).rearrange("p (b t q w) -> p b t q w", b=passes, q=BLOCKS, t=PACK)
-            copy(dst, src)
+            nc.gpsimd.tensor_copy(dst, src)
             return ordered
 
-        def interleave(name, planes, after="", copy=nc.vector.tensor_copy):
-            grouped = kept([P, planes.shape[2], PACK], BF16, name, after)
-            copy(
-                grouped[:].rearrange("p (c i) j -> p c j i", i=LINE),
-                planes.rearrange("p j (c i) -> p c j i", i=LINE),
-            )
-            return grouped
-
-        def quantise(name, grouped, after=""):
-            words = kept([P, grouped.shape[1]], I32, name + "_words", after)
-            scales = kept([P, grouped.shape[1]], U8, name + "_scales")
-            nc.vector.quantize_mx(words[:].bitcast(FP8X4), scales[:], grouped[:].rearrange("p c j -> p (c j)"))
+        def quantise(words, scales, grouped):
+            nc.vector.quantize_mx(words.bitcast(FP8X4), scales, grouped.rearrange("p c j -> p (c j)"))
             return words, scales
 
-        def interleave_w2(b):
-            grouped = kept([P, PASS, PACK], BF16, f"w2_grouped{b}", "staged")
-            if b == 0:
-                for u in range(2):
-                    nc.gpsimd.tensor_copy(
-                        grouped[:].rearrange("p (t q i) j -> p t q i j", q=BLOCKS, t=PACK)[:, :, 8 * u : 8 * u + 8],
-                        w2_raw[u].rearrange("p j (q t i) -> p t q i j", q=BLOCKS // 2, t=PACK),
-                    )
-                return grouped
-            nc.vector.tensor_copy(
-                grouped[:].rearrange("p (t q i) j -> p t q j i", q=BLOCKS, t=PACK),
-                w2_raw[2].rearrange("p j (q t i) -> p t q j i", q=BLOCKS, t=PACK),
-            )
-            return grouped
+        taken = []
 
-        taken = {True: [], False: []}
-
-        def next_bank(on_vector):
-            mine = taken[on_vector]
-            bank = len(mine) % VECTOR_BANKS if on_vector else (VECTOR_BANKS + len(mine) if len(mine) < 3 else VECTOR_BANKS + len(mine) - 3) % BANKS
-            mine.append(psum.tile([P, BANK], F32, name=f"acc{bank}_{len(mine)}", tag=f"bank{bank}"))
-            return mine[-1]
+        def bank(number):
+            taken.append(psum.tile([P, BANK], F32, name=f"acc{len(taken)}", tag=f"bank{number}"))
+            return taken[-1]
 
         offs_sb = keep.tile([P, S // PER_COLUMN], U16, name="offs_sb")
         pos1_sb = keep.tile([P, M // PER_COLUMN], U16, name="pos1_sb")
@@ -123,7 +102,7 @@ def tile_list_breakaway_gap_scores_kernel(
         w1_raw = at(W1_AT, [P, 2 * H], U8, "w1_raw")[:]
         warm = kept([P, 16], F32, "warm")
         nc.gpsimd.memset(warm[:, 0:1], 0.0)
-        rows = at(W3_AT, [P, TAB_AT - W3_AT], U8, "rows")[:, 0 : S + 2 * H]
+        rows = at(W3_AT, [P, W1_ORDERED_AT - W3_AT], U8, "rows")[:, 0 : S + 2 * H]
         other_rows = kept([P, S + 2 * H], U8, "other_rows")[:]
         first_s = kept([P, S + 2 * H], U8, "first_s")
         nc.vector.memset(tab_s[0 : P - BLOCKS, :].bitcast(I32), 0)
@@ -145,7 +124,7 @@ def tile_list_breakaway_gap_scores_kernel(
         part_offs = [offs_sb[:, h * BANK // PER_COLUMN : (h + 1) * BANK // PER_COLUMN] for h in range(PARTS)]
         picked_s = kept([P, S], U8, "picked_s")
         for staging in (rows, other_rows):
-            in_slice_order(staging[LAST_QUADRANT, S:], ws_raw[LAST_QUADRANT, :], 2 * PASSES, nc.gpsimd.tensor_copy)
+            in_slice_order(staging[LAST_QUADRANT, S:], ws_raw[LAST_QUADRANT, :], 2 * PASSES)
         nc.vector.tensor_copy(picked_s[:], tab_s[:].indirect(offs_sb[:]))
         for staging in (rows, other_rows):
             nc.vector.tensor_copy(staging[LAST_QUADRANT, 0:S].bitcast(I32), picked_s[LAST_QUADRANT, :].bitcast(I32))
@@ -155,17 +134,11 @@ def tile_list_breakaway_gap_scores_kernel(
         v_s = [first_s[:, h * BANK : (h + 1) * BANK] for h in range(PARTS)]
         w1_s, w3_s = first_s[:, S : S + H], first_s[:, S + H :]
 
-        def load_w3(b):
-            raw = at(W3_AT + b * PACK * PASS, [P, PACK * PASS], U8, f"w3_raw{b}")
-            nc.sync.dma_start(raw[:].bitcast(I32), w3_words[0][:, b * PASS : (b + 1) * PASS, :].rearrange("p c i -> p (c i)").bitcast(I32))
-            return raw
-
         w3_raw = [load_w3(b) for b in range(PASSES)]
-        w2_raw = [load_w2(0, PASS // 2, 0), load_w2(PASS // 2, PASS // 2, RAW_BYTES // 2, 3 * PACK)]
-        w2_raw.append(load_w2(PASS, PASS, 2 * RAW_BYTES))
+        w2_raw = [load_w2(0, PASS // 2), load_w2(PASS // 2, PASS // 2), load_w2(PASS, PASS)]
         w4_raw = [load_w4(b) for b in range(PASSES)]
 
-        idle_bank = psum.tile([P, BANK], F32, name="idle_bank", tag=f"bank{BANKS - 1}")
+        idle_bank = bank(BANKS - 1)
         for k in range(WARM_PASSES):
             nc.tensor.matmul_mx(
                 idle_bank[:], lhsT=tab_w[:, 0:P].bitcast(FP8X4), lhsT_scale=tab_s[:, 0:P],
@@ -174,112 +147,129 @@ def tile_list_breakaway_gap_scores_kernel(
 
         v_w = [at(0, [P, BANK], I32, "v_w0")]
         nc.vector.tensor_copy(v_w[0][:].bitcast(U32), tab_w[:].bitcast(U32).indirect(part_offs[0]))
-        w1_w = in_slice_order(kept([P, 2 * H], U8, "w1_w")[:], w1_raw, copy=nc.gpsimd.tensor_copy)
+        w1_w = in_slice_order(at(W1_ORDERED_AT, [P, 2 * H], U8, "w1_w")[:], w1_raw, PASSES)
         v_w.append(kept([P, BANK], I32, "v_w1"))
         nc.vector.tensor_copy(v_w[1][:].bitcast(U32), tab_w[:].bitcast(U32).indirect(part_offs[1]))
-        w3_w = [in_slice_order(kept([P, PACK * PASS], U8, f"w3_w{b}")[:], w3_raw[b][:], 1, nc.gpsimd.tensor_copy) for b in range(PASSES)]
+        w3_w = [in_slice_order(kept([P, PACK * PASS], U8, f"w3_w{b}")[:], w3_raw[b][:], 1) for b in range(PASSES)]
 
+        w2_grouped = [kept([P, PASS, PACK], BF16, f"w2_grouped{b}") for b in range(PASSES)]
+        w4_grouped = [kept([P, N, PACK], BF16, f"w4_grouped{b}") for b in range(PASSES)]
+        for raw, b, blocks in zip(w2_raw, (0, 0, 1), (slice(0, 8), slice(8, 16), slice(0, 16))):
+            nc.gpsimd.tensor_copy(
+                w2_grouped[b][:].rearrange("p (t q i) j -> p t q i j", q=BLOCKS, t=PACK)[:, :, blocks],
+                raw[:].rearrange("p j (q t i) -> p t q i j", t=PACK, i=RUN),
+            )
+        for b in range(PASSES):
+            nc.gpsimd.tensor_copy(w4_grouped[b][:], w4_raw[b][:].rearrange("p j c -> p c j"))
 
-        def project(x, h, lhs, lhs_scale, on_vector=False):
-            acc = next_bank(on_vector)
+        def project(x, h, lhs, lhs_scale, number, copy):
+            acc = bank(number)
             nc.tensor.matmul_mx(
                 acc[:], lhsT=lhs, lhsT_scale=lhs_scale, rhs=v_w[h][:].bitcast(FP8X4), rhs_scale=v_s[h],
                 start=True, stop=True,
             )
-            copy = nc.vector.tensor_copy if on_vector else nc.scalar.copy
             copy(x[:, h * BANK : (h + 1) * BANK], acc[:])
 
-        x1 = [kept([P, S], F32, f"x1_{s}") for s in range(EARLY)]
+        turns = {True: [], False: []}
 
-        def project_x1(s, h):
-            cols = slice(s * P, (s + 1) * P)
-            project(x1[s], h, w1_w[:, 2 * s * P : 2 * (s + 1) * P].bitcast(FP4X4), w1_s[:, cols], 0 < s < EARLY and (s, h) != (1, 0))
+        def early_bank(on_vector):
+            mine = turns[on_vector]
+            mine.append(len(mine) % VECTOR_BANKS if on_vector else VECTOR_BANKS + len(mine) % (BANKS - VECTOR_BANKS))
+            return mine[-1], nc.vector.tensor_copy if on_vector else nc.scalar.copy
 
-        z = kept([P, PACK, M], F32, "z")
-        z_lead = kept([P, PACK, CHUNKS[0].stop], F32, "z_lead")
-        gated, x2, w2_q, w4_q, z_first, staged, fronts, leads, held = [], [], [], [], [], [], [], [], []
+        x1 = [kept([P, S], F32, f"x1_{s}") for s in range(SLICES)]
+        x3 = [kept([P, S], F32, f"x3_{s}") for s in range(SLICES)]
+
+        def project_x1(s, h, on_vector):
+            project(x1[s], h, w1_w[:, 2 * s * P : 2 * (s + 1) * P].bitcast(FP4X4), w1_s[:, s * P : (s + 1) * P], *early_bank(on_vector))
+
+        def project_x3(s, h):
+            b, t = divmod(s, PACK)
+            project(x3[s], h, w3_w[b][:, PACK * t * P : PACK * (t + 1) * P].bitcast(FP8X4), w3_s[:, s * P : (s + 1) * P], *early_bank(True))
+
+        first, rest, whole = CHUNKS[0], slice(CHUNKS[0].stop, M), slice(0, M)
+        last = SLICES - 1
+        w2_scales = [at(LATE_AT, [P, PASS], U8, "w2_scales0"), kept([P, PASS], U8, "w2_scales1")]
+        lead_early = kept([P, PACK, M], F32, "lead_early")[:]
+        leads = [lead_early[:, t, :] for t in range(PACK)]
+        helpers = [kept([P, M], F32, f"helper{s}")[:] for s in range(last)]
 
         def columns(picks_sb, m):
             return picks_sb[:, m.start // PER_COLUMN : m.stop // PER_COLUMN]
 
-        def project_leader(s):
-            if s >= EARLY:
-                x1.append(kept([P, S], F32, f"x1_{s}", after=("x3_0", "x3_1", "x1_1")[s - AHEAD] if s >= AHEAD else ""))
-            for h in range(1 if s < 2 else 0, PARTS):
-                project_x1(s, h)
+        def leader(s, m):
+            lead = leads[s] if s < PACK else lead_late[m.start > 0][:, s % PACK, :]
+            nc.scalar.activation(lead, x1[s][:].indirect(columns(pos1_sb, m)), SIGMOID)
 
-        def leader(s):
-            lead = kept([P, M], F32, f"lead{s}")[:]
-            nc.scalar.activation(lead, x1[s][:].indirect(pos1_sb[:]), SIGMOID)
-            leads.append(lead)
+        def helper(s, m):
+            nc.scalar.activation(helpers[s][:, m], x3[s][:].indirect(columns(pos3_sb, m)), COPY)
 
-        def front(s):
-            cols = slice(s * P, (s + 1) * P)
-            lead = leads[s]
-            x3 = kept([P, S], F32, f"x3_{s}", after=f"x1_{s - 1}" if 2 <= s < EARLY else "")
+        for s in range(PACK):
+            project_x1(s, 0, s >= 2)
+        for s in range(PACK):
+            project_x1(s, 1, s >= 1)
+        leader(0, whole)
+        project_x1(last, 0, False)
+        for h in range(PARTS):
+            project_x1(PACK, h, True)
+        leader(1, whole)
+        project_x1(last, 1, False)
+        for s in range(2, PACK):
+            leader(s, whole)
+        for s in range(SLICES):
             for h in range(PARTS):
-                on_vector = s == 0 or (s, h) == (1, 0)
-                project(x3, h, w3_w[s // PACK][:, PACK * (s % PACK) * P : PACK * (s % PACK + 1) * P].bitcast(FP8X4), w3_s[:, cols], on_vector)
-            fronts.append((x3, lead))
+                project_x3(s, h)
+            if s < last:
+                helper(s, whole)
+        for s in range(PACK + 1, last):
+            for h in range(PARTS):
+                project_x1(s, h, True)
 
-        def gate(s):
-            x3, lead = fronts[s]
-            if s < SLICES - 1:
-                whole = at(W2_AT + RAW_BYTES // 2 + 4 * M * s, [P, M], F32, f"gated{s}") if s < 4 else kept([P, M], F32, f"gated{s}")
-                nc.vector.tensor_tensor(whole[:], x3[:].indirect(pos3_sb[:]), lead, MULT)
-                gated.append([whole[:, m] for m in CHUNKS] + [whole[:]])
-            else:
-                split = CHUNKS[0].stop
-                first, rest = kept([P, split], F32, "gated_first"), kept([P, M - split], F32, "gated_rest")
-                for part, m in ((first, CHUNKS[0]), (rest, slice(split, M))):
-                    nc.vector.tensor_tensor(part[:], x3[:].indirect(columns(pos3_sb, m)), lead[:, m], MULT)
-                gated.append([first[:]] + [rest[:, m.start - split : m.stop - split] for m in CHUNKS[1:]])
-            if staged:
-                name, grouped, done = staged.pop()
-                done.append(quantise(name, grouped[:, 0 : CHUNKS[0].stop, :] if name == "z_first" else grouped, after=f"lead{s}"))
-                held.append(grouped)
-            if s == 0:
-                staged.append(("w2_1", interleave_w2(1), w2_q))
-            elif s <= PASSES:
-                b = s - 1
-                staged.append((f"w4_{b}", interleave(f"w4_grouped{b}", w4_raw[b][:], "staged"), w4_q))
+        weight_words = at(TAB_AT - 4 * (H + N), [P, H + N], I32, "weight_words")
+        w2_q = [quantise(weight_words[:, b * PASS : (b + 1) * PASS], w2_scales[b][:], w2_grouped[b][:]) for b in range(PASSES)]
+        w4_q = [quantise(weight_words[:, H:], kept([P, N], U8, "w4_scales0")[:], w4_grouped[0][:])]
 
-        def chase(s):
+        pairs = [at(TAB_AT + b * RAW_BYTES, [P, PACK, M], F32, f"pair{b}")[:] for b in range(PASSES)]
+        late = at(LATE_AT, [P, (PACK + 1) * M], F32, "late")
+        lead_late = [late[:, PACK * m.start : PACK * m.stop].rearrange("p (j m) -> p j m", j=PACK) for m in (first, rest)]
+        helpers.append(late[:, PACK * M :])
+
+        def finish(name, pair, lead):
+            grouped = kept([P, pair.shape[2], PACK], BF16, name)
+            nc.vector.tensor_tensor(
+                grouped[:].rearrange("p (c i) j -> p c j i", i=PAIR),
+                pair.rearrange("p j (c i) -> p c j i", i=PAIR),
+                lead.rearrange("p j (c i) -> p c j i", i=PAIR),
+                MULT,
+            )
+            return grouped
+
+        def chase(s, m):
+            nc.vector.tensor_tensor(pairs[s // PACK][:, s % PACK, m], x2[s][:].indirect(columns(pos2_sb, m)), helpers[s][:, m], MULT)
+
+        x2 = []
+        for s in range(SLICES):
             b, t = divmod(s, PACK)
             cols = slice(t * P, (t + 1) * P)
-            x2.append(kept([P, S], F32, f"x2_{s}", after=f"x1_{s}" if s == 0 else ""))
+            x2.append(kept([P, S], F32, f"x2_{s}", after=f"x3_{s}" if s < last else ""))
+            if s == last:
+                helper(s, first)
             for h in range(PARTS):
-                project(x2[s], h, w2_q[b][0][:, cols].bitcast(FP8X4), w2_q[b][1][:, cols])
-            if b == 0:
-                nc.vector.tensor_tensor(z[:, t, :], x2[s][:].indirect(pos2_sb[:]), gated[s][-1], MULT)
-            else:
-                nc.vector.tensor_tensor(z_lead[:, t, :], x2[s][:].indirect(columns(pos2_sb, CHUNKS[0])), gated[s][0], MULT)
+                project(x2[s], h, w2_q[b][0][:, cols].bitcast(FP8X4), w2_q[b][1][:, cols], (PARTS * s + h + VECTOR_BANKS) % BANKS, nc.scalar.copy)
+            chase(s, whole if s < last else first)
             if s == PACK - 1:
-                staged.append(("z_first", interleave("z_first_grouped", z[:], "staged"), z_first))
+                z_first = finish("z_first", pairs[0], lead_early)
+            if s == PACK + 1:
+                z_early = quantise(kept([P, first.stop], I32, "z_early_words")[:], kept([P, first.stop], U8, "z_early_scales")[:], z_first[:, first, :])
+        for m in (first, rest):
+            leader(PACK, m)
+        for s in range(PACK + 1, SLICES):
+            leader(s, first)
+        helper(last, rest)
+        for s in range(PACK + 1, SLICES):
+            leader(s, rest)
 
-        for s in range(2):
-            project_x1(s, 0)
-        w2_first = interleave_w2(0)
-        for s in range(EARLY):
-            project_leader(s)
-        for s in range(EARLY + 2):
-            if s - 2 == PACK:
-                w2_q.append(quantise("w2_0", w2_first))
-            if s >= 2:
-                front(s - 2)
-            if s < EARLY:
-                leader(s)
-        for s in range(SLICES + LAG):
-            if EARLY <= s < SLICES:
-                project_leader(s)
-                leader(s)
-                front(s)
-            if s < SLICES:
-                gate(s)
-            if s >= LAG:
-                chase(s - LAG)
-
-        accs = [[next_bank(False) for pair in range(2)] for m in CHUNKS]
+        accs = [[bank((2 * c + pair + VECTOR_BANKS) % BANKS) for pair in range(2)] for c in range(len(CHUNKS))]
 
         def product(c, b, words, scales):
             width = CHUNKS[c].stop - CHUNKS[c].start
@@ -292,35 +282,33 @@ def tile_list_breakaway_gap_scores_kernel(
                     start=(b == 0 and j % 2 == 0), stop=(b == PASSES - 1 and j % 2 == 1),
                 )
 
-        product(0, 0, z_first[0][0][:], z_first[0][1][:])
-        split = CHUNKS[0].stop
-        words, scales = quantise("z_rest", held[-1][:, split:, :], after="lead1")
-        for d in range(1, len(CHUNKS)):
-            cols = slice(CHUNKS[d].start - split, CHUNKS[d].stop - split)
-            product(d, 0, words[:, cols], scales[:, cols])
+        def close(c):
+            width = CHUNKS[c].stop - CHUNKS[c].start
+            words, scales = quantise(kept([P, width], I32, f"z_words{c}")[:], kept([P, width], U8, f"z_scales{c}")[:], z_last[c][:])
+            product(c, 1, words, scales)
+
+        product(0, 0, *z_early)
+        w4_q.append(quantise(kept([P, N], I32, "w4_words1", after=f"x1_{PACK}")[:], kept([P, N], U8, "w4_scales1")[:], w4_grouped[1][:]))
+        z_last = [finish("z_last0", pairs[1][:, :, first], lead_late[0])]
+        chase(last, rest)
+        close(0)
+        words, scales = quantise(
+            kept([P, M - first.stop], I32, "z_late_words", after=f"x1_{PACK + 1}")[:], kept([P, M - first.stop], U8, "z_late_scales")[:], z_first[:, rest, :]
+        )
+        for c in range(1, len(CHUNKS)):
+            inner = slice(CHUNKS[c].start - first.stop, CHUNKS[c].stop - first.stop)
+            product(c, 0, words[:, inner], scales[:, inner])
+        for c in range(1, len(CHUNKS)):
+            inner = slice(CHUNKS[c].start - first.stop, CHUNKS[c].stop - first.stop)
+            z_last.append(finish(f"z_last{c}", pairs[1][:, :, CHUNKS[c]], lead_late[1][:, :, inner]))
+        for c in range(1, len(CHUNKS)):
+            close(c)
 
         out_rows = out.rearrange("(j p) m -> p j m", p=P)
-        holds = ("", "gated_first", "z_last_grouped0")
-        grouped = []
-        for c, m in enumerate(CHUNKS):
-            width = m.stop - m.start
-            last = c == len(CHUNKS) - 1
-            planes = z_lead
-            if c:
-                planes = kept([P, PACK, width], F32, f"z_last{c}", holds[c])
-                for t in range(PACK):
-                    nc.vector.tensor_tensor(planes[:, t, :], x2[PACK + t][:].indirect(columns(pos2_sb, m)), gated[PACK + t][c], MULT)
-            if c == 1:
-                words, scales = quantise("z_last0", grouped[0])
-                product(0, 1, words[:], scales[:])
-            grouped.append(interleave(f"z_last_grouped{c}", planes[:], copy=nc.vector.tensor_copy if last else nc.scalar.copy))
-        for c in range(1, len(CHUNKS)):
-            words, scales = quantise(f"z_last{c}", grouped[c])
-            product(c, 1, words[:], scales[:])
         for c, m in enumerate(CHUNKS):
             width = m.stop - m.start
             for pair in range(2):
                 res = kept([P, 2, width], F32, f"res{c}_{pair}")
-                copy = nc.vector.tensor_copy if pair and c == len(CHUNKS) - 1 else nc.scalar.copy
+                copy = nc.vector.tensor_copy if pair and c else nc.scalar.copy
                 copy(res[:].rearrange("p j m -> p (j m)"), accs[c][pair][:, 0 : 2 * width])
                 nc.sync.dma_start(out_rows[:, 2 * pair : 2 * pair + 2, m], res[:])

@@ -29,6 +29,7 @@ BANKS = 8
 PARTS = S // BANK
 PER_COLUMN = 16
 PAIR = 2
+LINE = 4
 CHUNKS = (slice(0, 256), slice(256, 384), slice(384, 512))
 VECTOR_BANKS = 5
 RAW_BYTES = PACK * PASS * 4
@@ -70,7 +71,7 @@ def tile_list_breakaway_gap_scores_kernel(
             return raw
 
         def load_w4(b):
-            raw = at(W4_AT + b * RAW_BYTES, [P, PACK, N], F32, f"w4_raw{b}")
+            raw = at(W4_AT + (1 - b) * RAW_BYTES, [P, PACK, N], F32, f"w4_raw{b}")
             rows = w4[b * PASS : (b + 1) * PASS, :].rearrange("(q t i) n -> t q i n", t=PACK, i=RUN)
             for t in range(PACK):
                 nc.sync.dma_start(raw[:, t, :], rows[t])
@@ -153,14 +154,13 @@ def tile_list_breakaway_gap_scores_kernel(
         w3_w = [in_slice_order(kept([P, PACK * PASS], U8, f"w3_w{b}")[:], w3_raw[b][:], 1) for b in range(PASSES)]
 
         w2_grouped = [kept([P, PASS, PACK], BF16, f"w2_grouped{b}") for b in range(PASSES)]
-        w4_grouped = [kept([P, N, PACK], BF16, f"w4_grouped{b}") for b in range(PASSES)]
+        w4_grouped = [kept([P, N, PACK], BF16, "w4_grouped0")]
         for raw, b, blocks in zip(w2_raw, (0, 0, 1), (slice(0, 8), slice(8, 16), slice(0, 16))):
             nc.gpsimd.tensor_copy(
                 w2_grouped[b][:].rearrange("p (t q i) j -> p t q i j", q=BLOCKS, t=PACK)[:, :, blocks],
                 raw[:].rearrange("p j (q t i) -> p t q i j", t=PACK, i=RUN),
             )
-        for b in range(PASSES):
-            nc.gpsimd.tensor_copy(w4_grouped[b][:], w4_raw[b][:].rearrange("p j c -> p c j"))
+        nc.gpsimd.tensor_copy(w4_grouped[0][:], w4_raw[0][:].rearrange("p j c -> p c j"))
 
         def project(x, h, lhs, lhs_scale, number, copy):
             acc = bank(number)
@@ -229,6 +229,10 @@ def tile_list_breakaway_gap_scores_kernel(
         w2_q = [quantise(weight_words[:, b * PASS : (b + 1) * PASS], w2_scales[b][:], w2_grouped[b][:]) for b in range(PASSES)]
         w4_q = [quantise(weight_words[:, H:], kept([P, N], U8, "w4_scales0")[:], w4_grouped[0][:])]
 
+        w4_grouped.append(kept([P, N, PACK], BF16, "w4_grouped1", after="w2_grouped0"))
+        nc.vector.tensor_copy(
+            w4_grouped[1][:].rearrange("p (c i) j -> p c j i", i=LINE), w4_raw[1][:].rearrange("p j (c i) -> p c j i", i=LINE)
+        )
         pairs = [at(TAB_AT + b * RAW_BYTES, [P, PACK, M], F32, f"pair{b}")[:] for b in range(PASSES)]
         late = at(LATE_AT, [P, (PACK + 1) * M], F32, "late")
         lead_late = [late[:, PACK * m.start : PACK * m.stop].rearrange("p (j m) -> p j m", j=PACK) for m in (first, rest)]

@@ -21,7 +21,8 @@ P = 128
 PACK = 4
 PASS = P * PACK
 BLOCKS = PASS // 32
-RUN = 32 // PACK
+RUN = 2
+GROUPS = P // RUN
 PASSES = H // PASS
 SLICES = PASSES * PACK
 BANK = 512
@@ -34,14 +35,14 @@ CHUNKS = (slice(0, 256), slice(256, 384), slice(384, 512))
 VECTOR_BANKS = 5
 RAW_BYTES = PACK * PASS * 4
 W3_AT = 2 * H + T
-W2_AT = W3_AT + PACK * H
+W2_AT = W3_AT + 2 * H + PACK * H
 W4_AT = W2_AT + PASSES * RAW_BYTES
 W1_ORDERED_AT = W4_AT + PASSES * RAW_BYTES
 TAB_AT = W1_ORDERED_AT + 2 * H
 W1_AT = TAB_AT + 4 * T
 LATE_AT = W1_AT + 2 * H
-LAST_QUADRANT = slice(96, P)
 WARM_PASSES = 3
+LAST_QUADRANT = slice(96, P)
 
 
 def tile_list_breakaway_gap_scores_kernel(
@@ -65,23 +66,26 @@ def tile_list_breakaway_gap_scores_kernel(
             return raw
 
         def load_w3(b):
-            raw = at(W3_AT + b * PACK * PASS, [P, PACK * PASS], U8, f"w3_raw{b}")
+            raw = at(W3_AT + 2 * H + b * PACK * PASS, [P, PACK * PASS], U8, f"w3_raw{b}")
             words = w3_words[0][:, b * PASS : (b + 1) * PASS, :].rearrange("p c i -> p (c i)")
             nc.sync.dma_start(raw[:].bitcast(I32), words.bitcast(I32))
             return raw
 
         def load_w4(b):
-            raw = at(W4_AT + (1 - b) * RAW_BYTES, [P, PACK, N], F32, f"w4_raw{b}")
-            rows = w4[b * PASS : (b + 1) * PASS, :].rearrange("(q t i) n -> t q i n", t=PACK, i=RUN)
+            raw = at(W4_AT + (PASSES - 1 - b) * RAW_BYTES, [P, PACK, N], F32, f"w4_raw{b}")
+            rows = w4[b * PASS : (b + 1) * PASS, :].rearrange("(g t e) n -> t g e n", t=PACK, e=RUN)
             for t in range(PACK):
                 nc.sync.dma_start(raw[:, t, :], rows[t])
             return raw
 
-        def in_slice_order(ordered, raw, passes):
-            src = raw.bitcast(I32).rearrange("p (b q t w) -> p b t q w", b=passes, q=BLOCKS, t=PACK)
-            dst = ordered.bitcast(I32).rearrange("p (b t q w) -> p b t q w", b=passes, q=BLOCKS, t=PACK)
-            nc.gpsimd.tensor_copy(dst, src)
+        def in_slice_order(ordered, raw):
+            src = raw.bitcast(I32).rearrange("p (g t w) -> p t g w", g=GROUPS, t=PACK)
+            nc.gpsimd.tensor_copy(ordered.bitcast(I32).rearrange("p (t g w) -> p t g w", g=GROUPS, t=PACK), src)
             return ordered
+
+        def dealt(ordered, raw, dtype):
+            src = raw.bitcast(dtype).rearrange("p (b g t) -> p b g t", g=GROUPS, t=PACK)
+            nc.scalar.copy(ordered.bitcast(dtype).rearrange("p (b t g) -> p b g t", g=GROUPS, t=PACK), src)
 
         def quantise(words, scales, grouped):
             nc.vector.quantize_mx(words.bitcast(FP8X4), scales, grouped.rearrange("p c j -> p (c j)"))
@@ -97,70 +101,95 @@ def tile_list_breakaway_gap_scores_kernel(
         pos1_sb = keep.tile([P, M // PER_COLUMN], U16, name="pos1_sb")
         pos2_sb = keep.tile([P, M // PER_COLUMN], U16, name="pos2_sb")
         pos3_sb = keep.tile([P, M // PER_COLUMN], U16, name="pos3_sb")
-        ws_raw = at(0, [P, 2 * H], U8, "ws_raw")
+        w1s_raw = at(0, [P, H], U8, "w1s_raw")
+        w3s_raw = kept([P, H], U8, "w3s_raw")
         tab_s = at(2 * H, [P, T], U8, "tab_s")
         tab_w = at(TAB_AT, [P, T], I32, "tab_w")
-        w1_raw = at(W1_AT, [P, 2 * H], U8, "w1_raw")[:]
         warm = kept([P, 16], F32, "warm")
         nc.gpsimd.memset(warm[:, 0:1], 0.0)
-        rows = at(W3_AT, [P, W1_ORDERED_AT - W3_AT], U8, "rows")[:, 0 : S + 2 * H]
-        other_rows = kept([P, S + 2 * H], U8, "other_rows")[:]
-        first_s = kept([P, S + 2 * H], U8, "first_s")
+        rows = at(W3_AT, [P, W1_ORDERED_AT - W3_AT], U8, "rows")[:, 0 : S + H]
+        other_rows = kept([P, S + H], U8, "other_rows")[:]
+        first_s = kept([P, S + H], U8, "first_s")
+        w3_s = kept([P, H], U8, "w3_s")
         nc.vector.memset(tab_s[0 : P - BLOCKS, :].bitcast(I32), 0)
-        nc.gpsimd.memset(ws_raw[LAST_QUADRANT.start : P - BLOCKS, :].bitcast(I32), 0)
-        nc.gpsimd.memset(first_s[:].bitcast(I32), 0)
+        for raw in (w1s_raw, w3s_raw):
+            nc.gpsimd.memset(raw[LAST_QUADRANT.start : P - BLOCKS, :].bitcast(I32), 0)
+        for plane in (first_s, w3_s):
+            nc.gpsimd.memset(plane[:].bitcast(I32), 0)
+
+        def load_w1(b, offset):
+            raw = at(offset, [P, H], U8, f"w1_raw{b}")
+            nc.sync.dma_start(raw[:].bitcast(I32), w1_words[0][:, b * H : (b + 1) * H].bitcast(I32))
+            return raw
 
         nc.sync.dma_start(offs_sb[:], offs)
         nc.sync.dma_start(tab_s[P - BLOCKS : P, :].bitcast(I32), tab_scales[0].bitcast(I32))
-        nc.sync.dma_start(ws_raw[P - BLOCKS : P, 0:H].bitcast(I32), w1_scales[0].bitcast(I32))
-        nc.sync.dma_start(ws_raw[P - BLOCKS : P, H:].bitcast(I32), w3_scales[0].bitcast(I32))
+        nc.sync.dma_start(w1s_raw[P - BLOCKS : P, :].bitcast(I32), w1_scales[0].bitcast(I32))
+        nc.sync.dma_start(w3s_raw[P - BLOCKS : P, :].bitcast(I32), w3_scales[0].bitcast(I32))
         nc.sync.dma_start(pos1_sb[:], pos1)
         nc.sync.dma_start(tab_w[:], tab_words[0].rearrange("p t i -> p (t i)").bitcast(I32))
-        nc.sync.dma_start(w1_raw.bitcast(I32), w1_words[0].bitcast(I32))
+        w1_raw = [load_w1(0, W1_AT)]
         nc.sync.dma_start(pos3_sb[:], pos3)
         nc.sync.dma_start(pos2_sb[:], pos2)
 
         nc.scalar.activation(warm[:, 8:9], warm[:, 0:1], SIGMOID)
 
         part_offs = [offs_sb[:, h * BANK // PER_COLUMN : (h + 1) * BANK // PER_COLUMN] for h in range(PARTS)]
-        picked_s = kept([P, S], U8, "picked_s")
+        picked_s = kept([P, 2 * S], U8, "picked_s")[:, 0:S]
+        w1s_ordered, w3s_ordered = kept([P, H], U8, "w1s_ordered"), kept([P, H], U8, "w3s_ordered")
+        dealt(w1s_ordered[LAST_QUADRANT, :], w1s_raw[LAST_QUADRANT, :], U16)
         for staging in (rows, other_rows):
-            in_slice_order(staging[LAST_QUADRANT, S:], ws_raw[LAST_QUADRANT, :], 2 * PASSES)
-        nc.vector.tensor_copy(picked_s[:], tab_s[:].indirect(offs_sb[:]))
+            nc.gpsimd.tensor_copy(staging[LAST_QUADRANT, S:].bitcast(I32), w1s_ordered[LAST_QUADRANT, :].bitcast(I32))
+        dealt(w3s_ordered[LAST_QUADRANT, :], w3s_raw[LAST_QUADRANT, :], U16)
+        nc.vector.tensor_copy(picked_s, tab_s[:].indirect(offs_sb[:]))
         for staging in (rows, other_rows):
             nc.vector.tensor_copy(staging[LAST_QUADRANT, 0:S].bitcast(I32), picked_s[LAST_QUADRANT, :].bitcast(I32))
         for r in range(4):
             staging = rows if r < 2 else other_rows
             nc.scalar.dma_start(first_s[r:P:32, :].bitcast(I32), staging[P - BLOCKS + r : P : 4, :].bitcast(I32))
         v_s = [first_s[:, h * BANK : (h + 1) * BANK] for h in range(PARTS)]
-        w1_s, w3_s = first_s[:, S : S + H], first_s[:, S + H :]
+        w1_s = first_s[:, S:]
 
+        w1_raw.append(load_w1(1, W3_AT))
+        w3_rows = at(W3_AT + H, [P, H], U8, "w3_rows")
+        nc.gpsimd.tensor_copy(w3_rows[LAST_QUADRANT, :].bitcast(I32), w3s_ordered[LAST_QUADRANT, :].bitcast(I32))
+        for r in range(4):
+            nc.sync.dma_start(w3_s[r:P:32, :].bitcast(I32), w3_rows[P - BLOCKS + r : P : 4, :].bitcast(I32))
         w3_raw = [load_w3(b) for b in range(PASSES)]
         w2_raw = [load_w2(0, PASS // 2), load_w2(PASS // 2, PASS // 2), load_w2(PASS, PASS)]
         w4_raw = [load_w4(b) for b in range(PASSES)]
 
-        idle_bank = bank(BANKS - 1)
+        zeros = kept([P, BANK, PACK], BF16, "zeros")
+        nc.vector.memset(zeros[:].rearrange("p c j -> p (c j)").bitcast(I32), 0)
+        idle_words, idle_scales = quantise(kept([P, BANK], I32, "idle_words", after="picked_s")[:], kept([P, BANK], U8, "idle_scales")[:], zeros[:])
+        idle_bank = bank(VECTOR_BANKS - 1)
         for k in range(WARM_PASSES):
             nc.tensor.matmul_mx(
-                idle_bank[:], lhsT=tab_w[:, 0:P].bitcast(FP8X4), lhsT_scale=tab_s[:, 0:P],
-                rhs=tab_w[:, 0:BANK].bitcast(FP8X4), rhs_scale=tab_s[:, 0:BANK], start=True, stop=True,
+                idle_bank[:], lhsT=idle_words[:, 0:P].bitcast(FP8X4), lhsT_scale=idle_scales[:, 0:P],
+                rhs=idle_words.bitcast(FP8X4), rhs_scale=idle_scales, start=True, stop=True,
             )
 
         v_w = [at(0, [P, BANK], I32, "v_w0")]
-        nc.vector.tensor_copy(v_w[0][:].bitcast(U32), tab_w[:].bitcast(U32).indirect(part_offs[0]))
-        w1_w = in_slice_order(at(W1_ORDERED_AT, [P, 2 * H], U8, "w1_w")[:], w1_raw, PASSES)
+        halves = (slice(0, BANK // 2), slice(BANK // 2, BANK))
+        for m in halves:
+            nc.vector.tensor_copy(v_w[0][:, m].bitcast(U32), tab_w[:].bitcast(U32).indirect(offs_sb[:, m.start // PER_COLUMN : m.stop // PER_COLUMN]))
+        w1_w = at(W1_ORDERED_AT, [P, 2 * H], U8, "w1_w")
+        dealt(w1_w[:, 0:H], w1_raw[0][:], U32)
+        in_slice_order(w1_w[:, H:], w1_raw[1][:])
         v_w.append(kept([P, BANK], I32, "v_w1"))
         nc.vector.tensor_copy(v_w[1][:].bitcast(U32), tab_w[:].bitcast(U32).indirect(part_offs[1]))
-        w3_w = [in_slice_order(kept([P, PACK * PASS], U8, f"w3_w{b}")[:], w3_raw[b][:], 1) for b in range(PASSES)]
+        w3_w = [in_slice_order(kept([P, PACK * PASS], U8, f"w3_w{b}")[:], w3_raw[b][:]) for b in range(PASSES)]
 
         w2_grouped = [kept([P, PASS, PACK], BF16, f"w2_grouped{b}") for b in range(PASSES)]
         w4_grouped = [kept([P, N, PACK], BF16, "w4_grouped0")]
-        for raw, b, blocks in zip(w2_raw, (0, 0, 1), (slice(0, 8), slice(8, 16), slice(0, 16))):
+        for raw, b, groups in zip(w2_raw, (0, 0, 1), (slice(0, GROUPS // 2), slice(GROUPS // 2, GROUPS), slice(0, GROUPS))):
             nc.gpsimd.tensor_copy(
-                w2_grouped[b][:].rearrange("p (t q i) j -> p t q i j", q=BLOCKS, t=PACK)[:, :, blocks],
-                raw[:].rearrange("p j (q t i) -> p t q i j", t=PACK, i=RUN),
+                w2_grouped[b][:].rearrange("p (t g e) j -> p g t j e", t=PACK, e=RUN)[:, groups],
+                raw[:].rearrange("p j (g t e) -> p g t j e", t=PACK, e=RUN),
             )
-        nc.gpsimd.tensor_copy(w4_grouped[0][:], w4_raw[0][:].rearrange("p j c -> p c j"))
+        nc.gpsimd.tensor_copy(
+            w4_grouped[0][:].rearrange("p (c e) j -> p c j e", e=PAIR), w4_raw[0][:].rearrange("p j (c e) -> p c j e", e=PAIR)
+        )
 
         def project(x, h, lhs, lhs_scale, number, copy):
             acc = bank(number)
@@ -204,18 +233,24 @@ def tile_list_breakaway_gap_scores_kernel(
         def helper(s, m):
             nc.scalar.activation(helpers[s][:, m], x3[s][:].indirect(columns(pos3_sb, m)), COPY)
 
+        for m in halves:
+            for s in range(2):
+                acc = bank(early_bank(False)[0])
+                nc.tensor.matmul_mx(
+                    acc[:, m], lhsT=w1_w[:, 2 * s * P : 2 * (s + 1) * P].bitcast(FP4X4), lhsT_scale=w1_s[:, s * P : (s + 1) * P],
+                    rhs=v_w[0][:, m].bitcast(FP8X4), rhs_scale=v_s[0][:, m], start=True, stop=True,
+                )
+                nc.scalar.copy(x1[s][:, m], acc[:, m])
+        for s in range(2, PACK):
+            project_x1(s, 0, True)
         for s in range(PACK):
-            project_x1(s, 0, s >= 2)
-        for s in range(PACK):
-            project_x1(s, 1, s >= 1)
-        leader(0, whole)
-        project_x1(last, 0, False)
+            project_x1(s, 1, s >= 2)
+            if s < 2:
+                leader(s, whole)
         for h in range(PARTS):
             project_x1(PACK, h, True)
-        leader(1, whole)
-        project_x1(last, 1, False)
-        for s in range(2, PACK):
-            leader(s, whole)
+            project_x1(last, h, False)
+            leader(2 + h, whole)
         for s in range(SLICES):
             for h in range(PARTS):
                 project_x3(s, h)
@@ -225,14 +260,15 @@ def tile_list_breakaway_gap_scores_kernel(
             for h in range(PARTS):
                 project_x1(s, h, True)
 
-        weight_words = at(TAB_AT - 4 * (H + N), [P, H + N], I32, "weight_words")
+        weight_words = at(TAB_AT - 4 * H, [P, H], I32, "w2_words")
+        w4_words = kept([P, PASSES * N], I32, "w4_words", after="w2_grouped1")
         w2_q = [quantise(weight_words[:, b * PASS : (b + 1) * PASS], w2_scales[b][:], w2_grouped[b][:]) for b in range(PASSES)]
-        w4_q = [quantise(weight_words[:, H:], kept([P, N], U8, "w4_scales0")[:], w4_grouped[0][:])]
-
         w4_grouped.append(kept([P, N, PACK], BF16, "w4_grouped1", after="w2_grouped0"))
         nc.vector.tensor_copy(
             w4_grouped[1][:].rearrange("p (c i) j -> p c j i", i=LINE), w4_raw[1][:].rearrange("p j (c i) -> p c j i", i=LINE)
         )
+        w4_scales = kept([P, PASSES * N], U8, "w4_scales")
+        w4_q = [quantise(w4_words[:, b * N : (b + 1) * N], w4_scales[:, b * N : (b + 1) * N], w4_grouped[b][:]) for b in range(PASSES)]
         pairs = [at(TAB_AT + b * RAW_BYTES, [P, PACK, M], F32, f"pair{b}")[:] for b in range(PASSES)]
         late = at(LATE_AT, [P, (PACK + 1) * M], F32, "late")
         lead_late = [late[:, PACK * m.start : PACK * m.stop].rearrange("p (j m) -> p j m", j=PACK) for m in (first, rest)]
@@ -260,11 +296,9 @@ def tile_list_breakaway_gap_scores_kernel(
                 helper(s, first)
             for h in range(PARTS):
                 project(x2[s], h, w2_q[b][0][:, cols].bitcast(FP8X4), w2_q[b][1][:, cols], (PARTS * s + h + VECTOR_BANKS) % BANKS, nc.scalar.copy)
-            chase(s, whole if s < last else first)
+            chase(s, whole if s < last - 1 else first)
             if s == PACK - 1:
                 z_first = finish("z_first", pairs[0], lead_early)
-            if s == PACK + 1:
-                z_early = quantise(kept([P, first.stop], I32, "z_early_words")[:], kept([P, first.stop], U8, "z_early_scales")[:], z_first[:, first, :])
         for m in (first, rest):
             leader(PACK, m)
         for s in range(PACK + 1, SLICES):
@@ -291,17 +325,22 @@ def tile_list_breakaway_gap_scores_kernel(
             words, scales = quantise(kept([P, width], I32, f"z_words{c}")[:], kept([P, width], U8, f"z_scales{c}")[:], z_last[c][:])
             product(c, 1, words, scales)
 
-        product(0, 0, *z_early)
-        w4_q.append(quantise(kept([P, N], I32, "w4_words1", after=f"x1_{PACK}")[:], kept([P, N], U8, "w4_scales1")[:], w4_grouped[1][:]))
+        def open_chunks(m, after):
+            width = m.stop - m.start
+            words, scales = quantise(
+                kept([P, width], I32, f"z_first_words{m.start}", after=after)[:], kept([P, width], U8, f"z_first_scales{m.start}")[:], z_first[:, m, :]
+            )
+            for c, chunk in enumerate(CHUNKS):
+                if m.start <= chunk.start < m.stop:
+                    inner = slice(chunk.start - m.start, chunk.stop - m.start)
+                    product(c, 0, words[:, inner], scales[:, inner])
+
+        open_chunks(first, f"x1_{PACK}")
         z_last = [finish("z_last0", pairs[1][:, :, first], lead_late[0])]
         chase(last, rest)
         close(0)
-        words, scales = quantise(
-            kept([P, M - first.stop], I32, "z_late_words", after=f"x1_{PACK + 1}")[:], kept([P, M - first.stop], U8, "z_late_scales")[:], z_first[:, rest, :]
-        )
-        for c in range(1, len(CHUNKS)):
-            inner = slice(CHUNKS[c].start - first.stop, CHUNKS[c].stop - first.stop)
-            product(c, 0, words[:, inner], scales[:, inner])
+        chase(last - 1, rest)
+        open_chunks(rest, f"x1_{PACK + 1}")
         for c in range(1, len(CHUNKS)):
             inner = slice(CHUNKS[c].start - first.stop, CHUNKS[c].stop - first.stop)
             z_last.append(finish(f"z_last{c}", pairs[1][:, :, CHUNKS[c]], lead_late[1][:, :, inner]))

@@ -30,7 +30,6 @@ BANKS = 8
 PARTS = S // BANK
 PER_COLUMN = 16
 PAIR = 2
-LINE = 4
 CHUNKS = (slice(0, 256), slice(256, 384), slice(384, 512))
 VECTOR_BANKS = 5
 RAW_BYTES = PACK * PASS * 4
@@ -41,6 +40,7 @@ W1_ORDERED_AT = W4_AT + PASSES * RAW_BYTES
 TAB_AT = W1_ORDERED_AT + 2 * H
 W1_AT = TAB_AT + 4 * T
 LATE_AT = W1_AT + 2 * H
+PICKED_AT = LATE_AT + (PACK + 1) * M * 4 + 4 * BANK - S // 2
 WARM_PASSES = 3
 LAST_QUADRANT = slice(96, P)
 
@@ -72,11 +72,15 @@ def tile_list_breakaway_gap_scores_kernel(
             return raw
 
         def load_w4(b):
-            raw = at(W4_AT + (PASSES - 1 - b) * RAW_BYTES, [P, PACK, N], F32, f"w4_raw{b}")
+            raw = at(W4_AT + b * RAW_BYTES, [P, PACK, N], F32, f"w4_raw{b}")
             rows = w4[b * PASS : (b + 1) * PASS, :].rearrange("(g t e) n -> t g e n", t=PACK, e=RUN)
             for t in range(PACK):
                 nc.sync.dma_start(raw[:, t, :], rows[t])
             return raw
+
+        def spread(engine, plane, rows):
+            for r in range(4):
+                engine.dma_start(plane[r:P:32, :].bitcast(I32), rows[P - BLOCKS + r : P : 4, :].bitcast(I32))
 
         def in_slice_order(ordered, raw):
             src = raw.bitcast(I32).rearrange("p (g t w) -> p t g w", g=GROUPS, t=PACK)
@@ -102,17 +106,16 @@ def tile_list_breakaway_gap_scores_kernel(
         pos2_sb = keep.tile([P, M // PER_COLUMN], U16, name="pos2_sb")
         pos3_sb = keep.tile([P, M // PER_COLUMN], U16, name="pos3_sb")
         w1s_raw = at(0, [P, H], U8, "w1s_raw")
-        w3s_raw = kept([P, H], U8, "w3s_raw")
+        w3s_raw = at(W3_AT, [P, W1_ORDERED_AT - W3_AT], U8, "w3s_raw")[:, 0:H]
         tab_s = at(2 * H, [P, T], U8, "tab_s")
         tab_w = at(TAB_AT, [P, T], I32, "tab_w")
         warm = kept([P, 16], F32, "warm")
         nc.gpsimd.memset(warm[:, 0:1], 0.0)
-        rows = at(W3_AT, [P, W1_ORDERED_AT - W3_AT], U8, "rows")[:, 0 : S + H]
-        other_rows = kept([P, S + H], U8, "other_rows")[:]
+        rows = kept([P, S + H], U8, "rows")
         first_s = kept([P, S + H], U8, "first_s")
         w3_s = kept([P, H], U8, "w3_s")
         nc.vector.memset(tab_s[0 : P - BLOCKS, :].bitcast(I32), 0)
-        for raw in (w1s_raw, w3s_raw):
+        for raw in (w1s_raw[:], w3s_raw):
             nc.gpsimd.memset(raw[LAST_QUADRANT.start : P - BLOCKS, :].bitcast(I32), 0)
         for plane in (first_s, w3_s):
             nc.gpsimd.memset(plane[:].bitcast(I32), 0)
@@ -135,33 +138,26 @@ def tile_list_breakaway_gap_scores_kernel(
         nc.scalar.activation(warm[:, 8:9], warm[:, 0:1], SIGMOID)
 
         part_offs = [offs_sb[:, h * BANK // PER_COLUMN : (h + 1) * BANK // PER_COLUMN] for h in range(PARTS)]
-        picked_s = kept([P, 2 * S], U8, "picked_s")[:, 0:S]
-        w1s_ordered, w3s_ordered = kept([P, H], U8, "w1s_ordered"), kept([P, H], U8, "w3s_ordered")
-        dealt(w1s_ordered[LAST_QUADRANT, :], w1s_raw[LAST_QUADRANT, :], U16)
-        for staging in (rows, other_rows):
-            nc.gpsimd.tensor_copy(staging[LAST_QUADRANT, S:].bitcast(I32), w1s_ordered[LAST_QUADRANT, :].bitcast(I32))
+        picked_s = at(PICKED_AT, [P, S], U8, "picked_s")
+        dealt(rows[LAST_QUADRANT, S:], w1s_raw[LAST_QUADRANT, :], U16)
+        nc.vector.tensor_copy(picked_s[:], tab_s[:].indirect(offs_sb[:]))
+        nc.vector.tensor_copy(rows[LAST_QUADRANT, 0:S].bitcast(I32), picked_s[LAST_QUADRANT, :].bitcast(I32))
+        spread(nc.scalar, first_s, rows)
+        w3s_ordered = at(PICKED_AT + S // 2, [P, H], U8, "w3s_ordered")
         dealt(w3s_ordered[LAST_QUADRANT, :], w3s_raw[LAST_QUADRANT, :], U16)
-        nc.vector.tensor_copy(picked_s, tab_s[:].indirect(offs_sb[:]))
-        for staging in (rows, other_rows):
-            nc.vector.tensor_copy(staging[LAST_QUADRANT, 0:S].bitcast(I32), picked_s[LAST_QUADRANT, :].bitcast(I32))
-        for r in range(4):
-            staging = rows if r < 2 else other_rows
-            nc.scalar.dma_start(first_s[r:P:32, :].bitcast(I32), staging[P - BLOCKS + r : P : 4, :].bitcast(I32))
         v_s = [first_s[:, h * BANK : (h + 1) * BANK] for h in range(PARTS)]
         w1_s = first_s[:, S:]
 
         w1_raw.append(load_w1(1, W3_AT))
-        w3_rows = at(W3_AT + H, [P, H], U8, "w3_rows")
-        nc.gpsimd.tensor_copy(w3_rows[LAST_QUADRANT, :].bitcast(I32), w3s_ordered[LAST_QUADRANT, :].bitcast(I32))
-        for r in range(4):
-            nc.sync.dma_start(w3_s[r:P:32, :].bitcast(I32), w3_rows[P - BLOCKS + r : P : 4, :].bitcast(I32))
         w3_raw = [load_w3(b) for b in range(PASSES)]
-        w2_raw = [load_w2(0, PASS // 2), load_w2(PASS // 2, PASS // 2), load_w2(PASS, PASS)]
+        w2_raw = [load_w2(0, PASS // 2)]
+        spread(nc.sync, w3_s, w3s_ordered)
+        w2_raw += [load_w2(first, PASS // 2) for first in range(PASS // 2, H, PASS // 2)]
         w4_raw = [load_w4(b) for b in range(PASSES)]
 
         zeros = kept([P, BANK, PACK], BF16, "zeros")
         nc.vector.memset(zeros[:].rearrange("p c j -> p (c j)").bitcast(I32), 0)
-        idle_words, idle_scales = quantise(kept([P, BANK], I32, "idle_words", after="picked_s")[:], kept([P, BANK], U8, "idle_scales")[:], zeros[:])
+        idle_words, idle_scales = quantise(at(PICKED_AT + S // 2 - 4 * BANK, [P, BANK], I32, "idle_words")[:], kept([P, BANK], U8, "idle_scales")[:], zeros[:])
         idle_bank = bank(VECTOR_BANKS - 1)
         for k in range(WARM_PASSES):
             nc.tensor.matmul_mx(
@@ -177,27 +173,30 @@ def tile_list_breakaway_gap_scores_kernel(
         dealt(w1_w[:, 0:H], w1_raw[0][:], U32)
         in_slice_order(w1_w[:, H:], w1_raw[1][:])
         v_w.append(kept([P, BANK], I32, "v_w1"))
-        nc.vector.tensor_copy(v_w[1][:].bitcast(U32), tab_w[:].bitcast(U32).indirect(part_offs[1]))
+        for m in halves:
+            nc.vector.tensor_copy(v_w[1][:, m].bitcast(U32), tab_w[:].bitcast(U32).indirect(part_offs[1][:, m.start // PER_COLUMN : m.stop // PER_COLUMN]))
         w3_w = [in_slice_order(kept([P, PACK * PASS], U8, f"w3_w{b}")[:], w3_raw[b][:]) for b in range(PASSES)]
 
         w2_grouped = [kept([P, PASS, PACK], BF16, f"w2_grouped{b}") for b in range(PASSES)]
-        w4_grouped = [kept([P, N, PACK], BF16, "w4_grouped0")]
-        for raw, b, groups in zip(w2_raw, (0, 0, 1), (slice(0, GROUPS // 2), slice(GROUPS // 2, GROUPS), slice(0, GROUPS))):
+        w4_grouped = [kept([P, N, PACK], BF16, f"w4_grouped{b}") for b in range(PASSES)]
+        for quarter, raw in enumerate(w2_raw):
+            b, groups = quarter // 2, slice(quarter % 2 * GROUPS // 2, (quarter % 2 + 1) * GROUPS // 2)
             nc.gpsimd.tensor_copy(
                 w2_grouped[b][:].rearrange("p (t g e) j -> p g t j e", t=PACK, e=RUN)[:, groups],
                 raw[:].rearrange("p j (g t e) -> p g t j e", t=PACK, e=RUN),
             )
-        nc.gpsimd.tensor_copy(
-            w4_grouped[0][:].rearrange("p (c e) j -> p c j e", e=PAIR), w4_raw[0][:].rearrange("p j (c e) -> p c j e", e=PAIR)
-        )
+        for b in range(PASSES):
+            nc.gpsimd.tensor_copy(
+                w4_grouped[b][:].rearrange("p (c e) j -> p c j e", e=PAIR), w4_raw[b][:].rearrange("p j (c e) -> p c j e", e=PAIR)
+            )
 
-        def project(x, h, lhs, lhs_scale, number, copy):
+        def project(x, h, lhs, lhs_scale, number, copy, m=slice(0, BANK)):
             acc = bank(number)
             nc.tensor.matmul_mx(
-                acc[:], lhsT=lhs, lhsT_scale=lhs_scale, rhs=v_w[h][:].bitcast(FP8X4), rhs_scale=v_s[h],
+                acc[:, m], lhsT=lhs, lhsT_scale=lhs_scale, rhs=v_w[h][:, m].bitcast(FP8X4), rhs_scale=v_s[h][:, m],
                 start=True, stop=True,
             )
-            copy(x[:, h * BANK : (h + 1) * BANK], acc[:])
+            copy(x[:, h * BANK + m.start : h * BANK + m.stop], acc[:, m])
 
         turns = {True: [], False: []}
 
@@ -209,8 +208,8 @@ def tile_list_breakaway_gap_scores_kernel(
         x1 = [kept([P, S], F32, f"x1_{s}") for s in range(SLICES)]
         x3 = [kept([P, S], F32, f"x3_{s}") for s in range(SLICES)]
 
-        def project_x1(s, h, on_vector):
-            project(x1[s], h, w1_w[:, 2 * s * P : 2 * (s + 1) * P].bitcast(FP4X4), w1_s[:, s * P : (s + 1) * P], *early_bank(on_vector))
+        def project_x1(s, h, on_vector, m=slice(0, BANK)):
+            project(x1[s], h, w1_w[:, 2 * s * P : 2 * (s + 1) * P].bitcast(FP4X4), w1_s[:, s * P : (s + 1) * P], *early_bank(on_vector), m)
 
         def project_x3(s, h):
             b, t = divmod(s, PACK)
@@ -235,21 +234,20 @@ def tile_list_breakaway_gap_scores_kernel(
 
         for m in halves:
             for s in range(2):
-                acc = bank(early_bank(False)[0])
-                nc.tensor.matmul_mx(
-                    acc[:, m], lhsT=w1_w[:, 2 * s * P : 2 * (s + 1) * P].bitcast(FP4X4), lhsT_scale=w1_s[:, s * P : (s + 1) * P],
-                    rhs=v_w[0][:, m].bitcast(FP8X4), rhs_scale=v_s[0][:, m], start=True, stop=True,
-                )
-                nc.scalar.copy(x1[s][:, m], acc[:, m])
+                project_x1(s, 0, False, m)
         for s in range(2, PACK):
             project_x1(s, 0, True)
+        for m in halves:
+            for s in range(2):
+                project_x1(s, 1, False, m)
         for s in range(PACK):
-            project_x1(s, 1, s >= 2)
             if s < 2:
                 leader(s, whole)
+            else:
+                project_x1(s, 1, True)
         for h in range(PARTS):
             project_x1(PACK, h, True)
-            project_x1(last, h, False)
+            project_x1(last, h, h > 0)
             leader(2 + h, whole)
         for s in range(SLICES):
             for h in range(PARTS):
@@ -262,11 +260,9 @@ def tile_list_breakaway_gap_scores_kernel(
 
         weight_words = at(TAB_AT - 4 * H, [P, H], I32, "w2_words")
         w4_words = kept([P, PASSES * N], I32, "w4_words", after="w2_grouped1")
-        w2_q = [quantise(weight_words[:, b * PASS : (b + 1) * PASS], w2_scales[b][:], w2_grouped[b][:]) for b in range(PASSES)]
-        w4_grouped.append(kept([P, N, PACK], BF16, "w4_grouped1", after="w2_grouped0"))
-        nc.vector.tensor_copy(
-            w4_grouped[1][:].rearrange("p (c i) j -> p c j i", i=LINE), w4_raw[1][:].rearrange("p j (c i) -> p c j i", i=LINE)
-        )
+        for b, cols in ((0, slice(0, P)), (0, slice(P, PASS)), (1, slice(0, PASS))):
+            quantise(weight_words[:, b * PASS : (b + 1) * PASS][:, cols], w2_scales[b][:, cols], w2_grouped[b][:, cols, :])
+        w2_q = [(weight_words[:, b * PASS : (b + 1) * PASS], w2_scales[b][:]) for b in range(PASSES)]
         w4_scales = kept([P, PASSES * N], U8, "w4_scales")
         w4_q = [quantise(w4_words[:, b * N : (b + 1) * N], w4_scales[:, b * N : (b + 1) * N], w4_grouped[b][:]) for b in range(PASSES)]
         pairs = [at(TAB_AT + b * RAW_BYTES, [P, PACK, M], F32, f"pair{b}")[:] for b in range(PASSES)]

@@ -41,6 +41,7 @@ TAB_AT = W1_ORDERED_AT + 2 * H
 W1_AT = TAB_AT + 4 * T
 LATE_AT = W1_AT + 2 * H
 PICKED_AT = LATE_AT + (PACK + 1) * M * 4 + 4 * BANK - S // 2
+ALIGN = 256
 WARM_PASSES = 3
 LAST_QUADRANT = slice(96, P)
 
@@ -55,10 +56,10 @@ def tile_list_breakaway_gap_scores_kernel(
         psum = ctx.enter_context(tc.psum_pool(name="psum", bufs=1))
 
         def kept(shape, dtype, name, after=""):
-            return keep.tile(shape, dtype, name=name, tag=after or name, align_bytes=64)
+            return keep.tile(shape, dtype, name=name, tag=after or name, align_bytes=ALIGN)
 
         def at(offset, shape, dtype, name):
-            return placed.tile(shape, dtype, name=name, offset=offset, align_bytes=64)
+            return placed.tile(shape, dtype, name=name, offset=offset, align_bytes=ALIGN)
 
         def load_w2(first, width):
             raw = at(W2_AT + first * PACK * 4, [P, PACK, width], F32, f"w2_raw{first}")

from contextlib import ExitStack

import concourse.mybir as mybir

K, H, N, T, S, M = 512, 1024, 512, 4096, 1024, 512
FLOPS = 2 * (3 * K * H * S + H * N * M)

F32 = mybir.dt.float32
BF16 = mybir.dt.bfloat16
I32 = mybir.dt.int32
U32 = mybir.dt.uint32
U16 = mybir.dt.uint16
U8 = mybir.dt.uint8
FP8X4 = mybir.dt.float8_e4m3fn_x4
FP4X4 = mybir.dt.float4_e2m1fn_x4
MULT = mybir.AluOpType.mult
SIGMOID = mybir.ActivationFunctionType.Sigmoid
COPY = mybir.ActivationFunctionType.Copy

P = 128
PACK = 4
PASS = P * PACK
BLOCKS = PASS // 32
RUN = 2
GROUPS = P // RUN
PASSES = H // PASS
SLICES = PASSES * PACK
BANK = 512
BANKS = 8
PARTS = S // BANK
PER_COLUMN = 16
PAIR = 2
CHUNKS = (slice(0, 256), slice(256, 384), slice(384, 512))
VECTOR_BANKS = 5
RAW_BYTES = PACK * PASS * 4
W3_AT = 2 * H + T
W2_AT = W3_AT + 2 * H + PACK * H
W4_AT = W2_AT + PASSES * RAW_BYTES
W1_ORDERED_AT = W4_AT + PASSES * RAW_BYTES
TAB_AT = W1_ORDERED_AT + 2 * H
W1_AT = TAB_AT + 4 * T
LATE_AT = W1_AT + 2 * H
PICKED_AT = LATE_AT + (PACK + 1) * M * 4 + 4 * BANK - S // 2
ALIGN = 256
WARM_PASSES = 3
LAST_QUADRANT = slice(96, P)


def tile_list_breakaway_gap_scores_kernel(
    tc, tab_words, tab_scales, offs, w1_words, w1_scales, w2, w3_words, w3_scales, pos1, pos2, pos3, w4, out
):
    nc = tc.nc
    with ExitStack() as ctx:
        keep = ctx.enter_context(tc.tile_pool(name="keep", bufs=1))
        placed = ctx.enter_context(tc.tile_pool(name="placed", bufs=1))
        psum = ctx.enter_context(tc.psum_pool(name="psum", bufs=1))

        def kept(shape, dtype, name, after=""):
            return keep.tile(shape, dtype, name=name, tag=after or name, align_bytes=ALIGN)

        def at(offset, shape, dtype, name):
            return placed.tile(shape, dtype, name=name, offset=offset, align_bytes=ALIGN)

        def load_w2(first, width):
            raw = at(W2_AT + first * PACK * 4, [P, PACK, width], F32, f"w2_raw{first}")
            nc.sync.dma_start(raw[:], w2[:, first : first + width].rearrange("(p j) c -> p j c", j=PACK))
            return raw

        def load_w3(b):
            raw = at(W3_AT + 2 * H + b * PACK * PASS, [P, PACK * PASS], U8, f"w3_raw{b}")
            words = w3_words[0][:, b * PASS : (b + 1) * PASS, :].rearrange("p c i -> p (c i)")
            nc.sync.dma_start(raw[:].bitcast(I32), words.bitcast(I32))
            return raw

        def load_w4(b):
            raw = at(W4_AT + b * RAW_BYTES, [P, PACK, N], F32, f"w4_raw{b}")
            rows = w4[b * PASS : (b + 1) * PASS, :].rearrange("(g t e) n -> t g e n", t=PACK, e=RUN)
            for t in range(PACK):
                nc.sync.dma_start(raw[:, t, :], rows[t])
            return raw

        def spread(engine, plane, rows):
            for r in range(4):
                engine.dma_start(plane[r:P:32, :].bitcast(I32), rows[P - BLOCKS + r : P : 4, :].bitcast(I32))

        def in_slice_order(ordered, raw):
            src = raw.bitcast(I32).rearrange("p (g t w) -> p t g w", g=GROUPS, t=PACK)
            nc.gpsimd.tensor_copy(ordered.bitcast(I32).rearrange("p (t g w) -> p t g w", g=GROUPS, t=PACK), src)
            return ordered

        def dealt(ordered, raw, dtype):
            src = raw.bitcast(dtype).rearrange("p (b g t) -> p b g t", g=GROUPS, t=PACK)
            nc.scalar.copy(ordered.bitcast(dtype).rearrange("p (b t g) -> p b g t", g=GROUPS, t=PACK), src)

        def quantise(words, scales, grouped):
            nc.vector.quantize_mx(words.bitcast(FP8X4), scales, grouped.rearrange("p c j -> p (c j)"))
            return words, scales

        taken = []

        def bank(number):
            taken.append(psum.tile([P, BANK], F32, name=f"acc{len(taken)}", tag=f"bank{number}"))
            return taken[-1]

        offs_sb = keep.tile([P, S // PER_COLUMN], U16, name="offs_sb")
        pos1_sb = keep.tile([P, M // PER_COLUMN], U16, name="pos1_sb")
        pos2_sb = keep.tile([P, M // PER_COLUMN], U16, name="pos2_sb")
        pos3_sb = keep.tile([P, M // PER_COLUMN], U16, name="pos3_sb")
        w1s_raw = at(0, [P, H], U8, "w1s_raw")
        w3s_raw = at(W3_AT, [P, W1_ORDERED_AT - W3_AT], U8, "w3s_raw")[:, 0:H]
        tab_s = at(2 * H, [P, T], U8, "tab_s")
        tab_w = at(TAB_AT, [P, T], I32, "tab_w")
        warm = kept([P, 16], F32, "warm")
        nc.gpsimd.memset(warm[:, 0:1], 0.0)
        rows = kept([P, S + H], U8, "rows")
        first_s = kept([P, S + H], U8, "first_s")
        w3_s = kept([P, H], U8, "w3_s")
        nc.vector.memset(tab_s[0 : P - BLOCKS, :].bitcast(I32), 0)
        for raw in (w1s_raw[:], w3s_raw):
            nc.gpsimd.memset(raw[LAST_QUADRANT.start : P - BLOCKS, :].bitcast(I32), 0)
        for plane in (first_s, w3_s):
            nc.gpsimd.memset(plane[:].bitcast(I32), 0)

        def load_w1(b, offset):
            raw = at(offset, [P, H], U8, f"w1_raw{b}")
            nc.sync.dma_start(raw[:].bitcast(I32), w1_words[0][:, b * H : (b + 1) * H].bitcast(I32))
            return raw

        nc.sync.dma_start(offs_sb[:], offs)
        nc.sync.dma_start(tab_s[P - BLOCKS : P, :].bitcast(I32), tab_scales[0].bitcast(I32))
        nc.sync.dma_start(w1s_raw[P - BLOCKS : P, :].bitcast(I32), w1_scales[0].bitcast(I32))
        nc.sync.dma_start(w3s_raw[P - BLOCKS : P, :].bitcast(I32), w3_scales[0].bitcast(I32))
        nc.sync.dma_start(pos1_sb[:], pos1)
        nc.sync.dma_start(tab_w[:], tab_words[0].rearrange("p t i -> p (t i)").bitcast(I32))
        w1_raw = [load_w1(0, W1_AT)]
        nc.sync.dma_start(pos3_sb[:], pos3)
        nc.sync.dma_start(pos2_sb[:], pos2)

        nc.scalar.activation(warm[:, 8:9], warm[:, 0:1], SIGMOID)

        part_offs = [offs_sb[:, h * BANK // PER_COLUMN : (h + 1) * BANK // PER_COLUMN] for h in range(PARTS)]
        picked_s = at(PICKED_AT, [P, S], U8, "picked_s")
        dealt(rows[LAST_QUADRANT, S:], w1s_raw[LAST_QUADRANT, :], U16)
        nc.vector.tensor_copy(picked_s[:], tab_s[:].indirect(offs_sb[:]))
        nc.vector.tensor_copy(rows[LAST_QUADRANT, 0:S].bitcast(I32), picked_s[LAST_QUADRANT, :].bitcast(I32))
        spread(nc.scalar, first_s, rows)
        w3s_ordered = at(PICKED_AT + S // 2, [P, H], U8, "w3s_ordered")
        dealt(w3s_ordered[LAST_QUADRANT, :], w3s_raw[LAST_QUADRANT, :], U16)
        v_s = [first_s[:, h * BANK : (h + 1) * BANK] for h in range(PARTS)]
        w1_s = first_s[:, S:]

        w1_raw.append(load_w1(1, W3_AT))
        w3_raw = [load_w3(b) for b in range(PASSES)]
        w2_raw = [load_w2(0, PASS // 2)]
        spread(nc.sync, w3_s, w3s_ordered)
        w2_raw += [load_w2(first, PASS // 2) for first in range(PASS // 2, H, PASS // 2)]
        w4_raw = [load_w4(b) for b in range(PASSES)]

        zeros = kept([P, BANK, PACK], BF16, "zeros")
        nc.vector.memset(zeros[:].rearrange("p c j -> p (c j)").bitcast(I32), 0)
        idle_words, idle_scales = quantise(at(PICKED_AT + S // 2 - 4 * BANK, [P, BANK], I32, "idle_words")[:], kept([P, BANK], U8, "idle_scales")[:], zeros[:])
        idle_bank = bank(VECTOR_BANKS - 1)
        for k in range(WARM_PASSES):
            nc.tensor.matmul_mx(
                idle_bank[:], lhsT=idle_words[:, 0:P].bitcast(FP8X4), lhsT_scale=idle_scales[:, 0:P],
                rhs=idle_words.bitcast(FP8X4), rhs_scale=idle_scales, start=True, stop=True,
            )

        v_w = [at(0, [P, BANK], I32, "v_w0")]
        halves = (slice(0, BANK // 2), slice(BANK // 2, BANK))
        for m in halves:
            nc.vector.tensor_copy(v_w[0][:, m].bitcast(U32), tab_w[:].bitcast(U32).indirect(offs_sb[:, m.start // PER_COLUMN : m.stop // PER_COLUMN]))
        w1_w = at(W1_ORDERED_AT, [P, 2 * H], U8, "w1_w")
        dealt(w1_w[:, 0:H], w1_raw[0][:], U32)
        in_slice_order(w1_w[:, H:], w1_raw[1][:])
        v_w.append(kept([P, BANK], I32, "v_w1"))
        for m in halves:
            nc.vector.tensor_copy(v_w[1][:, m].bitcast(U32), tab_w[:].bitcast(U32).indirect(part_offs[1][:, m.start // PER_COLUMN : m.stop // PER_COLUMN]))
        w3_w = [in_slice_order(kept([P, PACK * PASS], U8, f"w3_w{b}")[:], w3_raw[b][:]) for b in range(PASSES)]

        w2_grouped = [kept([P, PASS, PACK], BF16, f"w2_grouped{b}") for b in range(PASSES)]
        w4_grouped = [kept([P, N, PACK], BF16, f"w4_grouped{b}") for b in range(PASSES)]
        for quarter, raw in enumerate(w2_raw):
            b, groups = quarter // 2, slice(quarter % 2 * GROUPS // 2, (quarter % 2 + 1) * GROUPS // 2)
            nc.gpsimd.tensor_copy(
                w2_grouped[b][:].rearrange("p (t g e) j -> p g t j e", t=PACK, e=RUN)[:, groups],
                raw[:].rearrange("p j (g t e) -> p g t j e", t=PACK, e=RUN),
            )
        for b in range(PASSES):
            nc.gpsimd.tensor_copy(
                w4_grouped[b][:].rearrange("p (c e) j -> p c j e", e=PAIR), w4_raw[b][:].rearrange("p j (c e) -> p c j e", e=PAIR)
            )

        def project(x, h, lhs, lhs_scale, number, copy, m=slice(0, BANK)):
            acc = bank(number)
            nc.tensor.matmul_mx(
                acc[:, m], lhsT=lhs, lhsT_scale=lhs_scale, rhs=v_w[h][:, m].bitcast(FP8X4), rhs_scale=v_s[h][:, m],
                start=True, stop=True,
            )
            copy(x[:, h * BANK + m.start : h * BANK + m.stop], acc[:, m])

        turns = {True: [], False: []}

        def early_bank(on_vector):
            mine = turns[on_vector]
            mine.append(len(mine) % VECTOR_BANKS if on_vector else VECTOR_BANKS + len(mine) % (BANKS - VECTOR_BANKS))
            return mine[-1], nc.vector.tensor_copy if on_vector else nc.scalar.copy

        x1 = [kept([P, S], F32, f"x1_{s}") for s in range(SLICES)]
        x3 = [kept([P, S], F32, f"x3_{s}") for s in range(SLICES)]

        def project_x1(s, h, on_vector, m=slice(0, BANK)):
            project(x1[s], h, w1_w[:, 2 * s * P : 2 * (s + 1) * P].bitcast(FP4X4), w1_s[:, s * P : (s + 1) * P], *early_bank(on_vector), m)

        def project_x3(s, h):
            b, t = divmod(s, PACK)
            project(x3[s], h, w3_w[b][:, PACK * t * P : PACK * (t + 1) * P].bitcast(FP8X4), w3_s[:, s * P : (s + 1) * P], *early_bank(True))

        first, rest, whole = CHUNKS[0], slice(CHUNKS[0].stop, M), slice(0, M)
        last = SLICES - 1
        w2_scales = [at(LATE_AT, [P, PASS], U8, "w2_scales0"), kept([P, PASS], U8, "w2_scales1")]
        lead_early = kept([P, PACK, M], F32, "lead_early")[:]
        leads = [lead_early[:, t, :] for t in range(PACK)]
        helpers = [kept([P, M], F32, f"helper{s}")[:] for s in range(last)]

        def columns(picks_sb, m):
            return picks_sb[:, m.start // PER_COLUMN : m.stop // PER_COLUMN]

        def leader(s, m):
            lead = leads[s] if s < PACK else lead_late[m.start > 0][:, s % PACK, :]
            nc.scalar.activation(lead, x1[s][:].indirect(columns(pos1_sb, m)), SIGMOID)

        def helper(s, m):
            nc.scalar.activation(helpers[s][:, m], x3[s][:].indirect(columns(pos3_sb, m)), COPY)

        for m in halves:
            for s in range(2):
                project_x1(s, 0, False, m)
        for s in range(2, PACK):
            project_x1(s, 0, True)
        for m in halves:
            for s in range(2):
                project_x1(s, 1, False, m)
        for s in range(PACK):
            if s < 2:
                leader(s, whole)
            else:
                project_x1(s, 1, True)
        for h in range(PARTS):
            project_x1(PACK, h, True)
            project_x1(last, h, h > 0)
            leader(2 + h, whole)
        for s in range(SLICES):
            for h in range(PARTS):
                project_x3(s, h)
            if s < last:
                helper(s, whole)
        for s in range(PACK + 1, last):
            for h in range(PARTS):
                project_x1(s, h, True)

        weight_words = at(TAB_AT - 4 * H, [P, H], I32, "w2_words")
        w4_words = kept([P, PASSES * N], I32, "w4_words", after="w2_grouped1")
        for b, cols in ((0, slice(0, P)), (0, slice(P, PASS)), (1, slice(0, PASS))):
            quantise(weight_words[:, b * PASS : (b + 1) * PASS][:, cols], w2_scales[b][:, cols], w2_grouped[b][:, cols, :])
        w2_q = [(weight_words[:, b * PASS : (b + 1) * PASS], w2_scales[b][:]) for b in range(PASSES)]
        w4_scales = kept([P, PASSES * N], U8, "w4_scales")
        w4_q = [quantise(w4_words[:, b * N : (b + 1) * N], w4_scales[:, b * N : (b + 1) * N], w4_grouped[b][:]) for b in range(PASSES)]
        pairs = [at(TAB_AT + b * RAW_BYTES, [P, PACK, M], F32, f"pair{b}")[:] for b in range(PASSES)]
        late = at(LATE_AT, [P, (PACK + 1) * M], F32, "late")
        lead_late = [late[:, PACK * m.start : PACK * m.stop].rearrange("p (j m) -> p j m", j=PACK) for m in (first, rest)]
        helpers.append(late[:, PACK * M :])

        def finish(name, pair, lead):
            grouped = kept([P, pair.shape[2], PACK], BF16, name)
            nc.vector.tensor_tensor(
                grouped[:].rearrange("p (c i) j -> p c j i", i=PAIR),
                pair.rearrange("p j (c i) -> p c j i", i=PAIR),
                lead.rearrange("p j (c i) -> p c j i", i=PAIR),
                MULT,
            )
            return grouped

        def chase(s, m):
            nc.vector.tensor_tensor(pairs[s // PACK][:, s % PACK, m], x2[s][:].indirect(columns(pos2_sb, m)), helpers[s][:, m], MULT)

        x2 = []
        for s in range(SLICES):
            b, t = divmod(s, PACK)
            cols = slice(t * P, (t + 1) * P)
            x2.append(kept([P, S], F32, f"x2_{s}", after=f"x3_{s}" if s < last else ""))
            if s == last:
                helper(s, first)
            for h in range(PARTS):
                project(x2[s], h, w2_q[b][0][:, cols].bitcast(FP8X4), w2_q[b][1][:, cols], (PARTS * s + h + VECTOR_BANKS) % BANKS, nc.scalar.copy)
            chase(s, whole if s < last - 1 else first)
            if s == PACK - 1:
                z_first = finish("z_first", pairs[0], lead_early)
        for m in (first, rest):
            leader(PACK, m)
        for s in range(PACK + 1, SLICES):
            leader(s, first)
        helper(last, rest)
        for s in range(PACK + 1, SLICES):
            leader(s, rest)

        accs = [[bank((2 * c + pair + VECTOR_BANKS) % BANKS) for pair in range(2)] for c in range(len(CHUNKS))]

        def product(c, b, words, scales):
            width = CHUNKS[c].stop - CHUNKS[c].start
            for j in range(N // P):
                cols = slice(j * P, (j + 1) * P)
                nc.tensor.matmul_mx(
                    accs[c][j // 2][:, j % 2 * width : (j % 2 + 1) * width],
                    lhsT=w4_q[b][0][:, cols].bitcast(FP8X4), lhsT_scale=w4_q[b][1][:, cols],
                    rhs=words.bitcast(FP8X4), rhs_scale=scales,
                    start=(b == 0 and j % 2 == 0), stop=(b == PASSES - 1 and j % 2 == 1),
                )

        def close(c):
            width = CHUNKS[c].stop - CHUNKS[c].start
            words, scales = quantise(kept([P, width], I32, f"z_words{c}")[:], kept([P, width], U8, f"z_scales{c}")[:], z_last[c][:])
            product(c, 1, words, scales)

        def open_chunks(m, after):
            width = m.stop - m.start
            words, scales = quantise(
                kept([P, width], I32, f"z_first_words{m.start}", after=after)[:], kept([P, width], U8, f"z_first_scales{m.start}")[:], z_first[:, m, :]
            )
            for c, chunk in enumerate(CHUNKS):
                if m.start <= chunk.start < m.stop:
                    inner = slice(chunk.start - m.start, chunk.stop - m.start)
                    product(c, 0, words[:, inner], scales[:, inner])

        open_chunks(first, f"x1_{PACK}")
        z_last = [finish("z_last0", pairs[1][:, :, first], lead_late[0])]
        chase(last, rest)
        close(0)
        chase(last - 1, rest)
        open_chunks(rest, f"x1_{PACK + 1}")
        for c in range(1, len(CHUNKS)):
            inner = slice(CHUNKS[c].start - first.stop, CHUNKS[c].stop - first.stop)
            z_last.append(finish(f"z_last{c}", pairs[1][:, :, CHUNKS[c]], lead_late[1][:, :, inner]))
        for c in range(1, len(CHUNKS)):
            close(c)

        out_rows = out.rearrange("(j p) m -> p j m", p=P)
        for c, m in enumerate(CHUNKS):
            width = m.stop - m.start
            for pair in range(2):
                res = kept([P, 2, width], F32, f"res{c}_{pair}")
                copy = nc.vector.tensor_copy if pair and c else nc.scalar.copy
                copy(res[:].rearrange("p j m -> p (j m)"), accs[c][pair][:, 0 : 2 * width])
                nc.sync.dma_start(out_rows[:, 2 * pair : 2 * pair + 2, m], res[:])
